import numpy as np
import ml_dtypes


def mxq(x, axis, fmt="e4m3"):
    dtype, down = {"e4m3": (ml_dtypes.float8_e4m3fn, 7), "e5m2": (ml_dtypes.float8_e5m2, 14)}[fmt]
    v = np.moveaxis(np.asarray(x, np.float32).astype(ml_dtypes.bfloat16).astype(np.float64), axis, -1)
    blocks = v.reshape(v.shape[:-1] + (-1, 32))
    amax = np.abs(blocks).max(-1, keepdims=True)
    byte = np.maximum(np.where(amax > 0, np.frexp(amax)[1] - 1 + 127, 0) - down, 1)
    scale = np.exp2(byte - 127.0)
    codes = (blocks / scale).astype(np.float32).astype(dtype).astype(np.float64)
    return np.moveaxis((codes * scale).reshape(v.shape), -1, axis)


WIDE = False


def mx_kscale(k):
    if not WIDE:
        return np.ones(k)
    levels = np.array([10, -10, 5, -5, 0])
    if k % 512:
        return np.exp2(np.random.permutation(np.resize(levels, k // 32))).repeat(32)
    a = np.empty((k // 512, 16))
    for p in range(k // 512):
        a[p, :8] = np.random.permutation(np.resize(levels, 8))
        for g in range(8):
            far = levels[np.abs(levels - a[p, g]) >= 10]
            a[p, g + 8] = far[np.random.randint(len(far))]
    return np.exp2(a.ravel()).repeat(32)


def f64(x):
    return np.asarray(x).astype(np.float64)


def striped(idx):
    return np.tile(idx.reshape(-1, 16).T, (8, 1)).astype(np.uint16)


def unstriped(offs):
    return offs[:16].T.reshape(-1).astype(np.int64)


E2M1 = np.array([0.0, 0.5, 1.0, 1.5, 2.0, 3.0, 4.0, 6.0, -0.0, -0.5, -1.0, -1.5, -2.0, -3.0, -4.0, -6.0])


def pack_weight(w, fmt):
    k, n = w.shape
    w = f64(np.asarray(w, np.float32).astype(ml_dtypes.bfloat16)).reshape(k // 32, 32, n)
    amax = np.abs(w).max(1)
    if fmt == "e4m3":
        byte = np.frexp(amax)[1] - 1 + 127 - 7
    else:
        mant, ex = np.frexp(amax / 6.0)
        byte = np.where(mant > 0.5, ex, ex - 1) + 127
    byte = np.clip(np.where(amax > 0, byte, 1), 1, 254)
    scaled = (w * np.exp2(127.0 - byte)[:, None, :]).reshape(k, n).astype(np.float32)
    by_word = np.ascontiguousarray(scaled.reshape(k // 512, 128, 4, n).transpose(0, 1, 3, 2))
    if fmt == "e4m3":
        words = by_word.astype(ml_dtypes.float8_e4m3fn).view(np.uint8)
    else:
        c = by_word.astype(ml_dtypes.float4_e2m1fn).view(np.uint8) & 0xF
        words = (c[..., 0::2] | (c[..., 1::2] << 4)).reshape(k // 512, 128, 2 * n)
    return np.ascontiguousarray(words), np.ascontiguousarray(byte.astype(np.uint8).reshape(k // 512, 16, n))


def unpack_weight(words, scales, fmt):
    g, _, n = scales.shape
    words = np.ascontiguousarray(words).reshape(g, 128, n, -1)
    if fmt == "e4m3":
        vals = words.view(ml_dtypes.float8_e4m3fn).astype(np.float64)
    else:
        nib = np.empty((g, 128, n, 4), np.uint8)
        nib[..., 0::2] = words & 0xF
        nib[..., 1::2] = words >> 4
        vals = E2M1[nib]
    vals = vals * np.repeat(np.exp2(scales.astype(np.float64) - 127.0), 8, axis=1)[..., None]
    return vals.transpose(0, 1, 3, 2).reshape(g * 512, n)


def gelu(v):
    return 0.5 * v * (1.0 + np.tanh(np.sqrt(2.0 / np.pi) * (v + 0.044715 * v**3)))


def often(T, S):
    return np.random.permutation(T)[(T * np.random.uniform(0, 1, S) ** 4).astype(np.int64)]


K, K2, H, N, T, S = 1024, 512, 1024, 512, 4096, 1024

def setup_inputs():
    n = np.random.standard_normal
    s = mx_kscale(K)[:, None]
    s2 = mx_kscale(K2)[:, None]
    u = mx_kscale(H)[:, None]
    tab_words, tab_scales = pack_weight(n((K, T)) * s, "e4m3")
    tab2_words, tab2_scales = pack_weight(n((K2, T)) * s2, "e2m1")
    w1_words, w1_scales = pack_weight(1.5 * n((K, H)) / np.sqrt(K) / s, "e2m1")
    w2 = (1.5 * n((K2, H)) / np.sqrt(K2) / s2).astype(np.float32)
    w3_words, w3_scales = pack_weight(1.5 * n((H, N)) / np.sqrt(H) / u, "e4m3")
    return {
        "tab_words": tab_words, "tab_scales": tab_scales,
        "tab2_words": tab2_words, "tab2_scales": tab2_scales,
        "offs": striped(often(T, S)), "offs2": striped(often(T, S)),
        "w1_words": w1_words, "w1_scales": w1_scales,
        "w2": w2,
        "w3_words": w3_words, "w3_scales": w3_scales,
        "nozzle": (0.7 * n(H)).astype(np.float32),
        "flow": (np.exp(0.3 * n(H)) * u[:, 0]).astype(np.float32),
        "idle": (0.5 * n(N)).astype(np.float32),
    }

def reference(tab_words, tab_scales, tab2_words, tab2_scales, offs, offs2,
              w1_words, w1_scales, w2, w3_words, w3_scales, nozzle, flow, idle):
    v = unpack_weight(tab_words, tab_scales, "e4m3")[:, unstriped(offs)]
    v2 = unpack_weight(tab2_words, tab2_scales, "e2m1")[:, unstriped(offs2)]
    w1 = unpack_weight(w1_words, w1_scales, "e2m1")
    w3 = unpack_weight(w3_words, w3_scales, "e4m3")
    demand = w1.T @ v
    allowed = mxq(f64(w2), 0, "e4m3").T @ v2
    d = np.minimum(demand, allowed) - f64(nozzle)[:, None]
    h = d / (1.0 + np.exp(-d)) * f64(flow)[:, None]
    y = w3.T @ mxq(h, 0, "e4m3")
    return y + f64(idle)[:, None]

@@ -1,0 +1,288 @@
+from contextlib import ExitStack
+
+import concourse.mybir as mybir
+
+K, K2, H, N, T, S = 1024, 512, 1024, 512, 4096, 1024
+FLOPS = 2 * S * (K * H + K2 * H + H * N)
+
+F32 = mybir.dt.float32
+BF16 = mybir.dt.bfloat16
+I32 = mybir.dt.int32
+U32 = mybir.dt.uint32
+U16 = mybir.dt.uint16
+U8 = mybir.dt.uint8
+FP8X4 = mybir.dt.float8_e4m3fn_x4
+FP4X4 = mybir.dt.float4_e2m1fn_x4
+ACT = mybir.ActivationFunctionType
+ALU = mybir.AluOpType
+
+P = 128
+PACK = 4
+KP = P * PACK
+W = 512
+QUADS = 4
+
+
+def tile_list_orchard_spray_dosing_kernel(
+    tc, tab_words, tab_scales, tab2_words, tab2_scales, offs, offs2,
+    w1_words, w1_scales, w2, w3_words, w3_scales, nozzle, flow, idle, out,
+):
+    nc = tc.nc
+    with ExitStack() as ctx:
+        keep = ctx.enter_context(tc.tile_pool(name="keep", bufs=1))
+        ring = ctx.enter_context(tc.tile_pool(name="ring", bufs=2))
+        psum = ctx.enter_context(tc.psum_pool(name="psum", bufs=1))
+
+        def held(name, shape, dtype):
+            return keep.tile(shape, dtype, name=name, align_bytes=64)
+
+        def bank(i):
+            return psum.tile([P, W], F32, name="bank%d" % i)
+
+        list1 = keep.tile([P, S // 16], U16, name="list1")
+        list2 = keep.tile([P, S // 16], U16, name="list2")
+        tabw = [held("tabw%d" % a, [P, T], U32) for a in range(2)]
+        tabs = held("tabs", [P, T], U8)
+        tab2w = held("tab2w", [P, T], U16)
+        tab2s = held("tab2s", [P, T], U8)
+        w1w_raw = held("staged_words", [P, 2 * H], U16)
+        w1s_raw = held("w1s_raw", [P, 2 * H], U8)
+        w1w = held("w1w", [P, 2 * H], U16)
+        w1s = held("w1s", [P, 2 * H], U8)
+        w2_raw = {}
+        w2_bf = [held("w2_bf%d" % b, [P, PACK * KP], BF16) for b in range(2)]
+        w2w = [held("w2w%d" % b, [P, KP], U32) for b in range(2)]
+        w2s = [held("w2s%d" % b, [P, KP], U8) for b in range(2)]
+        w3s = held("w3s", [P, 2 * N], U8)
+        noz = held("noz", [P, 2, PACK], F32)
+        neg_noz = held("neg_noz", [P, 2, PACK], F32)
+        gain = held("gain", [P, 2, PACK], F32)
+        rest = held("rest", [P, N // P], F32)
+        warm_in = held("warm_in", [P, 1], F32)
+        warm_out = held("warm_out", [P, 1], F32)
+        vw = [[held("vw%d_%d" % (a, u), [P, W], U32) for u in range(2)] for a in range(2)]
+        vs_both = held("vs_both", [P, S], U8)
+        vs_second = held("vs_second", [P, S], U8)
+        v2w = held("v2w", [P, S], U16)
+        v2s = held("v2s", [P, S], U8)
+
+        def load_scale_rows(queue, tile, scales):
+            for q in range(QUADS):
+                queue.dma_start(
+                    out=tile[32 * q : 32 * q + 4, :].bitcast(I32).rearrange("p (a c) -> p a c", a=scales.shape[0]),
+                    in_=scales[:, 4 * q : 4 * q + 4, :].bitcast(I32).rearrange("a r c -> r a c"),
+                )
+
+        def load_stacked_scale_rows(queue, tile, scales):
+            for q in range(QUADS):
+                queue.dma_start(
+                    out=tile[32 * q : 32 * q + 8, :].bitcast(I32),
+                    in_=scales[:, 4 * q : 4 * q + 4, :].bitcast(I32),
+                )
+
+        def lift_second_plane(second, both):
+            nc.sync.dma_start(out=second[0:100, :].bitcast(I32), in_=both[4:104, :].bitcast(I32))
+
+        def order_columns(ordered, raw):
+            nc.vector.tensor_copy(
+                out=ordered[:].rearrange("p (g t m) -> p g t m", t=PACK, m=P),
+                in_=raw[:].rearrange("p (g m t) -> p g t m", t=PACK, m=P),
+            )
+
+        def load_w2(b):
+            w2_raw[b] = held("w2_raw", [P, PACK, KP], F32)
+            nc.sync.dma_start(
+                out=w2_raw[b][:], in_=w2[:, b * KP : (b + 1) * KP].rearrange("(p j) c -> p j c", j=PACK)
+            )
+
+        def load_tab(a):
+            nc.sync.dma_start(out=tabw[a][:].bitcast(I32), in_=tab_words[a].rearrange("p t i -> p (t i)").bitcast(I32))
+
+        def gather_words(a):
+            for u in range(2):
+                nc.vector.tensor_copy(vw[a][u][:], tabw[a][:].indirect(half(list1, u)))
+
+        def half(lst, u):
+            return lst[:, u * (W // 16) : (u + 1) * (W // 16)]
+
+        nc.vector.memset(tabs[:].bitcast(I32), 0)
+        nc.vector.memset(tab2s[:].bitcast(I32), 0)
+        nc.vector.memset(w1s_raw[:].bitcast(I32), 0)
+        nc.vector.memset(warm_in[:], 0.0)
+        nc.scalar.activation(warm_out[:], warm_in[:], ACT.Silu)
+
+        nc.sync.dma_start(list1[:], offs)
+        nc.sync.dma_start(out=tab2w[:].bitcast(I32), in_=tab2_words[0].bitcast(I32))
+        load_stacked_scale_rows(nc.sync, tabs, tab_scales)
+        nc.sync.dma_start(list2[:], offs2)
+        load_w2(0)
+        load_scale_rows(nc.sync, tab2s, tab2_scales)
+        nc.sync.dma_start(
+            out=w1w_raw[:].bitcast(I32).rearrange("p (a c) -> p a c", a=2),
+            in_=w1_words.bitcast(I32).rearrange("a p c -> p a c"),
+        )
+        load_tab(0)
+        load_scale_rows(nc.sync, w1s_raw, w1_scales)
+
+        nc.gpsimd.memset(vs_second[:].bitcast(I32), 0)
+        nc.gpsimd.memset(w3s[:].bitcast(I32), 0)
+        load_scale_rows(nc.gpsimd, w3s, w3_scales)
+
+        nc.vector.tensor_copy(vs_both[:], tabs[:].indirect(list1[:]))
+        lift_second_plane(vs_second, vs_both)
+        load_tab(1)
+        nc.sync.dma_start(out=noz[:], in_=nozzle.rearrange("(b p t) -> p b t", b=2, t=PACK))
+        nc.sync.dma_start(out=gain[:], in_=flow.rearrange("(b p t) -> p b t", b=2, t=PACK))
+        nc.gpsimd.tensor_scalar(neg_noz[:], noz[:], -1.0, 0.0, ALU.mult, ALU.add)
+        nc.vector.tensor_copy(v2w[:], tab2w[:].indirect(list2[:]))
+        nc.vector.tensor_copy(v2s[:], tab2s[:].indirect(list2[:]))
+
+        def cast_w2(b):
+            nc.scalar.copy(
+                out=w2_bf[b][:].rearrange("p (t m j) -> p m j t", t=PACK, j=PACK),
+                in_=w2_raw[b][:].rearrange("p j (m t) -> p m j t", t=PACK),
+            )
+
+        def quantize_w2(b):
+            nc.vector.quantize_mx(out=w2w[b][:].bitcast(FP8X4), scales=w2s[b][:], in_=w2_bf[b][:])
+
+        allowed = {}
+        side = [0]
+
+        def make_allowed(b, u):
+            for t in range(PACK):
+                acc = bank(side[0] % 3)
+                side.append(side.pop() + 1)
+                cols = slice(t * P, (t + 1) * P)
+                toks = slice(u * W, (u + 1) * W)
+                nc.tensor.matmul_mx(
+                    out=acc[:], lhsT=w2w[b][:, cols].bitcast(FP8X4), lhsT_scale=w2s[b][:, cols],
+                    rhs=v2w[:, toks].bitcast(FP4X4), rhs_scale=v2s[:, toks], start=True, stop=True,
+                )
+                allowed[b, u, t] = held("allowed%d_%d_%d" % (b, u, t), [P, W], F32)
+                nc.scalar.copy(out=allowed[b, u, t][:], in_=acc[:])
+
+        cast_w2(0)
+        load_w2(1)
+        quantize_w2(0)
+        make_allowed(0, 0)
+        make_allowed(0, 1)
+        order_columns(w1w, w1w_raw)
+        w3w = held("staged_words", [P, 2 * N], U32)
+        nc.sync.dma_start(
+            out=w3w[:].bitcast(I32).rearrange("p (a c) -> p a c", a=2),
+            in_=w3_words.rearrange("a p c i -> p a (c i)").bitcast(I32),
+        )
+        with nc.allow_non_contiguous_dma(reason="one idle value a partition"):
+            nc.sync.dma_start(out=rest[:], in_=idle.rearrange("(i p) -> p i", p=P))
+        gather_words(0)
+        order_columns(w1s, w1s_raw)
+        gather_words(1)
+        vs = [vs_both, vs_second]
+
+
+        units = [(0, 0), (0, 1), (1, 0), (1, 1)]
+        demand = {}
+        act = {}
+        h_bf = {}
+        hw = {}
+        hs = {}
+        whole = slice(0, W)
+        first, second = slice(0, W // 2), slice(W // 2, W)
+
+        def make_demand(k, t):
+            b, u = units[k]
+            demand[k, t] = bank(3 + (PACK * k + t) % 5)
+            toks = slice(u * W, (u + 1) * W)
+            for a in range(2):
+                cols = slice(a * H + b * KP + t * P, a * H + b * KP + (t + 1) * P)
+                nc.tensor.matmul_mx(
+                    out=demand[k, t][:], lhsT=w1w[:, cols].bitcast(FP4X4), lhsT_scale=w1s[:, cols],
+                    rhs=vw[a][u][:].bitcast(FP8X4), rhs_scale=vs[a][:, toks], start=(a == 0), stop=(a == 1),
+                )
+            if t == 0:
+                act[k] = ring.tile([P, PACK, W], F32, name="act")
+                h_bf[k] = ring.tile([P, PACK * W], BF16, name="h_bf", align_bytes=64)
+                hw[k] = held("hw%d" % k, [P, W], U32)
+                hs[k] = held("hs%d" % k, [P, W], U8)
+
+        def dose(k, t, part):
+            b, u = units[k]
+            least = ring.tile([P, part.stop - part.start], F32, name="least", bufs=4)
+            nc.vector.tensor_tensor(least[:], demand[k, t][:, part], allowed[b, u, t][:, part], ALU.min)
+            nc.scalar.activation(act[k][:, t, part], least[:], ACT.Silu, bias=neg_noz[:, b, t : t + 1])
+
+        def apply_gain(k, part):
+            b, u = units[k]
+            pairs = (part.stop - part.start) // 2
+            nc.vector.tensor_tensor(
+                h_bf[k][:, PACK * part.start : PACK * part.stop].rearrange("p (c i t) -> p c t i", i=2, t=PACK),
+                act[k][:, :, part].rearrange("p t (c i) -> p c t i", i=2),
+                gain[:, b, :].unsqueeze(1).unsqueeze(3).to_broadcast([P, pairs, PACK, 2]),
+                ALU.mult,
+            )
+
+        def quantize_h(k, part):
+            nc.vector.quantize_mx(
+                out=hw[k][:, part].bitcast(FP8X4), scales=hs[k][:, part],
+                in_=h_bf[k][:, PACK * part.start : PACK * part.stop],
+            )
+
+        def valve_pass(acc, i, b, u, part):
+            k = units.index((b, u))
+            cols = slice(b * N + i * P, b * N + (i + 1) * P)
+            nc.tensor.matmul_mx(
+                out=acc[:, part], lhsT=w3w[:, cols].bitcast(FP8X4), lhsT_scale=w3s[:, cols],
+                rhs=hw[k][:, part].bitcast(FP8X4), rhs_scale=hs[k][:, part], start=(b == 0), stop=(b == 1),
+            )
+
+        def finish(acc, i, u, part, on_vector):
+            res = held("res%d_%d_%d" % (i, u, part.start), [P, part.stop - part.start], F32)
+            if on_vector:
+                nc.vector.tensor_scalar(res[:], acc[:, part], rest[:, i : i + 1], None, ALU.add)
+            else:
+                nc.scalar.activation(res[:], acc[:, part], ACT.Identity, bias=rest[:, i : i + 1])
+            nc.sync.dma_start(out=out[i * P : (i + 1) * P, u * W + part.start : u * W + part.stop], in_=res[:])
+
+        for t in range(PACK):
+            make_demand(0, t)
+            dose(0, t, whole)
+        cast_w2(1)
+        for k in range(1, 4):
+            part = whole if k < 3 else first
+            for t in range(PACK):
+                make_demand(k, t)
+                dose(k, t, part)
+                if t == 0:
+                    apply_gain(k - 1, whole)
+                if t == 1:
+                    quantize_h(k - 1, whole)
+                if k == 1 and t == 1:
+                    quantize_w2(1)
+                    make_allowed(1, 0)
+            if k == 1:
+                make_allowed(1, 1)
+        for i in range(4):
+            acc = bank(i % 3)
+            valve_pass(acc, i, 0, 0, whole)
+            valve_pass(acc, i, 1, 0, whole)
+            finish(acc, i, 0, whole, False)
+        for t in range(PACK - 1):
+            dose(3, t, second)
+        apply_gain(3, first)
+        dose(3, PACK - 1, second)
+        early = [bank(j) for j in (4, 1, 2, 0)]
+        late = [bank(j) for j in (5, 6, 7, 3)]
+        for i in range(4):
+            valve_pass(early[i], i, 0, 1, first)
+        quantize_h(3, first)
+        apply_gain(3, second)
+        for i in range(4):
+            valve_pass(early[i], i, 1, 1, first)
+            finish(early[i], i, 1, first, False)
+        for i in range(4):
+            valve_pass(late[i], i, 0, 1, second)
+        quantize_h(3, second)
+        for i in range(4):
+            valve_pass(late[i], i, 1, 1, second)
+            finish(late[i], i, 1, second, i % 2 == 1)

@@ -105,18 +105,18 @@ def tile_list_orchard_spray_dosing_kernel(
         def half(lst, u):
             return lst[:, u * (W // 16) : (u + 1) * (W // 16)]
 
-        nc.vector.memset(tabs[:].bitcast(I32), 0)
         nc.vector.memset(tab2s[:].bitcast(I32), 0)
+        nc.vector.memset(tabs[:].bitcast(I32), 0)
         nc.vector.memset(w1s_raw[:].bitcast(I32), 0)
         nc.vector.memset(warm_in[:], 0.0)
         nc.scalar.activation(warm_out[:], warm_in[:], ACT.Silu)
 
-        nc.sync.dma_start(list1[:], offs)
-        nc.sync.dma_start(out=tab2w[:].bitcast(I32), in_=tab2_words[0].bitcast(I32))
-        load_stacked_scale_rows(nc.sync, tabs, tab_scales)
         nc.sync.dma_start(list2[:], offs2)
-        load_w2(0)
+        nc.sync.dma_start(out=tab2w[:].bitcast(I32), in_=tab2_words[0].bitcast(I32))
         load_scale_rows(nc.sync, tab2s, tab2_scales)
+        load_w2(0)
+        nc.sync.dma_start(list1[:], offs)
+        load_stacked_scale_rows(nc.sync, tabs, tab_scales)
         nc.sync.dma_start(
             out=w1w_raw[:].bitcast(I32).rearrange("p (a c) -> p a c", a=2),
             in_=w1_words.bitcast(I32).rearrange("a p c -> p a c"),
@@ -124,23 +124,19 @@ def tile_list_orchard_spray_dosing_kernel(
         load_tab(0)
         load_scale_rows(nc.sync, w1s_raw, w1_scales)
 
-        nc.gpsimd.memset(vs_second[:].bitcast(I32), 0)
-        nc.gpsimd.memset(w3s[:].bitcast(I32), 0)
-        load_scale_rows(nc.gpsimd, w3s, w3_scales)
+        nc.vector.memset(vs_second[:].bitcast(I32), 0)
+        nc.vector.memset(w3s[:].bitcast(I32), 0)
 
-        nc.vector.tensor_copy(vs_both[:], tabs[:].indirect(list1[:]))
-        lift_second_plane(vs_second, vs_both)
+        nc.vector.tensor_copy(v2w[:], tab2w[:].indirect(list2[:]))
+        nc.vector.tensor_copy(v2s[:], tab2s[:].indirect(list2[:]))
         load_tab(1)
         nc.sync.dma_start(out=noz[:], in_=nozzle.rearrange("(b p t) -> p b t", b=2, t=PACK))
         nc.sync.dma_start(out=gain[:], in_=flow.rearrange("(b p t) -> p b t", b=2, t=PACK))
-        nc.gpsimd.tensor_scalar(neg_noz[:], noz[:], -1.0, 0.0, ALU.mult, ALU.add)
-        nc.vector.tensor_copy(v2w[:], tab2w[:].indirect(list2[:]))
-        nc.vector.tensor_copy(v2s[:], tab2s[:].indirect(list2[:]))
 
         def cast_w2(b):
             nc.scalar.copy(
-                out=w2_bf[b][:].rearrange("p (t m j) -> p m j t", t=PACK, j=PACK),
-                in_=w2_raw[b][:].rearrange("p j (m t) -> p m j t", t=PACK),
+                out=w2_bf[b][:].rearrange("p (s e m j) -> p s m j e", s=2, e=2, j=PACK),
+                in_=w2_raw[b][:].rearrange("p j (m s e) -> p s m j e", s=2, e=2),
             )
 
         def quantize_w2(b):
@@ -163,8 +159,10 @@ def tile_list_orchard_spray_dosing_kernel(
                 nc.scalar.copy(out=allowed[b, u, t][:], in_=acc[:])
 
         cast_w2(0)
-        load_w2(1)
         quantize_w2(0)
+        nc.vector.tensor_copy(vs_both[:], tabs[:].indirect(list1[:]))
+        lift_second_plane(vs_second, vs_both)
+        load_w2(1)
         make_allowed(0, 0)
         make_allowed(0, 1)
         order_columns(w1w, w1w_raw)
@@ -173,6 +171,7 @@ def tile_list_orchard_spray_dosing_kernel(
             out=w3w[:].bitcast(I32).rearrange("p (a c) -> p a c", a=2),
             in_=w3_words.rearrange("a p c i -> p a (c i)").bitcast(I32),
         )
+        load_scale_rows(nc.sync, w3s, w3_scales)
         with nc.allow_non_contiguous_dma(reason="one idle value a partition"):
             nc.sync.dma_start(out=rest[:], in_=idle.rearrange("(i p) -> p i", p=P))
         gather_words(0)
@@ -201,14 +200,14 @@ def tile_list_orchard_spray_dosing_kernel(
                     rhs=vw[a][u][:].bitcast(FP8X4), rhs_scale=vs[a][:, toks], start=(a == 0), stop=(a == 1),
                 )
             if t == 0:
-                act[k] = ring.tile([P, PACK, W], F32, name="act")
+                act[k] = ring.tile([P, PACK, W], F32, name="act", bufs=3)
                 h_bf[k] = ring.tile([P, PACK * W], BF16, name="h_bf", align_bytes=64)
                 hw[k] = held("hw%d" % k, [P, W], U32)
                 hs[k] = held("hs%d" % k, [P, W], U8)
 
         def dose(k, t, part):
             b, u = units[k]
-            least = ring.tile([P, part.stop - part.start], F32, name="least", bufs=4)
+            least = ring.tile([P, part.stop - part.start], F32, name="least", bufs=8)
             nc.vector.tensor_tensor(least[:], demand[k, t][:, part], allowed[b, u, t][:, part], ALU.min)
             nc.scalar.activation(act[k][:, t, part], least[:], ACT.Silu, bias=neg_noz[:, b, t : t + 1])
 
@@ -244,39 +243,49 @@ def tile_list_orchard_spray_dosing_kernel(
                 nc.scalar.activation(res[:], acc[:, part], ACT.Identity, bias=rest[:, i : i + 1])
             nc.sync.dma_start(out=out[i * P : (i + 1) * P, u * W + part.start : u * W + part.stop], in_=res[:])
 
-        for t in range(PACK):
-            make_demand(0, t)
-            dose(0, t, whole)
-        cast_w2(1)
-        for k in range(1, 4):
-            part = whole if k < 3 else first
+        def dose_unit(k, part):
             for t in range(PACK):
                 make_demand(k, t)
                 dose(k, t, part)
-                if t == 0:
-                    apply_gain(k - 1, whole)
-                if t == 1:
-                    quantize_h(k - 1, whole)
-                if k == 1 and t == 1:
-                    quantize_w2(1)
-                    make_allowed(1, 0)
-            if k == 1:
-                make_allowed(1, 1)
+
+        nc.scalar.activation(neg_noz[:], noz[:], ACT.Copy, scale=-1.0)
+        cast_w2(1)
+        dose_unit(0, whole)
+        quantize_w2(1)
+        make_allowed(1, 0)
+        dose_unit(1, whole)
+        apply_gain(0, whole)
+        make_allowed(1, 1)
+        make_demand(2, 0)
+        dose(2, 0, whole)
+        quantize_h(0, whole)
+        for t in range(1, PACK):
+            make_demand(2, t)
+            dose(2, t, whole)
+        apply_gain(1, whole)
+        make_demand(3, 0)
+        dose(3, 0, first)
+        quantize_h(1, whole)
+        for t in range(1, PACK):
+            make_demand(3, t)
+            dose(3, t, first)
+        apply_gain(2, whole)
+        dose(3, 0, second)
+        quantize_h(2, whole)
+        for t in range(1, PACK):
+            dose(3, t, second)
         for i in range(4):
             acc = bank(i % 3)
             valve_pass(acc, i, 0, 0, whole)
             valve_pass(acc, i, 1, 0, whole)
             finish(acc, i, 0, whole, False)
-        for t in range(PACK - 1):
-            dose(3, t, second)
         apply_gain(3, first)
-        dose(3, PACK - 1, second)
-        early = [bank(j) for j in (4, 1, 2, 0)]
-        late = [bank(j) for j in (5, 6, 7, 3)]
+        early = [bank(j) for j in (4, 5, 6, 7)]
+        late = [bank(j) for j in (3, 1, 2, 0)]
         for i in range(4):
             valve_pass(early[i], i, 0, 1, first)
-        quantize_h(3, first)
         apply_gain(3, second)
+        quantize_h(3, first)
         for i in range(4):
             valve_pass(early[i], i, 1, 1, first)
             finish(early[i], i, 1, first, False)

@@ -115,6 +115,7 @@ def tile_list_orchard_spray_dosing_kernel(
         nc.sync.dma_start(out=tab2w[:].bitcast(I32), in_=tab2_words[0].bitcast(I32))
         load_scale_rows(nc.sync, tab2s, tab2_scales)
         load_w2(0)
+        nc.sync.dma_start(out=noz[:], in_=nozzle.rearrange("(b p t) -> p b t", b=2, t=PACK))
         nc.sync.dma_start(list1[:], offs)
         load_stacked_scale_rows(nc.sync, tabs, tab_scales)
         nc.sync.dma_start(
@@ -130,7 +131,6 @@ def tile_list_orchard_spray_dosing_kernel(
         nc.vector.tensor_copy(v2w[:], tab2w[:].indirect(list2[:]))
         nc.vector.tensor_copy(v2s[:], tab2s[:].indirect(list2[:]))
         load_tab(1)
-        nc.sync.dma_start(out=noz[:], in_=nozzle.rearrange("(b p t) -> p b t", b=2, t=PACK))
         nc.sync.dma_start(out=gain[:], in_=flow.rearrange("(b p t) -> p b t", b=2, t=PACK))
 
         def cast_w2(b):
@@ -156,9 +156,10 @@ def tile_list_orchard_spray_dosing_kernel(
                     rhs=v2w[:, toks].bitcast(FP4X4), rhs_scale=v2s[:, toks], start=True, stop=True,
                 )
                 allowed[b, u, t] = held("allowed%d_%d_%d" % (b, u, t), [P, W], F32)
-                nc.scalar.copy(out=allowed[b, u, t][:], in_=acc[:])
+                nc.scalar.activation(allowed[b, u, t][:], acc[:], ACT.Identity, bias=neg_noz[:, b, t : t + 1])
 
         cast_w2(0)
+        nc.scalar.activation(neg_noz[:], noz[:], ACT.Copy, scale=-1.0)
         quantize_w2(0)
         nc.vector.tensor_copy(vs_both[:], tabs[:].indirect(list1[:]))
         lift_second_plane(vs_second, vs_both)
@@ -182,6 +183,7 @@ def tile_list_orchard_spray_dosing_kernel(
 
         units = [(0, 0), (0, 1), (1, 0), (1, 1)]
         demand = {}
+        least = {}
         act = {}
         h_bf = {}
         hw = {}
@@ -200,24 +202,32 @@ def tile_list_orchard_spray_dosing_kernel(
                     rhs=vw[a][u][:].bitcast(FP8X4), rhs_scale=vs[a][:, toks], start=(a == 0), stop=(a == 1),
                 )
             if t == 0:
-                act[k] = ring.tile([P, PACK, W], F32, name="act", bufs=3)
+                least[k] = ring.tile([P, PACK, W], F32, name="least", bufs=2)
+                act[k] = ring.tile([P, PACK * W], F32, name="act", bufs=2)
                 h_bf[k] = ring.tile([P, PACK * W], BF16, name="h_bf", align_bytes=64)
                 hw[k] = held("hw%d" % k, [P, W], U32)
                 hs[k] = held("hs%d" % k, [P, W], U8)
 
         def dose(k, t, part):
             b, u = units[k]
-            least = ring.tile([P, part.stop - part.start], F32, name="least", bufs=8)
-            nc.vector.tensor_tensor(least[:], demand[k, t][:, part], allowed[b, u, t][:, part], ALU.min)
-            nc.scalar.activation(act[k][:, t, part], least[:], ACT.Silu, bias=neg_noz[:, b, t : t + 1])
+            nc.vector.scalar_tensor_tensor(
+                least[k][:, t, part], demand[k, t][:, part], neg_noz[:, b, t : t + 1], allowed[b, u, t][:, part],
+                ALU.add, ALU.min,
+            )
+            if t == PACK - 1:
+                nc.scalar.activation(
+                    act[k][:, PACK * part.start : PACK * part.stop].rearrange("p (c i t) -> p c t i", i=2, t=PACK),
+                    least[k][:, :, part].rearrange("p t (c i) -> p c t i", i=2),
+                    ACT.Silu,
+                )
 
         def apply_gain(k, part):
             b, u = units[k]
-            pairs = (part.stop - part.start) // 2
+            packed = slice(PACK * part.start, PACK * part.stop)
             nc.vector.tensor_tensor(
-                h_bf[k][:, PACK * part.start : PACK * part.stop].rearrange("p (c i t) -> p c t i", i=2, t=PACK),
-                act[k][:, :, part].rearrange("p t (c i) -> p c t i", i=2),
-                gain[:, b, :].unsqueeze(1).unsqueeze(3).to_broadcast([P, pairs, PACK, 2]),
+                h_bf[k][:, packed].rearrange("p (c t) -> p c t", t=PACK),
+                act[k][:, packed].rearrange("p (c t) -> p c t", t=PACK),
+                gain[:, b, :].unsqueeze(1).to_broadcast([P, part.stop - part.start, PACK]),
                 ALU.mult,
             )
 
@@ -248,7 +258,6 @@ def tile_list_orchard_spray_dosing_kernel(
                 make_demand(k, t)
                 dose(k, t, part)
 
-        nc.scalar.activation(neg_noz[:], noz[:], ACT.Copy, scale=-1.0)
         cast_w2(1)
         dose_unit(0, whole)
         quantize_w2(1)

@@ -45,7 +45,7 @@ def tile_list_orchard_spray_dosing_kernel(
         tabs = held("tabs", [P, T], U8)
         tab2w = held("tab2w", [P, T], U16)
         tab2s = held("tab2s", [P, T], U8)
-        w1w_raw = held("staged_words", [P, 2 * H], U16)
+        w1w_raw = held("w1w_raw", [P, 2 * H], U16)
         w1s_raw = held("w1s_raw", [P, 2 * H], U8)
         w1w = held("w1w", [P, 2 * H], U16)
         w1s = held("w1s", [P, 2 * H], U8)
@@ -53,16 +53,12 @@ def tile_list_orchard_spray_dosing_kernel(
         w2_bf = [held("w2_bf%d" % b, [P, PACK * KP], BF16) for b in range(2)]
         w2w = [held("w2w%d" % b, [P, KP], U32) for b in range(2)]
         w2s = [held("w2s%d" % b, [P, KP], U8) for b in range(2)]
-        w3s = held("w3s", [P, 2 * N], U8)
         noz = held("noz", [P, 2, PACK], F32)
         neg_noz = held("neg_noz", [P, 2, PACK], F32)
-        gain = held("gain", [P, 2, PACK], F32)
-        rest = held("rest", [P, N // P], F32)
         warm_in = held("warm_in", [P, 1], F32)
         warm_out = held("warm_out", [P, 1], F32)
         vw = [[held("vw%d_%d" % (a, u), [P, W], U32) for u in range(2)] for a in range(2)]
-        vs_both = held("vs_both", [P, S], U8)
-        vs_second = held("vs_second", [P, S], U8)
+        vs = [held("vs%d" % a, [P, S], U8) for a in range(2)]
         v2w = held("v2w", [P, S], U16)
         v2s = held("v2s", [P, S], U8)
 
@@ -76,12 +72,12 @@ def tile_list_orchard_spray_dosing_kernel(
         def load_stacked_scale_rows(queue, tile, scales):
             for q in range(QUADS):
                 queue.dma_start(
-                    out=tile[32 * q : 32 * q + 8, :].bitcast(I32),
+                    out=tile[32 * q + 4 : 32 * q + 12, :].bitcast(I32),
                     in_=scales[:, 4 * q : 4 * q + 4, :].bitcast(I32),
                 )
 
-        def lift_second_plane(second, both):
-            nc.sync.dma_start(out=second[0:100, :].bitcast(I32), in_=both[4:104, :].bitcast(I32))
+        def lift_plane(plane, both, a):
+            nc.sync.dma_start(out=plane[0:100, :].bitcast(I32), in_=both[4 + 4 * a : 104 + 4 * a, :].bitcast(I32))
 
         def order_columns(ordered, raw):
             nc.vector.tensor_copy(
@@ -90,7 +86,7 @@ def tile_list_orchard_spray_dosing_kernel(
             )
 
         def load_w2(b):
-            w2_raw[b] = held("w2_raw", [P, PACK, KP], F32)
+            w2_raw[b] = held(("w2_raw", "tabs")[b], [P, PACK, KP], F32)
             nc.sync.dma_start(
                 out=w2_raw[b][:], in_=w2[:, b * KP : (b + 1) * KP].rearrange("(p j) c -> p j c", j=PACK)
             )
@@ -105,9 +101,12 @@ def tile_list_orchard_spray_dosing_kernel(
         def half(lst, u):
             return lst[:, u * (W // 16) : (u + 1) * (W // 16)]
 
+        nc.gpsimd.memset(tabs[:].bitcast(I32), 0)
+        load_stacked_scale_rows(nc.gpsimd, tabs, tab_scales)
         nc.vector.memset(tab2s[:].bitcast(I32), 0)
-        nc.vector.memset(tabs[:].bitcast(I32), 0)
         nc.vector.memset(w1s_raw[:].bitcast(I32), 0)
+        for a in range(2):
+            nc.vector.memset(vs[a][:].bitcast(I32), 0)
         nc.vector.memset(warm_in[:], 0.0)
         nc.scalar.activation(warm_out[:], warm_in[:], ACT.Silu)
 
@@ -115,23 +114,18 @@ def tile_list_orchard_spray_dosing_kernel(
         nc.sync.dma_start(out=tab2w[:].bitcast(I32), in_=tab2_words[0].bitcast(I32))
         load_scale_rows(nc.sync, tab2s, tab2_scales)
         load_w2(0)
-        nc.sync.dma_start(out=noz[:], in_=nozzle.rearrange("(b p t) -> p b t", b=2, t=PACK))
         nc.sync.dma_start(list1[:], offs)
-        load_stacked_scale_rows(nc.sync, tabs, tab_scales)
         nc.sync.dma_start(
             out=w1w_raw[:].bitcast(I32).rearrange("p (a c) -> p a c", a=2),
             in_=w1_words.bitcast(I32).rearrange("a p c -> p a c"),
         )
         load_tab(0)
         load_scale_rows(nc.sync, w1s_raw, w1_scales)
-
-        nc.vector.memset(vs_second[:].bitcast(I32), 0)
-        nc.vector.memset(w3s[:].bitcast(I32), 0)
+        load_tab(1)
+        nc.sync.dma_start(out=noz[:], in_=nozzle.rearrange("(b p t) -> p b t", b=2, t=PACK))
 
         nc.vector.tensor_copy(v2w[:], tab2w[:].indirect(list2[:]))
         nc.vector.tensor_copy(v2s[:], tab2s[:].indirect(list2[:]))
-        load_tab(1)
-        nc.sync.dma_start(out=gain[:], in_=flow.rearrange("(b p t) -> p b t", b=2, t=PACK))
 
         def cast_w2(b):
             nc.scalar.copy(
@@ -156,34 +150,37 @@ def tile_list_orchard_spray_dosing_kernel(
                     rhs=v2w[:, toks].bitcast(FP4X4), rhs_scale=v2s[:, toks], start=True, stop=True,
                 )
                 allowed[b, u, t] = held("allowed%d_%d_%d" % (b, u, t), [P, W], F32)
-                nc.scalar.activation(allowed[b, u, t][:], acc[:], ACT.Identity, bias=neg_noz[:, b, t : t + 1])
+                nc.scalar.copy(out=allowed[b, u, t][:], in_=acc[:])
 
         cast_w2(0)
-        nc.scalar.activation(neg_noz[:], noz[:], ACT.Copy, scale=-1.0)
+        order_columns(w1w, w1w_raw)
         quantize_w2(0)
-        nc.vector.tensor_copy(vs_both[:], tabs[:].indirect(list1[:]))
-        lift_second_plane(vs_second, vs_both)
-        load_w2(1)
         make_allowed(0, 0)
         make_allowed(0, 1)
-        order_columns(w1w, w1w_raw)
-        w3w = held("staged_words", [P, 2 * N], U32)
+        vs_both = held("w2_bf0", [P, S], U8)
+        nc.vector.tensor_copy(vs_both[:], tabs[:].indirect(list1[:]))
+        for a in range(2):
+            lift_plane(vs[a], vs_both, a)
+        load_w2(1)
+        gather_words(0)
+        w3w = held("tabw0", [P, 2 * N], U32)
         nc.sync.dma_start(
             out=w3w[:].bitcast(I32).rearrange("p (a c) -> p a c", a=2),
             in_=w3_words.rearrange("a p c i -> p a (c i)").bitcast(I32),
         )
+        late_vectors = held("w2_bf0", [P, 4 * PACK], F32)
+        gain = late_vectors[:, 0 : 2 * PACK].rearrange("p (b t) -> p b t", b=2)
+        rest = late_vectors[:, 2 * PACK : 3 * PACK]
+        nc.sync.dma_start(out=gain, in_=flow.rearrange("(b p t) -> p b t", b=2, t=PACK))
+        order_columns(w1s, w1s_raw)
+        w3s = w1s_raw[:, 0 : 2 * N]
         load_scale_rows(nc.sync, w3s, w3_scales)
         with nc.allow_non_contiguous_dma(reason="one idle value a partition"):
-            nc.sync.dma_start(out=rest[:], in_=idle.rearrange("(i p) -> p i", p=P))
-        gather_words(0)
-        order_columns(w1s, w1s_raw)
+            nc.sync.dma_start(out=rest, in_=idle.rearrange("(i p) -> p i", p=P))
         gather_words(1)
-        vs = [vs_both, vs_second]
-
 
         units = [(0, 0), (0, 1), (1, 0), (1, 1)]
         demand = {}
-        least = {}
         act = {}
         h_bf = {}
         hw = {}
@@ -202,32 +199,25 @@ def tile_list_orchard_spray_dosing_kernel(
                     rhs=vw[a][u][:].bitcast(FP8X4), rhs_scale=vs[a][:, toks], start=(a == 0), stop=(a == 1),
                 )
             if t == 0:
-                least[k] = ring.tile([P, PACK, W], F32, name="least", bufs=2)
-                act[k] = ring.tile([P, PACK * W], F32, name="act", bufs=2)
+                act[k] = ring.tile([P, PACK, W], F32, name="act")
                 h_bf[k] = ring.tile([P, PACK * W], BF16, name="h_bf", align_bytes=64)
                 hw[k] = held("hw%d" % k, [P, W], U32)
                 hs[k] = held("hs%d" % k, [P, W], U8)
 
-        def dose(k, t, part):
+        def dose(k, t):
             b, u = units[k]
-            nc.vector.scalar_tensor_tensor(
-                least[k][:, t, part], demand[k, t][:, part], neg_noz[:, b, t : t + 1], allowed[b, u, t][:, part],
-                ALU.add, ALU.min,
-            )
-            if t == PACK - 1:
-                nc.scalar.activation(
-                    act[k][:, PACK * part.start : PACK * part.stop].rearrange("p (c i t) -> p c t i", i=2, t=PACK),
-                    least[k][:, :, part].rearrange("p t (c i) -> p c t i", i=2),
-                    ACT.Silu,
-                )
+            make_demand(k, t)
+            least = ring.tile([P, W], F32, name="least", bufs=8)
+            nc.vector.tensor_tensor(least[:], demand[k, t][:], allowed[b, u, t][:], ALU.min)
+            nc.scalar.activation(act[k][:, t, :], least[:], ACT.Silu, bias=neg_noz[:, b, t : t + 1])
 
         def apply_gain(k, part):
             b, u = units[k]
-            packed = slice(PACK * part.start, PACK * part.stop)
+            pairs = (part.stop - part.start) // 2
             nc.vector.tensor_tensor(
-                h_bf[k][:, packed].rearrange("p (c t) -> p c t", t=PACK),
-                act[k][:, packed].rearrange("p (c t) -> p c t", t=PACK),
-                gain[:, b, :].unsqueeze(1).to_broadcast([P, part.stop - part.start, PACK]),
+                h_bf[k][:, PACK * part.start : PACK * part.stop].rearrange("p (c i t) -> p c t i", i=2, t=PACK),
+                act[k][:, :, part].rearrange("p t (c i) -> p c t i", i=2),
+                gain[:, b, :].unsqueeze(1).unsqueeze(3).to_broadcast([P, pairs, PACK, 2]),
                 ALU.mult,
             )
 
@@ -253,54 +243,44 @@ def tile_list_orchard_spray_dosing_kernel(
                 nc.scalar.activation(res[:], acc[:, part], ACT.Identity, bias=rest[:, i : i + 1])
             nc.sync.dma_start(out=out[i * P : (i + 1) * P, u * W + part.start : u * W + part.stop], in_=res[:])
 
-        def dose_unit(k, part):
-            for t in range(PACK):
-                make_demand(k, t)
-                dose(k, t, part)
-
+        nc.scalar.activation(neg_noz[:], noz[:], ACT.Copy, scale=-1.0)
         cast_w2(1)
-        dose_unit(0, whole)
+        for k in range(2):
+            for t in range(PACK):
+                dose(k, t)
         quantize_w2(1)
         make_allowed(1, 0)
-        dose_unit(1, whole)
-        apply_gain(0, whole)
         make_allowed(1, 1)
-        make_demand(2, 0)
-        dose(2, 0, whole)
+        apply_gain(0, whole)
         quantize_h(0, whole)
-        for t in range(1, PACK):
-            make_demand(2, t)
-            dose(2, t, whole)
         apply_gain(1, whole)
-        make_demand(3, 0)
-        dose(3, 0, first)
+        dose(2, 0)
         quantize_h(1, whole)
         for t in range(1, PACK):
-            make_demand(3, t)
-            dose(3, t, first)
+            dose(2, t)
+        for t in range(PACK - 1):
+            dose(3, t)
         apply_gain(2, whole)
-        dose(3, 0, second)
+        dose(3, PACK - 1)
         quantize_h(2, whole)
-        for t in range(1, PACK):
-            dose(3, t, second)
+        lead = [bank(j) for j in (0, 1, 2, 4)]
+        early = [bank(j) for j in (5, 6, 7, 3)]
         for i in range(4):
-            acc = bank(i % 3)
-            valve_pass(acc, i, 0, 0, whole)
-            valve_pass(acc, i, 1, 0, whole)
-            finish(acc, i, 0, whole, False)
-        apply_gain(3, first)
-        early = [bank(j) for j in (4, 5, 6, 7)]
-        late = [bank(j) for j in (3, 1, 2, 0)]
+            valve_pass(lead[i], i, 0, 0, whole)
         for i in range(4):
             valve_pass(early[i], i, 0, 1, first)
+        for i in range(4):
+            valve_pass(lead[i], i, 1, 0, whole)
+            finish(lead[i], i, 0, whole, False)
+        apply_gain(3, first)
         apply_gain(3, second)
         quantize_h(3, first)
-        for i in range(4):
-            valve_pass(early[i], i, 1, 1, first)
-            finish(early[i], i, 1, first, False)
-        for i in range(4):
-            valve_pass(late[i], i, 0, 1, second)
         quantize_h(3, second)
         for i in range(4):
+            valve_pass(early[i], i, 1, 1, first)
+            finish(early[i], i, 1, first, i >= 2)
+        late = [bank(j) for j in (0, 1, 2, 4)]
+        for i in range(4):
+            valve_pass(late[i], i, 0, 1, second)
             valve_pass(late[i], i, 1, 1, second)
             finish(late[i], i, 1, second, i % 2 == 1)

@@ -41,7 +41,7 @@ def tile_list_orchard_spray_dosing_kernel(
 
         list1 = keep.tile([P, S // 16], U16, name="list1")
         list2 = keep.tile([P, S // 16], U16, name="list2")
-        tabw = [held("tabw%d" % a, [P, T], U32) for a in range(2)]
+        tabw = {}
         tabs = held("tabs", [P, T], U8)
         tab2w = held("tab2w", [P, T], U16)
         tab2s = held("tab2s", [P, T], U8)
@@ -58,26 +58,23 @@ def tile_list_orchard_spray_dosing_kernel(
         warm_in = held("warm_in", [P, 1], F32)
         warm_out = held("warm_out", [P, 1], F32)
         vw = [[held("vw%d_%d" % (a, u), [P, W], U32) for u in range(2)] for a in range(2)]
-        vs = [held("vs%d" % a, [P, S], U8) for a in range(2)]
+        vs = held("vs", [P, 2 * S], U8)
+        vs_rows = held("vs_rows", [P, S], U8)
         v2w = held("v2w", [P, S], U16)
         v2s = held("v2s", [P, S], U8)
 
-        def load_scale_rows(queue, tile, scales):
-            for q in range(QUADS):
-                queue.dma_start(
-                    out=tile[32 * q : 32 * q + 4, :].bitcast(I32).rearrange("p (a c) -> p a c", a=scales.shape[0]),
-                    in_=scales[:, 4 * q : 4 * q + 4, :].bitcast(I32).rearrange("a r c -> r a c"),
+        def load_scale_rows(tile, scales):
+            for r in range(4):
+                nc.sync.dma_start(
+                    out=tile[r:P:32, :].bitcast(I32).rearrange("p (a c) -> p a c", a=scales.shape[0]),
+                    in_=scales.bitcast(I32).rearrange("a (q r) c -> r q a c", r=4)[r],
                 )
 
-        def load_stacked_scale_rows(queue, tile, scales):
-            for q in range(QUADS):
-                queue.dma_start(
-                    out=tile[32 * q + 4 : 32 * q + 12, :].bitcast(I32),
-                    in_=scales[:, 4 * q : 4 * q + 4, :].bitcast(I32),
-                )
-
-        def lift_plane(plane, both, a):
-            nc.sync.dma_start(out=plane[0:100, :].bitcast(I32), in_=both[4 + 4 * a : 104 + 4 * a, :].bitcast(I32))
+        def lift_rows(a, r):
+            nc.sync.dma_start(
+                out=vs[r:P:32, a * S : (a + 1) * S].bitcast(I32),
+                in_=vs_rows[16 * a + r : 16 * (a + 1) : 4, :].bitcast(I32),
+            )
 
         def order_columns(ordered, raw):
             nc.vector.tensor_copy(
@@ -86,12 +83,13 @@ def tile_list_orchard_spray_dosing_kernel(
             )
 
         def load_w2(b):
-            w2_raw[b] = held(("w2_raw", "tabs")[b], [P, PACK, KP], F32)
+            w2_raw[b] = held("w2_raw", [P, PACK, KP], F32)
             nc.sync.dma_start(
                 out=w2_raw[b][:], in_=w2[:, b * KP : (b + 1) * KP].rearrange("(p j) c -> p j c", j=PACK)
             )
 
         def load_tab(a):
+            tabw[a] = held(("tabs", "tab2s")[a], [P, T], U32)
             nc.sync.dma_start(out=tabw[a][:].bitcast(I32), in_=tab_words[a].rearrange("p t i -> p (t i)").bitcast(I32))
 
         def gather_words(a):
@@ -101,31 +99,37 @@ def tile_list_orchard_spray_dosing_kernel(
         def half(lst, u):
             return lst[:, u * (W // 16) : (u + 1) * (W // 16)]
 
-        nc.gpsimd.memset(tabs[:].bitcast(I32), 0)
-        load_stacked_scale_rows(nc.gpsimd, tabs, tab_scales)
         nc.vector.memset(tab2s[:].bitcast(I32), 0)
         nc.vector.memset(w1s_raw[:].bitcast(I32), 0)
-        for a in range(2):
-            nc.vector.memset(vs[a][:].bitcast(I32), 0)
+        nc.vector.memset(tabs[32:64, :].bitcast(I32), 0)
+        nc.vector.memset(tabs[64:P, :].bitcast(I32), 0)
+        nc.vector.memset(vs[:].bitcast(I32), 0)
         nc.vector.memset(warm_in[:], 0.0)
         nc.scalar.activation(warm_out[:], warm_in[:], ACT.Silu)
 
+        nc.sync.dma_start(list1[:], offs)
+        nc.sync.dma_start(out=tabs[0:32, :].bitcast(I32), in_=tab_scales.bitcast(I32).rearrange("a q t -> (a q) t"))
         nc.sync.dma_start(list2[:], offs2)
         nc.sync.dma_start(out=tab2w[:].bitcast(I32), in_=tab2_words[0].bitcast(I32))
-        load_scale_rows(nc.sync, tab2s, tab2_scales)
+        load_scale_rows(tab2s, tab2_scales)
         load_w2(0)
-        nc.sync.dma_start(list1[:], offs)
+        load_scale_rows(w1s_raw, w1_scales)
         nc.sync.dma_start(
             out=w1w_raw[:].bitcast(I32).rearrange("p (a c) -> p a c", a=2),
             in_=w1_words.bitcast(I32).rearrange("a p c -> p a c"),
         )
-        load_tab(0)
-        load_scale_rows(nc.sync, w1s_raw, w1_scales)
-        load_tab(1)
         nc.sync.dma_start(out=noz[:], in_=nozzle.rearrange("(b p t) -> p b t", b=2, t=PACK))
 
+        nc.vector.tensor_copy(vs_rows[:], tabs[:].indirect(list1[:]))
+        rows = [(a, r) for a in range(2) for r in range(4)]
+        for a, r in rows[:2]:
+            lift_rows(a, r)
+        load_tab(0)
+        for a, r in rows[2:]:
+            lift_rows(a, r)
         nc.vector.tensor_copy(v2w[:], tab2w[:].indirect(list2[:]))
         nc.vector.tensor_copy(v2s[:], tab2s[:].indirect(list2[:]))
+        load_tab(1)
 
         def cast_w2(b):
             nc.scalar.copy(
@@ -153,28 +157,25 @@ def tile_list_orchard_spray_dosing_kernel(
                 nc.scalar.copy(out=allowed[b, u, t][:], in_=acc[:])
 
         cast_w2(0)
+        order_columns(w1s, w1s_raw)
         order_columns(w1w, w1w_raw)
         quantize_w2(0)
         make_allowed(0, 0)
         make_allowed(0, 1)
-        vs_both = held("w2_bf0", [P, S], U8)
-        nc.vector.tensor_copy(vs_both[:], tabs[:].indirect(list1[:]))
-        for a in range(2):
-            lift_plane(vs[a], vs_both, a)
         load_w2(1)
         gather_words(0)
-        w3w = held("tabw0", [P, 2 * N], U32)
+        w3_bytes = held("tabs", [P, 2 * N + 2 * N // 4], U32)
+        w3w = w3_bytes[:, 0 : 2 * N]
         nc.sync.dma_start(
-            out=w3w[:].bitcast(I32).rearrange("p (a c) -> p a c", a=2),
+            out=w3w.bitcast(I32).rearrange("p (a c) -> p a c", a=2),
             in_=w3_words.rearrange("a p c i -> p a (c i)").bitcast(I32),
         )
         late_vectors = held("w2_bf0", [P, 4 * PACK], F32)
         gain = late_vectors[:, 0 : 2 * PACK].rearrange("p (b t) -> p b t", b=2)
         rest = late_vectors[:, 2 * PACK : 3 * PACK]
         nc.sync.dma_start(out=gain, in_=flow.rearrange("(b p t) -> p b t", b=2, t=PACK))
-        order_columns(w1s, w1s_raw)
-        w3s = w1s_raw[:, 0 : 2 * N]
-        load_scale_rows(nc.sync, w3s, w3_scales)
+        w3s = w3_bytes[:, 2 * N :].bitcast(U8)
+        load_scale_rows(w3s, w3_scales)
         with nc.allow_non_contiguous_dma(reason="one idle value a partition"):
             nc.sync.dma_start(out=rest, in_=idle.rearrange("(i p) -> p i", p=P))
         gather_words(1)
@@ -191,12 +192,11 @@ def tile_list_orchard_spray_dosing_kernel(
         def make_demand(k, t):
             b, u = units[k]
             demand[k, t] = bank(3 + (PACK * k + t) % 5)
-            toks = slice(u * W, (u + 1) * W)
             for a in range(2):
                 cols = slice(a * H + b * KP + t * P, a * H + b * KP + (t + 1) * P)
                 nc.tensor.matmul_mx(
                     out=demand[k, t][:], lhsT=w1w[:, cols].bitcast(FP4X4), lhsT_scale=w1s[:, cols],
-                    rhs=vw[a][u][:].bitcast(FP8X4), rhs_scale=vs[a][:, toks], start=(a == 0), stop=(a == 1),
+                    rhs=vw[a][u][:].bitcast(FP8X4), rhs_scale=vs[:, a * S + u * W : a * S + (u + 1) * W], start=(a == 0), stop=(a == 1),
                 )
             if t == 0:
                 act[k] = ring.tile([P, PACK, W], F32, name="act")

@@ -20,7 +20,10 @@ P = 128
 PACK = 4
 KP = P * PACK
 W = 512
-QUADS = 4
+ROWS = 4
+FIRST_ROW = 96
+SCALAR_VISITS = (448, 448, 448)
+LAST_CUTS = (0, 256, 512)
 
 
 def tile_list_orchard_spray_dosing_kernel(
@@ -30,7 +33,7 @@ def tile_list_orchard_spray_dosing_kernel(
     nc = tc.nc
     with ExitStack() as ctx:
         keep = ctx.enter_context(tc.tile_pool(name="keep", bufs=1))
-        ring = ctx.enter_context(tc.tile_pool(name="ring", bufs=2))
+        ring = ctx.enter_context(tc.tile_pool(name="ring", bufs=3))
         psum = ctx.enter_context(tc.psum_pool(name="psum", bufs=1))
 
         def held(name, shape, dtype):
@@ -41,39 +44,45 @@ def tile_list_orchard_spray_dosing_kernel(
 
         list1 = keep.tile([P, S // 16], U16, name="list1")
         list2 = keep.tile([P, S // 16], U16, name="list2")
-        tabw = {}
-        tabs = held("tabs", [P, T], U8)
-        tab2w = held("tab2w", [P, T], U16)
+        tabs = held("window_a", [P, T], U8)
         tab2s = held("tab2s", [P, T], U8)
+        tab2w = held("tab2w", [P, T], U16)
         w1w_raw = held("w1w_raw", [P, 2 * H], U16)
         w1s_raw = held("w1s_raw", [P, 2 * H], U8)
-        w1w = held("w1w", [P, 2 * H], U16)
         w1s = held("w1s", [P, 2 * H], U8)
-        w2_raw = {}
+        w2_raw = [held("w2_raw%d" % b, [P, PACK, KP], F32) for b in range(2)]
         w2_bf = [held("w2_bf%d" % b, [P, PACK * KP], BF16) for b in range(2)]
         w2w = [held("w2w%d" % b, [P, KP], U32) for b in range(2)]
         w2s = [held("w2s%d" % b, [P, KP], U8) for b in range(2)]
         noz = held("noz", [P, 2, PACK], F32)
         neg_noz = held("neg_noz", [P, 2, PACK], F32)
-        warm_in = held("warm_in", [P, 1], F32)
-        warm_out = held("warm_out", [P, 1], F32)
         vw = [[held("vw%d_%d" % (a, u), [P, W], U32) for u in range(2)] for a in range(2)]
-        vs = held("vs", [P, 2 * S], U8)
         vs_rows = held("vs_rows", [P, S], U8)
+        vs = held("vs", [P, 2 * S], U8)
         v2w = held("v2w", [P, S], U16)
         v2s = held("v2s", [P, S], U8)
+        tabw = {}
 
         def load_scale_rows(tile, scales):
-            for r in range(4):
+            for r in range(ROWS):
                 nc.sync.dma_start(
                     out=tile[r:P:32, :].bitcast(I32).rearrange("p (a c) -> p a c", a=scales.shape[0]),
-                    in_=scales.bitcast(I32).rearrange("a (q r) c -> r q a c", r=4)[r],
+                    in_=scales.bitcast(I32).rearrange("a (q r) c -> r q a c", r=ROWS)[r],
                 )
 
         def lift_rows(a, r):
             nc.sync.dma_start(
                 out=vs[r:P:32, a * S : (a + 1) * S].bitcast(I32),
-                in_=vs_rows[16 * a + r : 16 * (a + 1) : 4, :].bitcast(I32),
+                in_=vs_rows[FIRST_ROW + 16 * a + r : FIRST_ROW + 16 * (a + 1) : ROWS, :].bitcast(I32),
+            )
+
+        def load_tab(a):
+            tabw[a] = held(("tabw0", "window_a")[a], [P, T], U32)
+            nc.sync.dma_start(out=tabw[a][:].bitcast(I32), in_=tab_words[a].rearrange("p t i -> p (t i)").bitcast(I32))
+
+        def load_w2(b):
+            nc.sync.dma_start(
+                out=w2_raw[b][:], in_=w2[:, b * KP : (b + 1) * KP].rearrange("(p j) c -> p j c", j=PACK)
             )
 
         def order_columns(ordered, raw):
@@ -82,57 +91,8 @@ def tile_list_orchard_spray_dosing_kernel(
                 in_=raw[:].rearrange("p (g m t) -> p g t m", t=PACK, m=P),
             )
 
-        def load_w2(b):
-            w2_raw[b] = held("w2_raw", [P, PACK, KP], F32)
-            nc.sync.dma_start(
-                out=w2_raw[b][:], in_=w2[:, b * KP : (b + 1) * KP].rearrange("(p j) c -> p j c", j=PACK)
-            )
-
-        def load_tab(a):
-            tabw[a] = held(("tabs", "tab2s")[a], [P, T], U32)
-            nc.sync.dma_start(out=tabw[a][:].bitcast(I32), in_=tab_words[a].rearrange("p t i -> p (t i)").bitcast(I32))
-
-        def gather_words(a):
-            for u in range(2):
-                nc.vector.tensor_copy(vw[a][u][:], tabw[a][:].indirect(half(list1, u)))
-
-        def half(lst, u):
-            return lst[:, u * (W // 16) : (u + 1) * (W // 16)]
-
-        nc.vector.memset(tab2s[:].bitcast(I32), 0)
-        nc.vector.memset(w1s_raw[:].bitcast(I32), 0)
-        nc.vector.memset(tabs[32:64, :].bitcast(I32), 0)
-        nc.vector.memset(tabs[64:P, :].bitcast(I32), 0)
-        nc.vector.memset(vs[:].bitcast(I32), 0)
-        nc.vector.memset(warm_in[:], 0.0)
-        nc.scalar.activation(warm_out[:], warm_in[:], ACT.Silu)
-
-        nc.sync.dma_start(list1[:], offs)
-        nc.sync.dma_start(out=tabs[0:32, :].bitcast(I32), in_=tab_scales.bitcast(I32).rearrange("a q t -> (a q) t"))
-        nc.sync.dma_start(list2[:], offs2)
-        nc.sync.dma_start(out=tab2w[:].bitcast(I32), in_=tab2_words[0].bitcast(I32))
-        load_scale_rows(tab2s, tab2_scales)
-        load_w2(0)
-        load_scale_rows(w1s_raw, w1_scales)
-        nc.sync.dma_start(
-            out=w1w_raw[:].bitcast(I32).rearrange("p (a c) -> p a c", a=2),
-            in_=w1_words.bitcast(I32).rearrange("a p c -> p a c"),
-        )
-        nc.sync.dma_start(out=noz[:], in_=nozzle.rearrange("(b p t) -> p b t", b=2, t=PACK))
-
-        nc.vector.tensor_copy(vs_rows[:], tabs[:].indirect(list1[:]))
-        rows = [(a, r) for a in range(2) for r in range(4)]
-        for a, r in rows[:2]:
-            lift_rows(a, r)
-        load_tab(0)
-        for a, r in rows[2:]:
-            lift_rows(a, r)
-        nc.vector.tensor_copy(v2w[:], tab2w[:].indirect(list2[:]))
-        nc.vector.tensor_copy(v2s[:], tab2s[:].indirect(list2[:]))
-        load_tab(1)
-
-        def cast_w2(b):
-            nc.scalar.copy(
+        def cast_w2(b, copy):
+            copy(
                 out=w2_bf[b][:].rearrange("p (s e m j) -> p s m j e", s=2, e=2, j=PACK),
                 in_=w2_raw[b][:].rearrange("p j (m s e) -> p s m j e", s=2, e=2),
             )
@@ -140,63 +100,101 @@ def tile_list_orchard_spray_dosing_kernel(
         def quantize_w2(b):
             nc.vector.quantize_mx(out=w2w[b][:].bitcast(FP8X4), scales=w2s[b][:], in_=w2_bf[b][:])
 
+        def gather_words(a, u):
+            nc.vector.tensor_copy(vw[a][u][:], tabw[a][:].indirect(list1[:, u * (W // 16) : (u + 1) * (W // 16)]))
+
         allowed = {}
-        side = [0]
 
-        def make_allowed(b, u):
-            for t in range(PACK):
-                acc = bank(side[0] % 3)
-                side.append(side.pop() + 1)
-                cols = slice(t * P, (t + 1) * P)
-                toks = slice(u * W, (u + 1) * W)
-                nc.tensor.matmul_mx(
-                    out=acc[:], lhsT=w2w[b][:, cols].bitcast(FP8X4), lhsT_scale=w2s[b][:, cols],
-                    rhs=v2w[:, toks].bitcast(FP4X4), rhs_scale=v2s[:, toks], start=True, stop=True,
-                )
-                allowed[b, u, t] = held("allowed%d_%d_%d" % (b, u, t), [P, W], F32)
-                nc.scalar.copy(out=allowed[b, u, t][:], in_=acc[:])
+        def make_allowed(b):
+            for u in range(2):
+                for t in range(PACK):
+                    acc = bank(t)
+                    cols = slice(t * P, (t + 1) * P)
+                    toks = slice(u * W, (u + 1) * W)
+                    nc.tensor.matmul_mx(
+                        out=acc[:], lhsT=w2w[b][:, cols].bitcast(FP8X4), lhsT_scale=w2s[b][:, cols],
+                        rhs=v2w[:, toks].bitcast(FP4X4), rhs_scale=v2s[:, toks], start=True, stop=True,
+                    )
+                    allowed[b, u, t] = held("allowed%d_%d_%d" % (b, u, t), [P, W], F32)
+                    nc.scalar.copy(out=allowed[b, u, t][:], in_=acc[:])
 
-        cast_w2(0)
-        order_columns(w1s, w1s_raw)
-        order_columns(w1w, w1w_raw)
-        quantize_w2(0)
-        make_allowed(0, 0)
-        make_allowed(0, 1)
+        nc.vector.memset(tab2s[:].bitcast(I32), 0)
+        nc.vector.memset(tabs[0:FIRST_ROW, :].bitcast(I32), 0)
+        nc.vector.memset(w1s_raw[:].bitcast(I32), 0)
+        nc.gpsimd.memset(vs[:].bitcast(I32), 0)
+        warm_in = held("warm_in", [P, 1], F32)
+        warm_out = held("warm_out", [P, 1], F32)
+        nc.vector.memset(warm_in[:], 0.0)
+        nc.scalar.activation(warm_out[:], warm_in[:], ACT.Silu)
+
+        nc.sync.dma_start(list1[:], offs)
+        nc.sync.dma_start(
+            out=tabs[FIRST_ROW:P, :].bitcast(I32), in_=tab_scales.bitcast(I32).rearrange("a q t -> (a q) t")
+        )
+        nc.sync.dma_start(list2[:], offs2)
+        nc.sync.dma_start(out=tab2w[:].bitcast(I32), in_=tab2_words[0].bitcast(I32))
+        load_scale_rows(tab2s, tab2_scales)
+        load_w2(0)
+        nc.sync.dma_start(
+            out=w1w_raw[:].bitcast(I32).rearrange("p (a c) -> p a c", a=2),
+            in_=w1_words.bitcast(I32).rearrange("a p c -> p a c"),
+        )
         load_w2(1)
-        gather_words(0)
-        w3_bytes = held("tabs", [P, 2 * N + 2 * N // 4], U32)
+        load_tab(0)
+        nc.sync.dma_start(out=noz[:], in_=nozzle.rearrange("(b p t) -> p b t", b=2, t=PACK))
+        load_scale_rows(w1s_raw, w1_scales)
+
+        nc.vector.tensor_copy(vs_rows[:], tabs[:].indirect(list1[:]))
+        rows = [(a, r) for a in range(2) for r in range(ROWS)]
+        lift_rows(*rows[0])
+        load_tab(1)
+        for a, r in rows[1:]:
+            lift_rows(a, r)
+        nc.vector.tensor_copy(v2w[:], tab2w[:].indirect(list2[:]))
+        nc.vector.tensor_copy(v2s[:], tab2s[:].indirect(list2[:]))
+
+        cast_w2(0, nc.scalar.copy)
+        quantize_w2(0)
+        make_allowed(0)
+        w1w = held("w2_bf0", [P, 2 * H], U16)
+        order_columns(w1w, w1w_raw)
+        cast_w2(1, nc.vector.tensor_copy)
+        quantize_w2(1)
+        make_allowed(1)
+        nc.scalar.activation(neg_noz[:], noz[:], ACT.Copy, scale=-1.0)
+        late_vectors = held("w2_bf1", [P, 4 * PACK], F32)
+        gain = late_vectors[:, 0 : 2 * PACK].rearrange("p (b t) -> p b t", b=2)
+        rest = late_vectors[:, 2 * PACK : 3 * PACK]
+        nc.sync.dma_start(out=gain, in_=flow.rearrange("(b p t) -> p b t", b=2, t=PACK))
+        gather_words(0, 0)
+        gather_words(0, 1)
+        order_columns(w1s, w1s_raw)
+        w3_bytes = held("tabw0", [P, 2 * N + 2 * N // 4], U32)
         w3w = w3_bytes[:, 0 : 2 * N]
+        w3s = w3_bytes[:, 2 * N :].bitcast(U8)
         nc.sync.dma_start(
             out=w3w.bitcast(I32).rearrange("p (a c) -> p a c", a=2),
             in_=w3_words.rearrange("a p c i -> p a (c i)").bitcast(I32),
         )
-        late_vectors = held("w2_bf0", [P, 4 * PACK], F32)
-        gain = late_vectors[:, 0 : 2 * PACK].rearrange("p (b t) -> p b t", b=2)
-        rest = late_vectors[:, 2 * PACK : 3 * PACK]
-        nc.sync.dma_start(out=gain, in_=flow.rearrange("(b p t) -> p b t", b=2, t=PACK))
-        w3s = w3_bytes[:, 2 * N :].bitcast(U8)
         load_scale_rows(w3s, w3_scales)
         with nc.allow_non_contiguous_dma(reason="one idle value a partition"):
             nc.sync.dma_start(out=rest, in_=idle.rearrange("(i p) -> p i", p=P))
-        gather_words(1)
+        gather_words(1, 0)
 
-        units = [(0, 0), (0, 1), (1, 0), (1, 1)]
-        demand = {}
-        act = {}
-        h_bf = {}
-        hw = {}
-        hs = {}
+        units = [(0, 0), (1, 0), (0, 1), (1, 1)]
+        demand, act, rounded, h_bf, hw, hs = {}, {}, {}, {}, {}, {}
         whole = slice(0, W)
-        first, second = slice(0, W // 2), slice(W // 2, W)
+        parts = [slice(lo, hi) for lo, hi in zip(LAST_CUTS, LAST_CUTS[1:])]
 
         def make_demand(k, t):
             b, u = units[k]
-            demand[k, t] = bank(3 + (PACK * k + t) % 5)
+            demand[k, t] = bank((4, 0, 4, 4)[k] + t)
             for a in range(2):
                 cols = slice(a * H + b * KP + t * P, a * H + b * KP + (t + 1) * P)
                 nc.tensor.matmul_mx(
                     out=demand[k, t][:], lhsT=w1w[:, cols].bitcast(FP4X4), lhsT_scale=w1s[:, cols],
-                    rhs=vw[a][u][:].bitcast(FP8X4), rhs_scale=vs[:, a * S + u * W : a * S + (u + 1) * W], start=(a == 0), stop=(a == 1),
+                    rhs=vw[a][u][:].bitcast(FP8X4), rhs_scale=vs[:, a * S + u * W : a * S + (u + 1) * W],
+                    start=(a == 0), stop=(a == 1),
                 )
             if t == 0:
                 act[k] = ring.tile([P, PACK, W], F32, name="act")
@@ -204,21 +202,35 @@ def tile_list_orchard_spray_dosing_kernel(
                 hw[k] = held("hw%d" % k, [P, W], U32)
                 hs[k] = held("hs%d" % k, [P, W], U8)
 
-        def dose(k, t):
+        def dose(k, t, part):
             b, u = units[k]
-            make_demand(k, t)
-            least = ring.tile([P, W], F32, name="least", bufs=8)
-            nc.vector.tensor_tensor(least[:], demand[k, t][:], allowed[b, u, t][:], ALU.min)
-            nc.scalar.activation(act[k][:, t, :], least[:], ACT.Silu, bias=neg_noz[:, b, t : t + 1])
+            if part.start == 0:
+                make_demand(k, t)
+            least = ring.tile([P, part.stop - part.start], F32, name="least", bufs=8)
+            nc.vector.tensor_tensor(least[:], demand[k, t][:, part], allowed[b, u, t][:, part], ALU.min)
+            nc.scalar.activation(act[k][:, t, part], least[:], ACT.Silu, bias=neg_noz[:, b, t : t + 1])
+            if k < 3:
+                if t == 0:
+                    rounded[k] = ring.tile([P, PACK, SCALAR_VISITS[k]], BF16, name="rounded")
+                nc.scalar.activation(
+                    rounded[k][:, t, :], act[k][:, t, W - SCALAR_VISITS[k] :], ACT.Copy, scale=gain[:, b, t : t + 1]
+                )
 
-        def apply_gain(k, part):
+        def apply_gain(engine, k, part):
             b, u = units[k]
             pairs = (part.stop - part.start) // 2
-            nc.vector.tensor_tensor(
+            engine.tensor_tensor(
                 h_bf[k][:, PACK * part.start : PACK * part.stop].rearrange("p (c i t) -> p c t i", i=2, t=PACK),
                 act[k][:, :, part].rearrange("p t (c i) -> p c t i", i=2),
                 gain[:, b, :].unsqueeze(1).unsqueeze(3).to_broadcast([P, pairs, PACK, 2]),
                 ALU.mult,
+            )
+
+        def vector_gain(k):
+            apply_gain(nc.vector, k, slice(0, W - SCALAR_VISITS[k]))
+            nc.vector.tensor_copy(
+                out=h_bf[k][:, PACK * (W - SCALAR_VISITS[k]) :].rearrange("p (c i t) -> p c t i", i=4, t=PACK),
+                in_=rounded[k][:].rearrange("p t (c i) -> p c t i", i=4),
             )
 
         def quantize_h(k, part):
@@ -243,44 +255,39 @@ def tile_list_orchard_spray_dosing_kernel(
                 nc.scalar.activation(res[:], acc[:, part], ACT.Identity, bias=rest[:, i : i + 1])
             nc.sync.dma_start(out=out[i * P : (i + 1) * P, u * W + part.start : u * W + part.stop], in_=res[:])
 
-        nc.scalar.activation(neg_noz[:], noz[:], ACT.Copy, scale=-1.0)
-        cast_w2(1)
-        for k in range(2):
-            for t in range(PACK):
-                dose(k, t)
-        quantize_w2(1)
-        make_allowed(1, 0)
-        make_allowed(1, 1)
-        apply_gain(0, whole)
-        quantize_h(0, whole)
-        apply_gain(1, whole)
-        dose(2, 0)
-        quantize_h(1, whole)
-        for t in range(1, PACK):
-            dose(2, t)
-        for t in range(PACK - 1):
-            dose(3, t)
-        apply_gain(2, whole)
-        dose(3, PACK - 1)
-        quantize_h(2, whole)
-        lead = [bank(j) for j in (0, 1, 2, 4)]
-        early = [bank(j) for j in (5, 6, 7, 3)]
-        for i in range(4):
-            valve_pass(lead[i], i, 0, 0, whole)
-        for i in range(4):
-            valve_pass(early[i], i, 0, 1, first)
-        for i in range(4):
-            valve_pass(lead[i], i, 1, 0, whole)
-            finish(lead[i], i, 0, whole, False)
-        apply_gain(3, first)
-        apply_gain(3, second)
-        quantize_h(3, first)
-        quantize_h(3, second)
-        for i in range(4):
-            valve_pass(early[i], i, 1, 1, first)
-            finish(early[i], i, 1, first, i >= 2)
-        late = [bank(j) for j in (0, 1, 2, 4)]
-        for i in range(4):
-            valve_pass(late[i], i, 0, 1, second)
-            valve_pass(late[i], i, 1, 1, second)
-            finish(late[i], i, 1, second, i % 2 == 1)
+        for t in range(PACK):
+            dose(0, t, whole)
+        for k in range(1, 3):
+            dose(k, 0, whole)
+            if k == 1:
+                gather_words(1, 1)
+            dose(k, 1, whole)
+            dose(k, 2, whole)
+            vector_gain(k - 1)
+            dose(k, 3, whole)
+            quantize_h(k - 1, whole)
+        lead = [bank(i) for i in range(4)]
+        for b in range(2):
+            for i in range(4):
+                valve_pass(lead[i], i, b, 0, whole)
+        for t in range(PACK):
+            dose(3, t, parts[0])
+            finish(lead[t], t, 0, whole, False)
+        vector_gain(2)
+        for j, part in enumerate(parts[1:]):
+            dose(3, 0, part)
+            if j == 0:
+                quantize_h(2, whole)
+            for t in range(1, PACK):
+                dose(3, t, part)
+            apply_gain(nc.vector, 3, parts[j])
+        apply_gain(nc.vector, 3, parts[-1])
+        for part in parts:
+            quantize_h(3, part)
+        for j, part in enumerate(parts):
+            acc = [bank(4 * (j % 2) + i) for i in range(4)]
+            for i in range(4):
+                valve_pass(acc[i], i, 0, 1, part)
+            for i in range(4):
+                valve_pass(acc[i], i, 1, 1, part)
+                finish(acc[i], i, 1, part, i % 2 == 1)

@@ -22,7 +22,9 @@ KP = P * PACK
 W = 512
 ROWS = 4
 FIRST_ROW = 96
-SCALAR_VISITS = (448, 448, 448)
+POOL_VISITS = (320, 320, 256)
+POOL_PIECE = 64
+SCALAR_VISITS = (192, 192, 256)
 LAST_CUTS = (0, 256, 512)
 
 
@@ -33,7 +35,7 @@ def tile_list_orchard_spray_dosing_kernel(
     nc = tc.nc
     with ExitStack() as ctx:
         keep = ctx.enter_context(tc.tile_pool(name="keep", bufs=1))
-        ring = ctx.enter_context(tc.tile_pool(name="ring", bufs=3))
+        ring = ctx.enter_context(tc.tile_pool(name="ring", bufs=4))
         psum = ctx.enter_context(tc.psum_pool(name="psum", bufs=1))
 
         def held(name, shape, dtype):
@@ -226,8 +228,11 @@ def tile_list_orchard_spray_dosing_kernel(
                 ALU.mult,
             )
 
+        def pool_gain(k):
+            for start in range(0, POOL_VISITS[k], POOL_PIECE):
+                apply_gain(nc.gpsimd, k, slice(start, min(start + POOL_PIECE, POOL_VISITS[k])))
+
         def vector_gain(k):
-            apply_gain(nc.vector, k, slice(0, W - SCALAR_VISITS[k]))
             nc.vector.tensor_copy(
                 out=h_bf[k][:, PACK * (W - SCALAR_VISITS[k]) :].rearrange("p (c i t) -> p c t i", i=4, t=PACK),
                 in_=rounded[k][:].rearrange("p t (c i) -> p c t i", i=4),
@@ -255,37 +260,40 @@ def tile_list_orchard_spray_dosing_kernel(
                 nc.scalar.activation(res[:], acc[:, part], ACT.Identity, bias=rest[:, i : i + 1])
             nc.sync.dma_start(out=out[i * P : (i + 1) * P, u * W + part.start : u * W + part.stop], in_=res[:])
 
+        first, second = parts
         for t in range(PACK):
             dose(0, t, whole)
-        for k in range(1, 3):
-            dose(k, 0, whole)
-            if k == 1:
-                gather_words(1, 1)
-            dose(k, 1, whole)
-            dose(k, 2, whole)
-            vector_gain(k - 1)
-            dose(k, 3, whole)
-            quantize_h(k - 1, whole)
+        pool_gain(0)
+        dose(1, 0, whole)
+        gather_words(1, 1)
+        for t in range(1, PACK):
+            dose(1, t, whole)
+        pool_gain(1)
+        vector_gain(0)
+        for t in range(PACK):
+            dose(2, t, whole)
+        pool_gain(2)
+        quantize_h(0, whole)
+        vector_gain(1)
+        for t in range(PACK):
+            dose(3, t, first)
+        quantize_h(1, whole)
         lead = [bank(i) for i in range(4)]
         for b in range(2):
             for i in range(4):
                 valve_pass(lead[i], i, b, 0, whole)
         for t in range(PACK):
-            dose(3, t, parts[0])
-            finish(lead[t], t, 0, whole, False)
+            dose(3, t, second)
+        for i in range(4):
+            finish(lead[i], i, 0, whole, False)
         vector_gain(2)
-        for j, part in enumerate(parts[1:]):
-            dose(3, 0, part)
-            if j == 0:
-                quantize_h(2, whole)
-            for t in range(1, PACK):
-                dose(3, t, part)
-            apply_gain(nc.vector, 3, parts[j])
-        apply_gain(nc.vector, 3, parts[-1])
+        apply_gain(nc.vector, 3, first)
+        quantize_h(2, whole)
+        apply_gain(nc.vector, 3, second)
         for part in parts:
             quantize_h(3, part)
         for j, part in enumerate(parts):
-            acc = [bank(4 * (j % 2) + i) for i in range(4)]
+            acc = [bank(4 * (1 - j) + i) for i in range(4)]
             for i in range(4):
                 valve_pass(acc[i], i, 0, 1, part)
             for i in range(4):

@@ -22,9 +22,8 @@ KP = P * PACK
 W = 512
 ROWS = 4
 FIRST_ROW = 96
-POOL_VISITS = (320, 320, 256)
-POOL_PIECE = 64
-SCALAR_VISITS = (192, 192, 256)
+POOL_EXTRA = 0
+POOL_PIECE = 128
 LAST_CUTS = (0, 256, 512)
 
 
@@ -52,7 +51,7 @@ def tile_list_orchard_spray_dosing_kernel(
         w1w_raw = held("w1w_raw", [P, 2 * H], U16)
         w1s_raw = held("w1s_raw", [P, 2 * H], U8)
         w1s = held("w1s", [P, 2 * H], U8)
-        w2_raw = [held("w2_raw%d" % b, [P, PACK, KP], F32) for b in range(2)]
+        w2_raw = held("w2_raw", [P, PACK, H], F32)
         w2_bf = [held("w2_bf%d" % b, [P, PACK * KP], BF16) for b in range(2)]
         w2w = [held("w2w%d" % b, [P, KP], U32) for b in range(2)]
         w2s = [held("w2s%d" % b, [P, KP], U8) for b in range(2)]
@@ -82,11 +81,6 @@ def tile_list_orchard_spray_dosing_kernel(
             tabw[a] = held(("tabw0", "window_a")[a], [P, T], U32)
             nc.sync.dma_start(out=tabw[a][:].bitcast(I32), in_=tab_words[a].rearrange("p t i -> p (t i)").bitcast(I32))
 
-        def load_w2(b):
-            nc.sync.dma_start(
-                out=w2_raw[b][:], in_=w2[:, b * KP : (b + 1) * KP].rearrange("(p j) c -> p j c", j=PACK)
-            )
-
         def order_columns(ordered, raw):
             nc.vector.tensor_copy(
                 out=ordered[:].rearrange("p (g t m) -> p g t m", t=PACK, m=P),
@@ -96,7 +90,7 @@ def tile_list_orchard_spray_dosing_kernel(
         def cast_w2(b, copy):
             copy(
                 out=w2_bf[b][:].rearrange("p (s e m j) -> p s m j e", s=2, e=2, j=PACK),
-                in_=w2_raw[b][:].rearrange("p j (m s e) -> p s m j e", s=2, e=2),
+                in_=w2_raw[:, :, b * KP : (b + 1) * KP].rearrange("p j (m s e) -> p s m j e", s=2, e=2),
             )
 
         def quantize_w2(b):
@@ -136,12 +130,11 @@ def tile_list_orchard_spray_dosing_kernel(
         nc.sync.dma_start(list2[:], offs2)
         nc.sync.dma_start(out=tab2w[:].bitcast(I32), in_=tab2_words[0].bitcast(I32))
         load_scale_rows(tab2s, tab2_scales)
-        load_w2(0)
+        nc.sync.dma_start(out=w2_raw[:].rearrange("p j c -> p (j c)"), in_=w2.rearrange("(p j) c -> p (j c)", j=PACK))
         nc.sync.dma_start(
             out=w1w_raw[:].bitcast(I32).rearrange("p (a c) -> p a c", a=2),
             in_=w1_words.bitcast(I32).rearrange("a p c -> p a c"),
         )
-        load_w2(1)
         load_tab(0)
         nc.sync.dma_start(out=noz[:], in_=nozzle.rearrange("(b p t) -> p b t", b=2, t=PACK))
         load_scale_rows(w1s_raw, w1_scales)
@@ -190,7 +183,7 @@ def tile_list_orchard_spray_dosing_kernel(
 
         def make_demand(k, t):
             b, u = units[k]
-            demand[k, t] = bank((4, 0, 4, 4)[k] + t)
+            demand[k, t] = bank((4, 0, 4, 0)[k] + t)
             for a in range(2):
                 cols = slice(a * H + b * KP + t * P, a * H + b * KP + (t + 1) * P)
                 nc.tensor.matmul_mx(
@@ -211,12 +204,6 @@ def tile_list_orchard_spray_dosing_kernel(
             least = ring.tile([P, part.stop - part.start], F32, name="least", bufs=8)
             nc.vector.tensor_tensor(least[:], demand[k, t][:, part], allowed[b, u, t][:, part], ALU.min)
             nc.scalar.activation(act[k][:, t, part], least[:], ACT.Silu, bias=neg_noz[:, b, t : t + 1])
-            if k < 3:
-                if t == 0:
-                    rounded[k] = ring.tile([P, PACK, SCALAR_VISITS[k]], BF16, name="rounded")
-                nc.scalar.activation(
-                    rounded[k][:, t, :], act[k][:, t, W - SCALAR_VISITS[k] :], ACT.Copy, scale=gain[:, b, t : t + 1]
-                )
 
         def apply_gain(engine, k, part):
             b, u = units[k]
@@ -228,13 +215,19 @@ def tile_list_orchard_spray_dosing_kernel(
                 ALU.mult,
             )
 
-        def pool_gain(k):
-            for start in range(0, POOL_VISITS[k], POOL_PIECE):
-                apply_gain(nc.gpsimd, k, slice(start, min(start + POOL_PIECE, POOL_VISITS[k])))
+        def pool_gain(k, part):
+            for start in range(part.start, part.stop, POOL_PIECE):
+                apply_gain(nc.gpsimd, k, slice(start, min(start + POOL_PIECE, part.stop)))
 
-        def vector_gain(k):
+        def scalar_gain(k, part):
+            b, u = units[k]
+            rounded[k] = ring.tile([P, PACK, part.stop - part.start], BF16, name="rounded")
+            for t in range(PACK):
+                nc.scalar.activation(rounded[k][:, t, :], act[k][:, t, part], ACT.Copy, scale=gain[:, b, t : t + 1])
+
+        def interleave(k, part):
             nc.vector.tensor_copy(
-                out=h_bf[k][:, PACK * (W - SCALAR_VISITS[k]) :].rearrange("p (c i t) -> p c t i", i=4, t=PACK),
+                out=h_bf[k][:, PACK * part.start : PACK * part.stop].rearrange("p (c i t) -> p c t i", i=4, t=PACK),
                 in_=rounded[k][:].rearrange("p t (c i) -> p c t i", i=4),
             )
 
@@ -260,42 +253,42 @@ def tile_list_orchard_spray_dosing_kernel(
                 nc.scalar.activation(res[:], acc[:, part], ACT.Identity, bias=rest[:, i : i + 1])
             nc.sync.dma_start(out=out[i * P : (i + 1) * P, u * W + part.start : u * W + part.stop], in_=res[:])
 
-        first, second = parts
-        for t in range(PACK):
-            dose(0, t, whole)
-        pool_gain(0)
-        dose(1, 0, whole)
-        gather_words(1, 1)
-        for t in range(1, PACK):
-            dose(1, t, whole)
-        pool_gain(1)
-        vector_gain(0)
-        for t in range(PACK):
-            dose(2, t, whole)
-        pool_gain(2)
-        quantize_h(0, whole)
-        vector_gain(1)
-        for t in range(PACK):
-            dose(3, t, first)
-        quantize_h(1, whole)
-        lead = [bank(i) for i in range(4)]
-        for b in range(2):
+        def lead_half():
+            lead = [bank(4 + i) for i in range(4)]
+            for b in range(2):
+                for i in range(4):
+                    valve_pass(lead[i], i, b, 0, whole)
             for i in range(4):
-                valve_pass(lead[i], i, b, 0, whole)
-        for t in range(PACK):
-            dose(3, t, second)
-        for i in range(4):
-            finish(lead[i], i, 0, whole, False)
-        vector_gain(2)
-        apply_gain(nc.vector, 3, first)
-        quantize_h(2, whole)
-        apply_gain(nc.vector, 3, second)
-        for part in parts:
-            quantize_h(3, part)
-        for j, part in enumerate(parts):
-            acc = [bank(4 * (1 - j) + i) for i in range(4)]
+                finish(lead[i], i, 0, whole, False)
+
+        def last_part(j, part, on_vector):
+            acc = [bank(4 * j + i) for i in range(4)]
             for i in range(4):
                 valve_pass(acc[i], i, 0, 1, part)
             for i in range(4):
                 valve_pass(acc[i], i, 1, 1, part)
-                finish(acc[i], i, 1, part, i % 2 == 1)
+                finish(acc[i], i, 1, part, on_vector[i])
+
+        first, second = parts
+        for k in range(4):
+            for t in range(PACK):
+                dose(k, t, whole)
+                if (k, t) == (1, 0):
+                    gather_words(1, 1)
+            if k == 0:
+                pool_gain(0, whole)
+            if k == 1:
+                pool_gain(1, slice(0, POOL_EXTRA))
+        apply_gain(nc.vector, 1, slice(POOL_EXTRA, W))
+        scalar_gain(2, whole)
+        quantize_h(0, whole)
+        quantize_h(1, whole)
+        lead_half()
+        interleave(2, whole)
+        apply_gain(nc.vector, 3, first)
+        quantize_h(2, whole)
+        quantize_h(3, first)
+        apply_gain(nc.vector, 3, second)
+        last_part(0, first, (False, False, False, False))
+        quantize_h(3, second)
+        last_part(1, second, (False, True, False, True))

@@ -35,18 +35,22 @@ def tile_list_orchard_spray_dosing_kernel(
     with ExitStack() as ctx:
         keep = ctx.enter_context(tc.tile_pool(name="keep", bufs=1))
         ring = ctx.enter_context(tc.tile_pool(name="ring", bufs=4))
+        reuse = ctx.enter_context(tc.tile_pool(name="reuse", bufs=1))
         psum = ctx.enter_context(tc.psum_pool(name="psum", bufs=1))
 
         def held(name, shape, dtype):
             return keep.tile(shape, dtype, name=name, align_bytes=64)
+
+        def placed(name, shape, dtype, offset):
+            return reuse.tile(shape, dtype, name=name, align_bytes=64, offset=offset)
 
         def bank(i):
             return psum.tile([P, W], F32, name="bank%d" % i)
 
         list1 = keep.tile([P, S // 16], U16, name="list1")
         list2 = keep.tile([P, S // 16], U16, name="list2")
-        tabs = held("window_a", [P, T], U8)
-        tab2s = held("tab2s", [P, T], U8)
+        tabs = placed("tabs", [P, T], U8, 0)
+        tab2s = placed("tab2s", [P, T], U8, T)
         tab2w = held("tab2w", [P, T], U16)
         w1w_raw = held("w1w_raw", [P, 2 * H], U16)
         w1s_raw = held("w1s_raw", [P, 2 * H], U8)
@@ -59,9 +63,7 @@ def tile_list_orchard_spray_dosing_kernel(
         neg_noz = held("neg_noz", [P, 2, PACK], F32)
         vw = [[held("vw%d_%d" % (a, u), [P, W], U32) for u in range(2)] for a in range(2)]
         vs_rows = held("vs_rows", [P, S], U8)
-        vs = held("vs", [P, 2 * S], U8)
-        v2w = held("v2w", [P, S], U16)
-        v2s = held("v2s", [P, S], U8)
+        v2s_rows = held("v2s_rows", [P, S], U8)
         tabw = {}
 
         def load_scale_rows(tile, scales):
@@ -78,7 +80,6 @@ def tile_list_orchard_spray_dosing_kernel(
             )
 
         def load_tab(a):
-            tabw[a] = held(("tabw0", "window_a")[a], [P, T], U32)
             nc.sync.dma_start(out=tabw[a][:].bitcast(I32), in_=tab_words[a].rearrange("p t i -> p (t i)").bitcast(I32))
 
         def order_columns(ordered, raw):
@@ -116,8 +117,7 @@ def tile_list_orchard_spray_dosing_kernel(
 
         nc.vector.memset(tab2s[:].bitcast(I32), 0)
         nc.vector.memset(tabs[0:FIRST_ROW, :].bitcast(I32), 0)
-        nc.vector.memset(w1s_raw[:].bitcast(I32), 0)
-        nc.gpsimd.memset(vs[:].bitcast(I32), 0)
+        nc.gpsimd.memset(w1s_raw[:].bitcast(I32), 0)
         warm_in = held("warm_in", [P, 1], F32)
         warm_out = held("warm_out", [P, 1], F32)
         nc.vector.memset(warm_in[:], 0.0)
@@ -129,32 +129,40 @@ def tile_list_orchard_spray_dosing_kernel(
         )
         nc.sync.dma_start(list2[:], offs2)
         nc.sync.dma_start(out=tab2w[:].bitcast(I32), in_=tab2_words[0].bitcast(I32))
-        load_scale_rows(tab2s, tab2_scales)
+        nc.sync.dma_start(out=tab2s[0:P:8, :].bitcast(I32), in_=tab2_scales[0].bitcast(I32))
         nc.sync.dma_start(out=w2_raw[:].rearrange("p j c -> p (j c)"), in_=w2.rearrange("(p j) c -> p (j c)", j=PACK))
+        nc.sync.dma_start(out=noz[:], in_=nozzle.rearrange("(b p t) -> p b t", b=2, t=PACK))
+        load_scale_rows(w1s_raw, w1_scales)
         nc.sync.dma_start(
             out=w1w_raw[:].bitcast(I32).rearrange("p (a c) -> p a c", a=2),
             in_=w1_words.bitcast(I32).rearrange("a p c -> p a c"),
         )
-        load_tab(0)
-        nc.sync.dma_start(out=noz[:], in_=nozzle.rearrange("(b p t) -> p b t", b=2, t=PACK))
-        load_scale_rows(w1s_raw, w1_scales)
 
         nc.vector.tensor_copy(vs_rows[:], tabs[:].indirect(list1[:]))
+        nc.vector.tensor_copy(v2s_rows[:], tab2s[:].indirect(list2[:]))
+        v2w = placed("v2w", [P, S], U16, T + 64)
+        nc.vector.tensor_copy(v2w[:], tab2w[:].indirect(list2[:]))
+        v2s = placed("v2s", [P, S], U8, 0)
+        vs = placed("vs", [P, 2 * S], U8, T + 64 - 2 * S)
+        tabw[0] = placed("tabw0", [P, T], U32, T + 64 + 2 * S)
+        tabw[1] = held("tab2w", [P, T], U32)
+        for r in range(ROWS):
+            nc.sync.dma_start(out=v2s[r:P:32, :].bitcast(I32), in_=v2s_rows[8 * r : P : 32, :].bitcast(I32))
+        load_tab(0)
         rows = [(a, r) for a in range(2) for r in range(ROWS)]
-        lift_rows(*rows[0])
+        for a, r in rows[:1]:
+            lift_rows(a, r)
         load_tab(1)
         for a, r in rows[1:]:
             lift_rows(a, r)
-        nc.vector.tensor_copy(v2w[:], tab2w[:].indirect(list2[:]))
-        nc.vector.tensor_copy(v2s[:], tab2s[:].indirect(list2[:]))
 
-        cast_w2(0, nc.scalar.copy)
+        cast_w2(0, nc.vector.tensor_copy)
+        cast_w2(1, nc.scalar.copy)
         quantize_w2(0)
         make_allowed(0)
+        quantize_w2(1)
         w1w = held("w2_bf0", [P, 2 * H], U16)
         order_columns(w1w, w1w_raw)
-        cast_w2(1, nc.vector.tensor_copy)
-        quantize_w2(1)
         make_allowed(1)
         nc.scalar.activation(neg_noz[:], noz[:], ACT.Copy, scale=-1.0)
         late_vectors = held("w2_bf1", [P, 4 * PACK], F32)
@@ -164,7 +172,7 @@ def tile_list_orchard_spray_dosing_kernel(
         gather_words(0, 0)
         gather_words(0, 1)
         order_columns(w1s, w1s_raw)
-        w3_bytes = held("tabw0", [P, 2 * N + 2 * N // 4], U32)
+        w3_bytes = placed("w3_bytes", [P, 2 * N + 2 * N // 4], U32, T + 64 + 2 * S)
         w3w = w3_bytes[:, 0 : 2 * N]
         w3s = w3_bytes[:, 2 * N :].bitcast(U8)
         nc.sync.dma_start(
@@ -221,14 +229,14 @@ def tile_list_orchard_spray_dosing_kernel(
 
         def scalar_gain(k, part):
             b, u = units[k]
-            rounded[k] = ring.tile([P, PACK, part.stop - part.start], BF16, name="rounded")
+            rounded[k, part.start] = held("rounded%d_%d" % (k, part.start), [P, PACK, part.stop - part.start], BF16)
             for t in range(PACK):
-                nc.scalar.activation(rounded[k][:, t, :], act[k][:, t, part], ACT.Copy, scale=gain[:, b, t : t + 1])
+                nc.scalar.activation(rounded[k, part.start][:, t, :], act[k][:, t, part], ACT.Copy, scale=gain[:, b, t : t + 1])
 
         def interleave(k, part):
             nc.vector.tensor_copy(
                 out=h_bf[k][:, PACK * part.start : PACK * part.stop].rearrange("p (c i t) -> p c t i", i=4, t=PACK),
-                in_=rounded[k][:].rearrange("p t (c i) -> p c t i", i=4),
+                in_=rounded[k, part.start][:].rearrange("p t (c i) -> p c t i", i=4),
             )
 
         def quantize_h(k, part):
@@ -237,39 +245,30 @@ def tile_list_orchard_spray_dosing_kernel(
                 in_=h_bf[k][:, PACK * part.start : PACK * part.stop],
             )
 
-        def valve_pass(acc, i, b, u, part):
-            k = units.index((b, u))
-            cols = slice(b * N + i * P, b * N + (i + 1) * P)
-            nc.tensor.matmul_mx(
-                out=acc[:, part], lhsT=w3w[:, cols].bitcast(FP8X4), lhsT_scale=w3s[:, cols],
-                rhs=hw[k][:, part].bitcast(FP8X4), rhs_scale=hs[k][:, part], start=(b == 0), stop=(b == 1),
-            )
-
-        def finish(acc, i, u, part, on_vector):
-            res = held("res%d_%d_%d" % (i, u, part.start), [P, part.stop - part.start], F32)
-            if on_vector:
-                nc.vector.tensor_scalar(res[:], acc[:, part], rest[:, i : i + 1], None, ALU.add)
-            else:
-                nc.scalar.activation(res[:], acc[:, part], ACT.Identity, bias=rest[:, i : i + 1])
-            nc.sync.dma_start(out=out[i * P : (i + 1) * P, u * W + part.start : u * W + part.stop], in_=res[:])
-
-        def lead_half():
-            lead = [bank(4 + i) for i in range(4)]
-            for b in range(2):
+        def valves(first_bank, u, part, blocks, vector_pair):
+            acc = [bank(first_bank + i) for i in range(4)]
+            for b in blocks:
+                k = units.index((b, u))
                 for i in range(4):
-                    valve_pass(lead[i], i, b, 0, whole)
-            for i in range(4):
-                finish(lead[i], i, 0, whole, False)
+                    cols = slice(b * N + i * P, b * N + (i + 1) * P)
+                    nc.tensor.matmul_mx(
+                        out=acc[i][:, part], lhsT=w3w[:, cols].bitcast(FP8X4), lhsT_scale=w3s[:, cols],
+                        rhs=hw[k][:, part].bitcast(FP8X4), rhs_scale=hs[k][:, part],
+                        start=(b == blocks[0]), stop=(b == blocks[1]),
+                    )
+            for pair in range(2):
+                res = held("res%d_%d_%d" % (pair, u, part.start), [P, 2, part.stop - part.start], F32)
+                for j in range(2):
+                    i = 2 * j + pair
+                    if pair == vector_pair:
+                        nc.vector.tensor_scalar(res[:, j, :], acc[i][:, part], rest[:, i : i + 1], None, ALU.add)
+                    else:
+                        nc.scalar.activation(res[:, j, :], acc[i][:, part], ACT.Identity, bias=rest[:, i : i + 1])
+                rows = out[:, u * W + part.start : u * W + part.stop].rearrange("(j e p) n -> e p j n", j=2, e=2)
+                nc.sync.dma_start(out=rows[pair], in_=res[:])
 
-        def last_part(j, part, on_vector):
-            acc = [bank(4 * j + i) for i in range(4)]
-            for i in range(4):
-                valve_pass(acc[i], i, 0, 1, part)
-            for i in range(4):
-                valve_pass(acc[i], i, 1, 1, part)
-                finish(acc[i], i, 1, part, on_vector[i])
-
-        first, second = parts
+        low, high = slice(0, W // 2), slice(W // 2, W)
+        third, fourth = slice(W // 2, 3 * W // 4), slice(3 * W // 4, W)
         for k in range(4):
             for t in range(PACK):
                 dose(k, t, whole)
@@ -279,16 +278,23 @@ def tile_list_orchard_spray_dosing_kernel(
                 pool_gain(0, whole)
             if k == 1:
                 pool_gain(1, slice(0, POOL_EXTRA))
-        apply_gain(nc.vector, 1, slice(POOL_EXTRA, W))
-        scalar_gain(2, whole)
+        apply_gain(nc.vector, 1, low)
         quantize_h(0, whole)
-        quantize_h(1, whole)
-        lead_half()
-        interleave(2, whole)
-        apply_gain(nc.vector, 3, first)
-        quantize_h(2, whole)
-        quantize_h(3, first)
-        apply_gain(nc.vector, 3, second)
-        last_part(0, first, (False, False, False, False))
-        quantize_h(3, second)
-        last_part(1, second, (False, True, False, True))
+        quantize_h(1, low)
+        scalar_gain(2, low)
+        scalar_gain(2, high)
+        valves(4, 0, low, (0, 1), None)
+        apply_gain(nc.vector, 1, high)
+        interleave(2, low)
+        quantize_h(1, high)
+        scalar_gain(3, high)
+        valves(0, 0, high, (0, 1), None)
+        apply_gain(nc.vector, 3, low)
+        quantize_h(2, low)
+        quantize_h(3, low)
+        valves(4, 1, low, (0, 1), None)
+        interleave(2, high)
+        interleave(3, high)
+        quantize_h(2, high)
+        quantize_h(3, high)
+        valves(0, 1, high, (0, 1), 1)

@@ -22,7 +22,7 @@ KP = P * PACK
 W = 512
 ROWS = 4
 FIRST_ROW = 96
-POOL_EXTRA = 0
+POOL_VISITS = 384
 POOL_PIECE = 128
 LAST_CUTS = (0, 256, 512)
 
@@ -54,7 +54,6 @@ def tile_list_orchard_spray_dosing_kernel(
         tab2w = held("tab2w", [P, T], U16)
         w1w_raw = held("w1w_raw", [P, 2 * H], U16)
         w1s_raw = held("w1s_raw", [P, 2 * H], U8)
-        w1s = held("w1s", [P, 2 * H], U8)
         w2_raw = held("w2_raw", [P, PACK, H], F32)
         w2_bf = [held("w2_bf%d" % b, [P, PACK * KP], BF16) for b in range(2)]
         w2w = [held("w2w%d" % b, [P, KP], U32) for b in range(2)]
@@ -118,10 +117,6 @@ def tile_list_orchard_spray_dosing_kernel(
         nc.vector.memset(tab2s[:].bitcast(I32), 0)
         nc.vector.memset(tabs[0:FIRST_ROW, :].bitcast(I32), 0)
         nc.gpsimd.memset(w1s_raw[:].bitcast(I32), 0)
-        warm_in = held("warm_in", [P, 1], F32)
-        warm_out = held("warm_out", [P, 1], F32)
-        nc.vector.memset(warm_in[:], 0.0)
-        nc.scalar.activation(warm_out[:], warm_in[:], ACT.Silu)
 
         nc.sync.dma_start(list1[:], offs)
         nc.sync.dma_start(
@@ -165,13 +160,14 @@ def tile_list_orchard_spray_dosing_kernel(
         order_columns(w1w, w1w_raw)
         make_allowed(1)
         nc.scalar.activation(neg_noz[:], noz[:], ACT.Copy, scale=-1.0)
-        late_vectors = held("w2_bf1", [P, 4 * PACK], F32)
+        w1s = held("w2_bf1", [P, 2 * H], U8)
+        order_columns(w1s, w1s_raw)
+        late_vectors = held("w1s_raw", [P, 4 * PACK], F32)
         gain = late_vectors[:, 0 : 2 * PACK].rearrange("p (b t) -> p b t", b=2)
         rest = late_vectors[:, 2 * PACK : 3 * PACK]
         nc.sync.dma_start(out=gain, in_=flow.rearrange("(b p t) -> p b t", b=2, t=PACK))
         gather_words(0, 0)
         gather_words(0, 1)
-        order_columns(w1s, w1s_raw)
         w3_bytes = placed("w3_bytes", [P, 2 * N + 2 * N // 4], U32, T + 64 + 2 * S)
         w3w = w3_bytes[:, 0 : 2 * N]
         w3s = w3_bytes[:, 2 * N :].bitcast(U8)
@@ -256,16 +252,13 @@ def tile_list_orchard_spray_dosing_kernel(
                         rhs=hw[k][:, part].bitcast(FP8X4), rhs_scale=hs[k][:, part],
                         start=(b == blocks[0]), stop=(b == blocks[1]),
                     )
-            for pair in range(2):
-                res = held("res%d_%d_%d" % (pair, u, part.start), [P, 2, part.stop - part.start], F32)
-                for j in range(2):
-                    i = 2 * j + pair
-                    if pair == vector_pair:
-                        nc.vector.tensor_scalar(res[:, j, :], acc[i][:, part], rest[:, i : i + 1], None, ALU.add)
-                    else:
-                        nc.scalar.activation(res[:, j, :], acc[i][:, part], ACT.Identity, bias=rest[:, i : i + 1])
-                rows = out[:, u * W + part.start : u * W + part.stop].rearrange("(j e p) n -> e p j n", j=2, e=2)
-                nc.sync.dma_start(out=rows[pair], in_=res[:])
+            for i in range(4):
+                res = held("res%d_%d_%d" % (i, u, part.start), [P, part.stop - part.start], F32)
+                if i % 2 == vector_pair:
+                    nc.vector.tensor_scalar(res[:], acc[i][:, part], rest[:, i : i + 1], None, ALU.add)
+                else:
+                    nc.scalar.activation(res[:], acc[i][:, part], ACT.Identity, bias=rest[:, i : i + 1])
+                nc.sync.dma_start(out=out[i * P : (i + 1) * P, u * W + part.start : u * W + part.stop], in_=res[:])
 
         low, high = slice(0, W // 2), slice(W // 2, W)
         third, fourth = slice(W // 2, 3 * W // 4), slice(3 * W // 4, W)
@@ -275,9 +268,8 @@ def tile_list_orchard_spray_dosing_kernel(
                 if (k, t) == (1, 0):
                     gather_words(1, 1)
             if k == 0:
-                pool_gain(0, whole)
-            if k == 1:
-                pool_gain(1, slice(0, POOL_EXTRA))
+                pool_gain(0, slice(0, POOL_VISITS))
+        apply_gain(nc.vector, 0, slice(POOL_VISITS, W))
         apply_gain(nc.vector, 1, low)
         quantize_h(0, whole)
         quantize_h(1, low)

@@ -58,7 +58,6 @@ def tile_list_orchard_spray_dosing_kernel(
         w2_bf = [held("w2_bf%d" % b, [P, PACK * KP], BF16) for b in range(2)]
         w2w = [held("w2w%d" % b, [P, KP], U32) for b in range(2)]
         w2s = [held("w2s%d" % b, [P, KP], U8) for b in range(2)]
-        noz = held("noz", [P, 2, PACK], F32)
         neg_noz = held("neg_noz", [P, 2, PACK], F32)
         vw = [[held("vw%d_%d" % (a, u), [P, W], U32) for u in range(2)] for a in range(2)]
         vs_rows = held("vs_rows", [P, S], U8)
@@ -126,7 +125,6 @@ def tile_list_orchard_spray_dosing_kernel(
         nc.sync.dma_start(out=tab2w[:].bitcast(I32), in_=tab2_words[0].bitcast(I32))
         nc.sync.dma_start(out=tab2s[0:P:8, :].bitcast(I32), in_=tab2_scales[0].bitcast(I32))
         nc.sync.dma_start(out=w2_raw[:].rearrange("p j c -> p (j c)"), in_=w2.rearrange("(p j) c -> p (j c)", j=PACK))
-        nc.sync.dma_start(out=noz[:], in_=nozzle.rearrange("(b p t) -> p b t", b=2, t=PACK))
         load_scale_rows(w1s_raw, w1_scales)
         nc.sync.dma_start(
             out=w1w_raw[:].bitcast(I32).rearrange("p (a c) -> p a c", a=2),
@@ -159,12 +157,13 @@ def tile_list_orchard_spray_dosing_kernel(
         w1w = held("w2_bf0", [P, 2 * H], U16)
         order_columns(w1w, w1w_raw)
         make_allowed(1)
-        nc.scalar.activation(neg_noz[:], noz[:], ACT.Copy, scale=-1.0)
         w1s = held("w2_bf1", [P, 2 * H], U8)
         order_columns(w1s, w1s_raw)
-        late_vectors = held("w1s_raw", [P, 4 * PACK], F32)
+        late_vectors = held("w1s_raw", [P, 6 * PACK], F32)
         gain = late_vectors[:, 0 : 2 * PACK].rearrange("p (b t) -> p b t", b=2)
         rest = late_vectors[:, 2 * PACK : 3 * PACK]
+        noz = late_vectors[:, 4 * PACK : 6 * PACK].rearrange("p (b t) -> p b t", b=2)
+        nc.sync.dma_start(out=noz, in_=nozzle.rearrange("(b p t) -> p b t", b=2, t=PACK))
         nc.sync.dma_start(out=gain, in_=flow.rearrange("(b p t) -> p b t", b=2, t=PACK))
         gather_words(0, 0)
         gather_words(0, 1)
@@ -179,6 +178,7 @@ def tile_list_orchard_spray_dosing_kernel(
         with nc.allow_non_contiguous_dma(reason="one idle value a partition"):
             nc.sync.dma_start(out=rest, in_=idle.rearrange("(i p) -> p i", p=P))
         gather_words(1, 0)
+        nc.vector.tensor_scalar(neg_noz[:], noz, -1.0, None, ALU.mult)
 
         units = [(0, 0), (1, 0), (0, 1), (1, 1)]
         demand, act, rounded, h_bf, hw, hs = {}, {}, {}, {}, {}, {}

@@ -21,7 +21,8 @@ PACK = 4
 KP = P * PACK
 W = 512
 ROWS = 4
-FIRST_ROW = 96
+TAB_ROWS = (80, 112)
+TAB2_ROW = 48
 POOL_VISITS = 384
 POOL_PIECE = 128
 LAST_CUTS = (0, 256, 512)
@@ -74,7 +75,7 @@ def tile_list_orchard_spray_dosing_kernel(
         def lift_rows(a, r):
             nc.sync.dma_start(
                 out=vs[r:P:32, a * S : (a + 1) * S].bitcast(I32),
-                in_=vs_rows[FIRST_ROW + 16 * a + r : FIRST_ROW + 16 * (a + 1) : ROWS, :].bitcast(I32),
+                in_=vs_rows[TAB_ROWS[a] + r : TAB_ROWS[a] + 16 : ROWS, :].bitcast(I32),
             )
 
         def load_tab(a):
@@ -113,17 +114,18 @@ def tile_list_orchard_spray_dosing_kernel(
                     allowed[b, u, t] = held("allowed%d_%d_%d" % (b, u, t), [P, W], F32)
                     nc.scalar.copy(out=allowed[b, u, t][:], in_=acc[:])
 
-        nc.vector.memset(tab2s[:].bitcast(I32), 0)
-        nc.vector.memset(tabs[0:FIRST_ROW, :].bitcast(I32), 0)
+        for lo, hi in ((0, TAB_ROWS[0]), (96, TAB_ROWS[1])):
+            nc.vector.memset(tabs[lo:hi, :].bitcast(I32), 0)
         nc.gpsimd.memset(w1s_raw[:].bitcast(I32), 0)
+        for lo, hi in ((0, TAB2_ROW), (64, P)):
+            nc.gpsimd.memset(tab2s[lo:hi, :].bitcast(I32), 0)
 
         nc.sync.dma_start(list1[:], offs)
-        nc.sync.dma_start(
-            out=tabs[FIRST_ROW:P, :].bitcast(I32), in_=tab_scales.bitcast(I32).rearrange("a q t -> (a q) t")
-        )
+        for a in range(2):
+            nc.sync.dma_start(out=tabs[TAB_ROWS[a] : TAB_ROWS[a] + 16, :].bitcast(I32), in_=tab_scales[a].bitcast(I32))
         nc.sync.dma_start(list2[:], offs2)
         nc.sync.dma_start(out=tab2w[:].bitcast(I32), in_=tab2_words[0].bitcast(I32))
-        nc.sync.dma_start(out=tab2s[0:P:8, :].bitcast(I32), in_=tab2_scales[0].bitcast(I32))
+        nc.sync.dma_start(out=tab2s[TAB2_ROW : TAB2_ROW + 16, :].bitcast(I32), in_=tab2_scales[0].bitcast(I32))
         nc.sync.dma_start(out=w2_raw[:].rearrange("p j c -> p (j c)"), in_=w2.rearrange("(p j) c -> p (j c)", j=PACK))
         load_scale_rows(w1s_raw, w1_scales)
         nc.sync.dma_start(
@@ -140,7 +142,7 @@ def tile_list_orchard_spray_dosing_kernel(
         tabw[0] = placed("tabw0", [P, T], U32, T + 64 + 2 * S)
         tabw[1] = held("tab2w", [P, T], U32)
         for r in range(ROWS):
-            nc.sync.dma_start(out=v2s[r:P:32, :].bitcast(I32), in_=v2s_rows[8 * r : P : 32, :].bitcast(I32))
+            nc.sync.dma_start(out=v2s[r:P:32, :].bitcast(I32), in_=v2s_rows[TAB2_ROW + r : TAB2_ROW + 16 : ROWS, :].bitcast(I32))
         load_tab(0)
         rows = [(a, r) for a in range(2) for r in range(ROWS)]
         for a, r in rows[:1]:

@@ -21,8 +21,8 @@ PACK = 4
 KP = P * PACK
 W = 512
 ROWS = 4
-TAB_ROWS = (80, 112)
-TAB2_ROW = 48
+TAB_ROWS = (48, 112)
+TAB2_ROW = 4
 POOL_VISITS = 384
 POOL_PIECE = 128
 LAST_CUTS = (0, 256, 512)
@@ -114,18 +114,17 @@ def tile_list_orchard_spray_dosing_kernel(
                     allowed[b, u, t] = held("allowed%d_%d_%d" % (b, u, t), [P, W], F32)
                     nc.scalar.copy(out=allowed[b, u, t][:], in_=acc[:])
 
-        for lo, hi in ((0, TAB_ROWS[0]), (96, TAB_ROWS[1])):
+        for lo, hi in ((0, TAB_ROWS[0]), (64, TAB_ROWS[1])):
             nc.vector.memset(tabs[lo:hi, :].bitcast(I32), 0)
+        nc.gpsimd.memset(tab2s[:].bitcast(I32), 0)
         nc.gpsimd.memset(w1s_raw[:].bitcast(I32), 0)
-        for lo, hi in ((0, TAB2_ROW), (64, P)):
-            nc.gpsimd.memset(tab2s[lo:hi, :].bitcast(I32), 0)
 
         nc.sync.dma_start(list1[:], offs)
         for a in range(2):
             nc.sync.dma_start(out=tabs[TAB_ROWS[a] : TAB_ROWS[a] + 16, :].bitcast(I32), in_=tab_scales[a].bitcast(I32))
         nc.sync.dma_start(list2[:], offs2)
         nc.sync.dma_start(out=tab2w[:].bitcast(I32), in_=tab2_words[0].bitcast(I32))
-        nc.sync.dma_start(out=tab2s[TAB2_ROW : TAB2_ROW + 16, :].bitcast(I32), in_=tab2_scales[0].bitcast(I32))
+        nc.sync.dma_start(out=tab2s[TAB2_ROW:P:8, :].bitcast(I32), in_=tab2_scales[0].bitcast(I32))
         nc.sync.dma_start(out=w2_raw[:].rearrange("p j c -> p (j c)"), in_=w2.rearrange("(p j) c -> p (j c)", j=PACK))
         load_scale_rows(w1s_raw, w1_scales)
         nc.sync.dma_start(
@@ -142,7 +141,7 @@ def tile_list_orchard_spray_dosing_kernel(
         tabw[0] = placed("tabw0", [P, T], U32, T + 64 + 2 * S)
         tabw[1] = held("tab2w", [P, T], U32)
         for r in range(ROWS):
-            nc.sync.dma_start(out=v2s[r:P:32, :].bitcast(I32), in_=v2s_rows[TAB2_ROW + r : TAB2_ROW + 16 : ROWS, :].bitcast(I32))
+            nc.sync.dma_start(out=v2s[r:P:32, :].bitcast(I32), in_=v2s_rows[TAB2_ROW + 8 * r : P : 32, :].bitcast(I32))
         load_tab(0)
         rows = [(a, r) for a in range(2) for r in range(ROWS)]
         for a, r in rows[:1]:
@@ -271,15 +270,16 @@ def tile_list_orchard_spray_dosing_kernel(
                     gather_words(1, 1)
             if k == 0:
                 pool_gain(0, slice(0, POOL_VISITS))
-        apply_gain(nc.vector, 0, slice(POOL_VISITS, W))
         apply_gain(nc.vector, 1, low)
-        quantize_h(0, whole)
+        quantize_h(0, low)
         quantize_h(1, low)
         scalar_gain(2, low)
-        scalar_gain(2, high)
         valves(4, 0, low, (0, 1), None)
+        scalar_gain(2, high)
+        apply_gain(nc.vector, 0, slice(POOL_VISITS, W))
         apply_gain(nc.vector, 1, high)
         interleave(2, low)
+        quantize_h(0, high)
         quantize_h(1, high)
         scalar_gain(3, high)
         valves(0, 0, high, (0, 1), None)

@@ -52,9 +52,9 @@ def tile_list_orchard_spray_dosing_kernel(
         list2 = keep.tile([P, S // 16], U16, name="list2")
         tabs = placed("tabs", [P, T], U8, 0)
         tab2s = placed("tab2s", [P, T], U8, T)
-        tab2w = held("tab2w", [P, T], U16)
+        tab2w = placed("tab2w", [P, T], U16, 6 * T)
         w1w_raw = held("w1w_raw", [P, 2 * H], U16)
-        w1s_raw = held("w1s_raw", [P, 2 * H], U8)
+        w1s_raw = placed("w1s_raw", [P, H], U8, 8 * T)
         w2_raw = held("w2_raw", [P, PACK, H], F32)
         w2_bf = [held("w2_bf%d" % b, [P, PACK * KP], BF16) for b in range(2)]
         w2w = [held("w2w%d" % b, [P, KP], U32) for b in range(2)]
@@ -74,8 +74,8 @@ def tile_list_orchard_spray_dosing_kernel(
 
         def lift_rows(a, r):
             nc.sync.dma_start(
-                out=vs[r:P:32, a * S : (a + 1) * S].bitcast(I32),
-                in_=vs_rows[TAB_ROWS[a] + r : TAB_ROWS[a] + 16 : ROWS, :].bitcast(I32),
+                out=planes[a][r:P:32, :].bitcast(I32),
+                in_=joined[TAB_ROWS[a] + r : TAB_ROWS[a] + 16 : ROWS, :].bitcast(I32),
             )
 
         def load_tab(a):
@@ -83,7 +83,7 @@ def tile_list_orchard_spray_dosing_kernel(
 
         def order_columns(ordered, raw):
             nc.vector.tensor_copy(
-                out=ordered[:].rearrange("p (g t m) -> p g t m", t=PACK, m=P),
+                out=ordered.rearrange("p (g t m) -> p g t m", t=PACK, m=P),
                 in_=raw[:].rearrange("p (g m t) -> p g t m", t=PACK, m=P),
             )
 
@@ -117,7 +117,8 @@ def tile_list_orchard_spray_dosing_kernel(
         for lo, hi in ((0, TAB_ROWS[0]), (64, TAB_ROWS[1])):
             nc.vector.memset(tabs[lo:hi, :].bitcast(I32), 0)
         nc.gpsimd.memset(tab2s[:].bitcast(I32), 0)
-        nc.gpsimd.memset(w1s_raw[:].bitcast(I32), 0)
+        for lo, hi in ((0, TAB_ROWS[0]), (64, TAB_ROWS[1])):
+            nc.gpsimd.memset(w1s_raw[lo:hi, :].bitcast(I32), 0)
 
         nc.sync.dma_start(list1[:], offs)
         for a in range(2):
@@ -126,7 +127,8 @@ def tile_list_orchard_spray_dosing_kernel(
         nc.sync.dma_start(out=tab2w[:].bitcast(I32), in_=tab2_words[0].bitcast(I32))
         nc.sync.dma_start(out=tab2s[TAB2_ROW:P:8, :].bitcast(I32), in_=tab2_scales[0].bitcast(I32))
         nc.sync.dma_start(out=w2_raw[:].rearrange("p j c -> p (j c)"), in_=w2.rearrange("(p j) c -> p (j c)", j=PACK))
-        load_scale_rows(w1s_raw, w1_scales)
+        for a in range(2):
+            nc.sync.dma_start(out=w1s_raw[TAB_ROWS[a] : TAB_ROWS[a] + 16, :].bitcast(I32), in_=w1_scales[a].bitcast(I32))
         nc.sync.dma_start(
             out=w1w_raw[:].bitcast(I32).rearrange("p (a c) -> p a c", a=2),
             in_=w1_words.bitcast(I32).rearrange("a p c -> p a c"),
@@ -134,12 +136,18 @@ def tile_list_orchard_spray_dosing_kernel(
 
         nc.vector.tensor_copy(vs_rows[:], tabs[:].indirect(list1[:]))
         nc.vector.tensor_copy(v2s_rows[:], tab2s[:].indirect(list2[:]))
-        v2w = placed("v2w", [P, S], U16, T + 64)
+        v2w = placed("v2w", [P, S], U16, T + S)
         nc.vector.tensor_copy(v2w[:], tab2w[:].indirect(list2[:]))
+        cast_w2(0, nc.vector.tensor_copy)
+        cast_w2(1, nc.scalar.copy)
+        quantize_w2(0)
+        joined = held("w2_bf0", [P, S + H], U8)
+        nc.vector.tensor_copy(out=joined[:, 0:S].bitcast(I32), in_=vs_rows[:].bitcast(I32))
+        order_columns(joined[:, S:], w1s_raw)
         v2s = placed("v2s", [P, S], U8, 0)
-        vs = placed("vs", [P, 2 * S], U8, T + 64 - 2 * S)
-        tabw[0] = placed("tabw0", [P, T], U32, T + 64 + 2 * S)
-        tabw[1] = held("tab2w", [P, T], U32)
+        planes = [placed("plane%d" % a, [P, S + H], U8, S + a * (S + H)) for a in range(2)]
+        tabw[0] = placed("tabw0", [P, T], U32, T + 3 * S)
+        tabw[1] = placed("tabw1", [P, T], U32, 6 * T)
         for r in range(ROWS):
             nc.sync.dma_start(out=v2s[r:P:32, :].bitcast(I32), in_=v2s_rows[TAB2_ROW + 8 * r : P : 32, :].bitcast(I32))
         load_tab(0)
@@ -150,17 +158,12 @@ def tile_list_orchard_spray_dosing_kernel(
         for a, r in rows[1:]:
             lift_rows(a, r)
 
-        cast_w2(0, nc.vector.tensor_copy)
-        cast_w2(1, nc.scalar.copy)
-        quantize_w2(0)
         make_allowed(0)
         quantize_w2(1)
-        w1w = held("w2_bf0", [P, 2 * H], U16)
-        order_columns(w1w, w1w_raw)
+        w1w = held("w2_bf1", [P, 2 * H], U16)
+        order_columns(w1w[:], w1w_raw)
         make_allowed(1)
-        w1s = held("w2_bf1", [P, 2 * H], U8)
-        order_columns(w1s, w1s_raw)
-        late_vectors = held("w1s_raw", [P, 6 * PACK], F32)
+        late_vectors = held("w1w_raw", [P, 6 * PACK], F32)
         gain = late_vectors[:, 0 : 2 * PACK].rearrange("p (b t) -> p b t", b=2)
         rest = late_vectors[:, 2 * PACK : 3 * PACK]
         noz = late_vectors[:, 4 * PACK : 6 * PACK].rearrange("p (b t) -> p b t", b=2)
@@ -168,7 +171,7 @@ def tile_list_orchard_spray_dosing_kernel(
         nc.sync.dma_start(out=gain, in_=flow.rearrange("(b p t) -> p b t", b=2, t=PACK))
         gather_words(0, 0)
         gather_words(0, 1)
-        w3_bytes = placed("w3_bytes", [P, 2 * N + 2 * N // 4], U32, T + 64 + 2 * S)
+        w3_bytes = placed("w3_bytes", [P, 2 * N + 2 * N // 4], U32, T + 3 * S)
         w3w = w3_bytes[:, 0 : 2 * N]
         w3s = w3_bytes[:, 2 * N :].bitcast(U8)
         nc.sync.dma_start(
@@ -192,8 +195,8 @@ def tile_list_orchard_spray_dosing_kernel(
             for a in range(2):
                 cols = slice(a * H + b * KP + t * P, a * H + b * KP + (t + 1) * P)
                 nc.tensor.matmul_mx(
-                    out=demand[k, t][:], lhsT=w1w[:, cols].bitcast(FP4X4), lhsT_scale=w1s[:, cols],
-                    rhs=vw[a][u][:].bitcast(FP8X4), rhs_scale=vs[:, a * S + u * W : a * S + (u + 1) * W],
+                    out=demand[k, t][:], lhsT=w1w[:, cols].bitcast(FP4X4), lhsT_scale=planes[a][:, S + b * KP + t * P : S + b * KP + (t + 1) * P],
+                    rhs=vw[a][u][:].bitcast(FP8X4), rhs_scale=planes[a][:, u * W : (u + 1) * W],
                     start=(a == 0), stop=(a == 1),
                 )
             if t == 0:

@@ -72,6 +72,9 @@ def tile_list_orchard_spray_dosing_kernel(
                     in_=scales.bitcast(I32).rearrange("a (q r) c -> r q a c", r=ROWS)[r],
                 )
 
+        def load_wide(tile, scales, a):
+            nc.sync.dma_start(out=tile[TAB_ROWS[a] : TAB_ROWS[a] + 16, :].bitcast(I32), in_=scales[a].bitcast(I32))
+
         def lift_rows(a, r):
             nc.sync.dma_start(
                 out=planes[a][r:P:32, :].bitcast(I32),
@@ -122,13 +125,13 @@ def tile_list_orchard_spray_dosing_kernel(
 
         nc.sync.dma_start(list1[:], offs)
         for a in range(2):
-            nc.sync.dma_start(out=tabs[TAB_ROWS[a] : TAB_ROWS[a] + 16, :].bitcast(I32), in_=tab_scales[a].bitcast(I32))
+            load_wide(tabs, tab_scales, a)
         nc.sync.dma_start(list2[:], offs2)
         nc.sync.dma_start(out=tab2w[:].bitcast(I32), in_=tab2_words[0].bitcast(I32))
         nc.sync.dma_start(out=tab2s[TAB2_ROW:P:8, :].bitcast(I32), in_=tab2_scales[0].bitcast(I32))
+        load_wide(w1s_raw, w1_scales, 0)
         nc.sync.dma_start(out=w2_raw[:].rearrange("p j c -> p (j c)"), in_=w2.rearrange("(p j) c -> p (j c)", j=PACK))
-        for a in range(2):
-            nc.sync.dma_start(out=w1s_raw[TAB_ROWS[a] : TAB_ROWS[a] + 16, :].bitcast(I32), in_=w1_scales[a].bitcast(I32))
+        load_wide(w1s_raw, w1_scales, 1)
         nc.sync.dma_start(
             out=w1w_raw[:].bitcast(I32).rearrange("p (a c) -> p a c", a=2),
             in_=w1_words.bitcast(I32).rearrange("a p c -> p a c"),
@@ -151,12 +154,10 @@ def tile_list_orchard_spray_dosing_kernel(
         for r in range(ROWS):
             nc.sync.dma_start(out=v2s[r:P:32, :].bitcast(I32), in_=v2s_rows[TAB2_ROW + 8 * r : P : 32, :].bitcast(I32))
         load_tab(0)
-        rows = [(a, r) for a in range(2) for r in range(ROWS)]
-        for a, r in rows[:1]:
-            lift_rows(a, r)
         load_tab(1)
-        for a, r in rows[1:]:
-            lift_rows(a, r)
+        for a in range(2):
+            for r in range(ROWS):
+                lift_rows(a, r)
 
         make_allowed(0)
         quantize_w2(1)

@@ -1,6 +1,7 @@
 from contextlib import ExitStack
 
 import concourse.mybir as mybir
+from concourse.masks import make_identity
 
 K, K2, H, N, T, S = 1024, 512, 1024, 512, 4096, 1024
 FLOPS = 2 * S * (K * H + K2 * H + H * N)
@@ -20,12 +21,13 @@ P = 128
 PACK = 4
 KP = P * PACK
 W = 512
+KIB = 1024
 ROWS = 4
 TAB_ROWS = (48, 112)
 TAB2_ROW = 4
-POOL_VISITS = 384
-POOL_PIECE = 128
-LAST_CUTS = (0, 256, 512)
+POOL_PIECE = 256
+FLOW_ROW = 126
+FLOW_BANK = 7
 
 
 def tile_list_orchard_spray_dosing_kernel(
@@ -51,10 +53,10 @@ def tile_list_orchard_spray_dosing_kernel(
         list1 = keep.tile([P, S // 16], U16, name="list1")
         list2 = keep.tile([P, S // 16], U16, name="list2")
         tabs = placed("tabs", [P, T], U8, 0)
-        tab2s = placed("tab2s", [P, T], U8, T)
-        tab2w = placed("tab2w", [P, T], U16, 6 * T)
+        tab2s = placed("tab2s", [P, T], U8, 11 * KIB // 2)
+        tab2w = placed("tab2w", [P, T], U16, 26 * KIB)
         w1w_raw = held("w1w_raw", [P, 2 * H], U16)
-        w1s_raw = placed("w1s_raw", [P, H], U8, 8 * T)
+        w1s_raw = placed("w1s_raw", [P, H], U8, 34 * KIB)
         w2_raw = held("w2_raw", [P, PACK, H], F32)
         w2_bf = [held("w2_bf%d" % b, [P, PACK * KP], BF16) for b in range(2)]
         w2w = [held("w2w%d" % b, [P, KP], U32) for b in range(2)]
@@ -63,6 +65,8 @@ def tile_list_orchard_spray_dosing_kernel(
         vw = [[held("vw%d_%d" % (a, u), [P, W], U32) for u in range(2)] for a in range(2)]
         vs_rows = held("vs_rows", [P, S], U8)
         v2s_rows = held("v2s_rows", [P, S], U8)
+        ident = held("ident", [P, P], F32)
+        gain = held("gain", [P, 2, PACK], F32)
         tabw = {}
 
         def load_scale_rows(tile, scales):
@@ -122,6 +126,7 @@ def tile_list_orchard_spray_dosing_kernel(
         nc.gpsimd.memset(tab2s[:].bitcast(I32), 0)
         for lo, hi in ((0, TAB_ROWS[0]), (64, TAB_ROWS[1])):
             nc.gpsimd.memset(w1s_raw[lo:hi, :].bitcast(I32), 0)
+        make_identity(nc, ident[:])
 
         nc.sync.dma_start(list1[:], offs)
         for a in range(2):
@@ -139,7 +144,7 @@ def tile_list_orchard_spray_dosing_kernel(
 
         nc.vector.tensor_copy(vs_rows[:], tabs[:].indirect(list1[:]))
         nc.vector.tensor_copy(v2s_rows[:], tab2s[:].indirect(list2[:]))
-        v2w = placed("v2w", [P, S], U16, T + S)
+        v2w = placed("v2w", [P, S], U16, 7 * KIB)
         nc.vector.tensor_copy(v2w[:], tab2w[:].indirect(list2[:]))
         cast_w2(0, nc.vector.tensor_copy)
         cast_w2(1, nc.scalar.copy)
@@ -147,32 +152,38 @@ def tile_list_orchard_spray_dosing_kernel(
         joined = held("w2_bf0", [P, S + H], U8)
         nc.vector.tensor_copy(out=joined[:, 0:S].bitcast(I32), in_=vs_rows[:].bitcast(I32))
         order_columns(joined[:, S:], w1s_raw)
-        v2s = placed("v2s", [P, S], U8, 0)
-        planes = [placed("plane%d" % a, [P, S + H], U8, S + a * (S + H)) for a in range(2)]
-        tabw[0] = placed("tabw0", [P, T], U32, T + 3 * S)
-        tabw[1] = placed("tabw1", [P, T], U32, 6 * T)
+        v2s = placed("v2s", [P, S], U8, 6 * KIB)
+        planes = [placed("plane%d" % a, [P, S + H], U8, a * (S + H)) for a in range(2)]
+        tabw[0] = placed("tabw0", [P, T], U32, 9 * KIB)
+        tabw[1] = placed("tabw1", [P, T], U32, 26 * KIB)
+        flow_rows = placed("flow_rows", [P, KP], F32, 4 * KIB)
         for r in range(ROWS):
             nc.sync.dma_start(out=v2s[r:P:32, :].bitcast(I32), in_=v2s_rows[TAB2_ROW + 8 * r : P : 32, :].bitcast(I32))
         load_tab(0)
+        nc.sync.dma_start(out=flow_rows[FLOW_ROW:P, :], in_=flow.rearrange("(b c) -> b c", b=2))
+        nc.gpsimd.memset(flow_rows[0:FLOW_ROW, :], 0.0)
         load_tab(1)
         for a in range(2):
             for r in range(ROWS):
                 lift_rows(a, r)
 
         make_allowed(0)
+        flow_bank = bank(FLOW_BANK)
+        for t in range(PACK):
+            nc.tensor.transpose(flow_bank[:, t * P : (t + 1) * P], flow_rows[:, t:KP:PACK], ident[:])
+        turned = flow_bank[:].rearrange("p (t j) -> p j t", t=PACK)[:, FLOW_ROW:P, :]
+        nc.scalar.copy(out=gain[:], in_=turned)
         quantize_w2(1)
         w1w = held("w2_bf1", [P, 2 * H], U16)
         order_columns(w1w[:], w1w_raw)
         make_allowed(1)
         late_vectors = held("w1w_raw", [P, 6 * PACK], F32)
-        gain = late_vectors[:, 0 : 2 * PACK].rearrange("p (b t) -> p b t", b=2)
         rest = late_vectors[:, 2 * PACK : 3 * PACK]
         noz = late_vectors[:, 4 * PACK : 6 * PACK].rearrange("p (b t) -> p b t", b=2)
         nc.sync.dma_start(out=noz, in_=nozzle.rearrange("(b p t) -> p b t", b=2, t=PACK))
-        nc.sync.dma_start(out=gain, in_=flow.rearrange("(b p t) -> p b t", b=2, t=PACK))
         gather_words(0, 0)
         gather_words(0, 1)
-        w3_bytes = placed("w3_bytes", [P, 2 * N + 2 * N // 4], U32, T + 3 * S)
+        w3_bytes = placed("w3_bytes", [P, 2 * N + 2 * N // 4], U32, 9 * KIB)
         w3w = w3_bytes[:, 0 : 2 * N]
         w3s = w3_bytes[:, 2 * N :].bitcast(U8)
         nc.sync.dma_start(
@@ -188,11 +199,10 @@ def tile_list_orchard_spray_dosing_kernel(
         units = [(0, 0), (1, 0), (0, 1), (1, 1)]
         demand, act, rounded, h_bf, hw, hs = {}, {}, {}, {}, {}, {}
         whole = slice(0, W)
-        parts = [slice(lo, hi) for lo, hi in zip(LAST_CUTS, LAST_CUTS[1:])]
 
         def make_demand(k, t):
             b, u = units[k]
-            demand[k, t] = bank((4, 0, 4, 0)[k] + t)
+            demand[k, t] = bank((4 + PACK * k + t) % FLOW_BANK)
             for a in range(2):
                 cols = slice(a * H + b * KP + t * P, a * H + b * KP + (t + 1) * P)
                 nc.tensor.matmul_mx(
@@ -214,19 +224,19 @@ def tile_list_orchard_spray_dosing_kernel(
             nc.vector.tensor_tensor(least[:], demand[k, t][:, part], allowed[b, u, t][:, part], ALU.min)
             nc.scalar.activation(act[k][:, t, part], least[:], ACT.Silu, bias=neg_noz[:, b, t : t + 1])
 
-        def apply_gain(engine, k, part):
+        def apply_gain(engine, factors, k, part):
             b, u = units[k]
             pairs = (part.stop - part.start) // 2
             engine.tensor_tensor(
                 h_bf[k][:, PACK * part.start : PACK * part.stop].rearrange("p (c i t) -> p c t i", i=2, t=PACK),
                 act[k][:, :, part].rearrange("p t (c i) -> p c t i", i=2),
-                gain[:, b, :].unsqueeze(1).unsqueeze(3).to_broadcast([P, pairs, PACK, 2]),
+                factors[:, b, :].unsqueeze(1).unsqueeze(3).to_broadcast([P, pairs, PACK, 2]),
                 ALU.mult,
             )
 
         def pool_gain(k, part):
             for start in range(part.start, part.stop, POOL_PIECE):
-                apply_gain(nc.gpsimd, k, slice(start, min(start + POOL_PIECE, part.stop)))
+                apply_gain(nc.gpsimd, gain, k, slice(start, min(start + POOL_PIECE, part.stop)))
 
         def scalar_gain(k, part):
             b, u = units[k]
@@ -247,7 +257,7 @@ def tile_list_orchard_spray_dosing_kernel(
             )
 
         def valves(first_bank, u, part, blocks, vector_pair):
-            acc = [bank(first_bank + i) for i in range(4)]
+            acc = [bank((first_bank + i) % FLOW_BANK) for i in range(4)]
             for b in blocks:
                 k = units.index((b, u))
                 for i in range(4):
@@ -266,33 +276,30 @@ def tile_list_orchard_spray_dosing_kernel(
                 nc.sync.dma_start(out=out[i * P : (i + 1) * P, u * W + part.start : u * W + part.stop], in_=res[:])
 
         low, high = slice(0, W // 2), slice(W // 2, W)
-        third, fourth = slice(W // 2, 3 * W // 4), slice(3 * W // 4, W)
         for k in range(4):
             for t in range(PACK):
                 dose(k, t, whole)
                 if (k, t) == (1, 0):
                     gather_words(1, 1)
             if k == 0:
-                pool_gain(0, slice(0, POOL_VISITS))
-        apply_gain(nc.vector, 1, low)
+                pool_gain(0, whole)
+        apply_gain(nc.vector, turned, 1, whole)
+        scalar_gain(2, low)
+        scalar_gain(2, high)
+        scalar_gain(3, high)
         quantize_h(0, low)
         quantize_h(1, low)
-        scalar_gain(2, low)
-        valves(4, 0, low, (0, 1), None)
-        scalar_gain(2, high)
-        apply_gain(nc.vector, 0, slice(POOL_VISITS, W))
-        apply_gain(nc.vector, 1, high)
-        interleave(2, low)
+        valves(0, 0, low, (0, 1), None)
         quantize_h(0, high)
         quantize_h(1, high)
-        scalar_gain(3, high)
-        valves(0, 0, high, (0, 1), None)
-        apply_gain(nc.vector, 3, low)
-        quantize_h(2, low)
+        valves(4, 0, high, (0, 1), None)
+        apply_gain(nc.vector, turned, 3, low)
+        interleave(2, low)
         quantize_h(3, low)
-        valves(4, 1, low, (0, 1), None)
+        quantize_h(2, low)
+        valves(8, 1, low, (0, 1), None)
         interleave(2, high)
         interleave(3, high)
         quantize_h(2, high)
         quantize_h(3, high)
-        valves(0, 1, high, (0, 1), 1)
+        valves(12, 1, high, (0, 1), 1)

@@ -28,6 +28,7 @@ TAB2_ROW = 4
 POOL_PIECE = 256
 FLOW_ROW = 126
 FLOW_BANK = 7
+EARLY_SUMS = 3
 
 
 def tile_list_orchard_spray_dosing_kernel(
@@ -203,12 +204,13 @@ def tile_list_orchard_spray_dosing_kernel(
         def make_demand(k, t):
             b, u = units[k]
             demand[k, t] = bank((4 + PACK * k + t) % FLOW_BANK)
-            for a in range(2):
+            passes = (0, 1) if PACK * k + t < EARLY_SUMS else (1, 0)
+            for a in passes:
                 cols = slice(a * H + b * KP + t * P, a * H + b * KP + (t + 1) * P)
                 nc.tensor.matmul_mx(
                     out=demand[k, t][:], lhsT=w1w[:, cols].bitcast(FP4X4), lhsT_scale=planes[a][:, S + b * KP + t * P : S + b * KP + (t + 1) * P],
                     rhs=vw[a][u][:].bitcast(FP8X4), rhs_scale=planes[a][:, u * W : (u + 1) * W],
-                    start=(a == 0), stop=(a == 1),
+                    start=(a == passes[0]), stop=(a == passes[1]),
                 )
             if t == 0:
                 act[k] = ring.tile([P, PACK, W], F32, name="act")

@@ -25,7 +25,6 @@ KIB = 1024
 ROWS = 4
 TAB_ROWS = (48, 112)
 TAB2_ROW = 4
-POOL_PIECE = 256
 FLOW_ROW = 126
 FLOW_BANK = 7
 EARLY_SUMS = 3
@@ -57,14 +56,13 @@ def tile_list_orchard_spray_dosing_kernel(
         tab2s = placed("tab2s", [P, T], U8, 11 * KIB // 2)
         tab2w = placed("tab2w", [P, T], U16, 26 * KIB)
         w1w_raw = held("w1w_raw", [P, 2 * H], U16)
-        w1s_raw = placed("w1s_raw", [P, H], U8, 34 * KIB)
+        w1s_raw = held("w1s_raw", [P, H], U8)
         w2_raw = held("w2_raw", [P, PACK, H], F32)
         w2_bf = [held("w2_bf%d" % b, [P, PACK * KP], BF16) for b in range(2)]
         w2w = [held("w2w%d" % b, [P, KP], U32) for b in range(2)]
         w2s = [held("w2s%d" % b, [P, KP], U8) for b in range(2)]
-        neg_noz = held("neg_noz", [P, 2, PACK], F32)
         vw = [[held("vw%d_%d" % (a, u), [P, W], U32) for u in range(2)] for a in range(2)]
-        vs_rows = held("vs_rows", [P, S], U8)
+        vs_rows = placed("vs_rows", [P, S], U8, 34 * KIB)
         v2s_rows = held("v2s_rows", [P, S], U8)
         ident = held("ident", [P, P], F32)
         gain = held("gain", [P, 2, PACK], F32)
@@ -129,6 +127,10 @@ def tile_list_orchard_spray_dosing_kernel(
             nc.gpsimd.memset(w1s_raw[lo:hi, :].bitcast(I32), 0)
         make_identity(nc, ident[:])
 
+        warm = held("warm", [P, 2], F32)
+        nc.vector.memset(warm[:, 0:1], 0.0)
+        nc.scalar.activation(warm[:, 1:2], warm[:, 0:1], ACT.Silu)
+
         nc.sync.dma_start(list1[:], offs)
         for a in range(2):
             load_wide(tabs, tab_scales, a)
@@ -151,22 +153,26 @@ def tile_list_orchard_spray_dosing_kernel(
         cast_w2(1, nc.scalar.copy)
         quantize_w2(0)
         joined = held("w2_bf0", [P, S + H], U8)
-        nc.vector.tensor_copy(out=joined[:, 0:S].bitcast(I32), in_=vs_rows[:].bitcast(I32))
         order_columns(joined[:, S:], w1s_raw)
+        for half in (slice(0, P // 2), slice(P // 2, P)):
+            nc.vector.tensor_copy(out=joined[half, 0:S].bitcast(I32), in_=vs_rows[half, :].bitcast(I32))
         v2s = placed("v2s", [P, S], U8, 6 * KIB)
         planes = [placed("plane%d" % a, [P, S + H], U8, a * (S + H)) for a in range(2)]
-        tabw[0] = placed("tabw0", [P, T], U32, 9 * KIB)
+        tabw[0] = placed("tabw0", [P, T], U32, 9 * KIB + 64)
+        noz = placed("noz", [P, 2, PACK], F32, 9 * KIB)
         tabw[1] = placed("tabw1", [P, T], U32, 26 * KIB)
         flow_rows = placed("flow_rows", [P, KP], F32, 4 * KIB)
         for r in range(ROWS):
             nc.sync.dma_start(out=v2s[r:P:32, :].bitcast(I32), in_=v2s_rows[TAB2_ROW + 8 * r : P : 32, :].bitcast(I32))
         load_tab(0)
         nc.sync.dma_start(out=flow_rows[FLOW_ROW:P, :], in_=flow.rearrange("(b c) -> b c", b=2))
+        nc.sync.dma_start(out=noz[:], in_=nozzle.rearrange("(b p t) -> p b t", b=2, t=PACK))
         nc.gpsimd.memset(flow_rows[0:FLOW_ROW, :], 0.0)
+        lifts = [(a, r) for a in range(2) for r in range(ROWS)]
+        lift_rows(*lifts[0])
         load_tab(1)
-        for a in range(2):
-            for r in range(ROWS):
-                lift_rows(a, r)
+        for a, r in lifts[1:]:
+            lift_rows(a, r)
 
         make_allowed(0)
         flow_bank = bank(FLOW_BANK)
@@ -178,13 +184,11 @@ def tile_list_orchard_spray_dosing_kernel(
         w1w = held("w2_bf1", [P, 2 * H], U16)
         order_columns(w1w[:], w1w_raw)
         make_allowed(1)
-        late_vectors = held("w1w_raw", [P, 6 * PACK], F32)
-        rest = late_vectors[:, 2 * PACK : 3 * PACK]
-        noz = late_vectors[:, 4 * PACK : 6 * PACK].rearrange("p (b t) -> p b t", b=2)
-        nc.sync.dma_start(out=noz, in_=nozzle.rearrange("(b p t) -> p b t", b=2, t=PACK))
         gather_words(0, 0)
         gather_words(0, 1)
-        w3_bytes = placed("w3_bytes", [P, 2 * N + 2 * N // 4], U32, 9 * KIB)
+        neg_noz = placed("neg_noz", [P, 2, PACK], F32, 15 * KIB)
+        nc.vector.tensor_scalar(neg_noz[:], noz[:], -1.0, None, ALU.mult)
+        w3_bytes = placed("w3_bytes", [P, 2 * N + 2 * N // 4], U32, 10 * KIB)
         w3w = w3_bytes[:, 0 : 2 * N]
         w3s = w3_bytes[:, 2 * N :].bitcast(U8)
         nc.sync.dma_start(
@@ -192,10 +196,10 @@ def tile_list_orchard_spray_dosing_kernel(
             in_=w3_words.rearrange("a p c i -> p a (c i)").bitcast(I32),
         )
         load_scale_rows(w3s, w3_scales)
+        rest = placed("rest", [P, PACK], F32, 15 * KIB + 64)
         with nc.allow_non_contiguous_dma(reason="one idle value a partition"):
-            nc.sync.dma_start(out=rest, in_=idle.rearrange("(i p) -> p i", p=P))
+            nc.sync.dma_start(out=rest[:], in_=idle.rearrange("(i p) -> p i", p=P))
         gather_words(1, 0)
-        nc.vector.tensor_scalar(neg_noz[:], noz, -1.0, None, ALU.mult)
 
         units = [(0, 0), (1, 0), (0, 1), (1, 1)]
         demand, act, rounded, h_bf, hw, hs = {}, {}, {}, {}, {}, {}
@@ -214,7 +218,6 @@ def tile_list_orchard_spray_dosing_kernel(
                 )
             if t == 0:
                 act[k] = ring.tile([P, PACK, W], F32, name="act")
-                h_bf[k] = ring.tile([P, PACK * W], BF16, name="h_bf", align_bytes=64)
                 hw[k] = held("hw%d" % k, [P, W], U32)
                 hs[k] = held("hs%d" % k, [P, W], U8)
 
@@ -226,19 +229,22 @@ def tile_list_orchard_spray_dosing_kernel(
             nc.vector.tensor_tensor(least[:], demand[k, t][:, part], allowed[b, u, t][:, part], ALU.min)
             nc.scalar.activation(act[k][:, t, part], least[:], ACT.Silu, bias=neg_noz[:, b, t : t + 1])
 
+        def rounded_h(k, part):
+            first = part.start // (W // 2) * (W // 2)
+            return h_bf[k, first][:, PACK * (part.start - first) : PACK * (part.stop - first)]
+
+        def half_tile(k, part):
+            h_bf[k, part.start] = held("h_bf%d_%d" % (k, part.start), [P, PACK * W // 2], BF16)
+
         def apply_gain(engine, factors, k, part):
             b, u = units[k]
             pairs = (part.stop - part.start) // 2
             engine.tensor_tensor(
-                h_bf[k][:, PACK * part.start : PACK * part.stop].rearrange("p (c i t) -> p c t i", i=2, t=PACK),
+                rounded_h(k, part).rearrange("p (c i t) -> p c t i", i=2, t=PACK),
                 act[k][:, :, part].rearrange("p t (c i) -> p c t i", i=2),
                 factors[:, b, :].unsqueeze(1).unsqueeze(3).to_broadcast([P, pairs, PACK, 2]),
                 ALU.mult,
             )
-
-        def pool_gain(k, part):
-            for start in range(part.start, part.stop, POOL_PIECE):
-                apply_gain(nc.gpsimd, gain, k, slice(start, min(start + POOL_PIECE, part.stop)))
 
         def scalar_gain(k, part):
             b, u = units[k]
@@ -248,14 +254,14 @@ def tile_list_orchard_spray_dosing_kernel(
 
         def interleave(k, part):
             nc.vector.tensor_copy(
-                out=h_bf[k][:, PACK * part.start : PACK * part.stop].rearrange("p (c i t) -> p c t i", i=4, t=PACK),
+                out=rounded_h(k, part).rearrange("p (c i t) -> p c t i", i=4, t=PACK),
                 in_=rounded[k, part.start][:].rearrange("p t (c i) -> p c t i", i=4),
             )
 
         def quantize_h(k, part):
             nc.vector.quantize_mx(
                 out=hw[k][:, part].bitcast(FP8X4), scales=hs[k][:, part],
-                in_=h_bf[k][:, PACK * part.start : PACK * part.stop],
+                in_=rounded_h(k, part),
             )
 
         def valves(first_bank, u, part, blocks, vector_pair):
@@ -284,22 +290,32 @@ def tile_list_orchard_spray_dosing_kernel(
                 if (k, t) == (1, 0):
                     gather_words(1, 1)
             if k == 0:
-                pool_gain(0, whole)
-        apply_gain(nc.vector, turned, 1, whole)
+                for part in (low, high):
+                    half_tile(0, part)
+                apply_gain(nc.gpsimd, gain, 0, low)
+                apply_gain(nc.gpsimd, gain, 0, high)
+        half_tile(1, low)
+        apply_gain(nc.vector, turned, 1, low)
         scalar_gain(2, low)
         scalar_gain(2, high)
         scalar_gain(3, high)
         quantize_h(0, low)
         quantize_h(1, low)
         valves(0, 0, low, (0, 1), None)
+        h_bf[1, high.start] = h_bf[0, low.start]
+        apply_gain(nc.vector, turned, 1, high)
         quantize_h(0, high)
         quantize_h(1, high)
         valves(4, 0, high, (0, 1), None)
+        h_bf[3, low.start] = h_bf[1, low.start]
         apply_gain(nc.vector, turned, 3, low)
+        half_tile(2, low)
         interleave(2, low)
         quantize_h(3, low)
         quantize_h(2, low)
-        valves(8, 1, low, (0, 1), None)
+        valves(8, 1, low, (1, 0), None)
+        half_tile(2, high)
+        half_tile(3, high)
         interleave(2, high)
         interleave(3, high)
         quantize_h(2, high)

@@ -27,6 +27,7 @@ TAB_ROWS = (48, 112)
 TAB2_ROW = 4
 FLOW_ROW = 126
 FLOW_BANK = 7
+POOL_LATE = 48
 EARLY_SUMS = 3
 
 
@@ -290,11 +291,12 @@ def tile_list_orchard_spray_dosing_kernel(
                 if (k, t) == (1, 0):
                     gather_words(1, 1)
             if k == 0:
-                for part in (low, high):
-                    half_tile(0, part)
+                half_tile(0, low)
+                shared = held("h_bf_shared", [P, PACK * (W - POOL_LATE)], BF16)
+                h_bf[0, high.start] = shared[:, 0 : PACK * W // 2]
+                h_bf[1, low.start] = shared[:, PACK * (W // 2 - POOL_LATE) :]
                 apply_gain(nc.gpsimd, gain, 0, low)
-                apply_gain(nc.gpsimd, gain, 0, high)
-        half_tile(1, low)
+                apply_gain(nc.gpsimd, gain, 0, slice(high.start, W - POOL_LATE))
         apply_gain(nc.vector, turned, 1, low)
         scalar_gain(2, low)
         scalar_gain(2, high)
@@ -302,6 +304,7 @@ def tile_list_orchard_spray_dosing_kernel(
         quantize_h(0, low)
         quantize_h(1, low)
         valves(0, 0, low, (0, 1), None)
+        apply_gain(nc.gpsimd, gain, 0, slice(W - POOL_LATE, W))
         h_bf[1, high.start] = h_bf[0, low.start]
         apply_gain(nc.vector, turned, 1, high)
         quantize_h(0, high)

@@ -27,6 +27,7 @@ TAB_ROWS = (48, 112)
 TAB2_ROW = 4
 FLOW_ROW = 126
 FLOW_BANK = 7
+POOL_EXTRA = 64
 POOL_LATE = 48
 EARLY_SUMS = 3
 
@@ -57,13 +58,14 @@ def tile_list_orchard_spray_dosing_kernel(
         tab2s = placed("tab2s", [P, T], U8, 11 * KIB // 2)
         tab2w = placed("tab2w", [P, T], U16, 26 * KIB)
         w1w_raw = held("w1w_raw", [P, 2 * H], U16)
-        w1s_raw = held("w1s_raw", [P, H], U8)
+        w1s_raw = placed("w1s_raw", [P, H], U8, 34 * KIB)
         w2_raw = held("w2_raw", [P, PACK, H], F32)
         w2_bf = [held("w2_bf%d" % b, [P, PACK * KP], BF16) for b in range(2)]
         w2w = [held("w2w%d" % b, [P, KP], U32) for b in range(2)]
         w2s = [held("w2s%d" % b, [P, KP], U8) for b in range(2)]
+        neg_noz = held("neg_noz", [P, 2, PACK], F32)
         vw = [[held("vw%d_%d" % (a, u), [P, W], U32) for u in range(2)] for a in range(2)]
-        vs_rows = placed("vs_rows", [P, S], U8, 34 * KIB)
+        vs_rows = held("vs_rows", [P, S], U8)
         v2s_rows = held("v2s_rows", [P, S], U8)
         ident = held("ident", [P, P], F32)
         gain = held("gain", [P, 2, PACK], F32)
@@ -80,7 +82,8 @@ def tile_list_orchard_spray_dosing_kernel(
             nc.sync.dma_start(out=tile[TAB_ROWS[a] : TAB_ROWS[a] + 16, :].bitcast(I32), in_=scales[a].bitcast(I32))
 
         def lift_rows(a, r):
-            nc.sync.dma_start(
+            queue = nc.gpsimd if (a, r) == (1, ROWS - 1) else nc.sync
+            queue.dma_start(
                 out=planes[a][r:P:32, :].bitcast(I32),
                 in_=joined[TAB_ROWS[a] + r : TAB_ROWS[a] + 16 : ROWS, :].bitcast(I32),
             )
@@ -154,26 +157,22 @@ def tile_list_orchard_spray_dosing_kernel(
         cast_w2(1, nc.scalar.copy)
         quantize_w2(0)
         joined = held("w2_bf0", [P, S + H], U8)
+        nc.vector.tensor_copy(out=joined[:, 0:S].bitcast(I32), in_=vs_rows[:].bitcast(I32))
         order_columns(joined[:, S:], w1s_raw)
-        for half in (slice(0, P // 2), slice(P // 2, P)):
-            nc.vector.tensor_copy(out=joined[half, 0:S].bitcast(I32), in_=vs_rows[half, :].bitcast(I32))
         v2s = placed("v2s", [P, S], U8, 6 * KIB)
         planes = [placed("plane%d" % a, [P, S + H], U8, a * (S + H)) for a in range(2)]
-        tabw[0] = placed("tabw0", [P, T], U32, 9 * KIB + 64)
-        noz = placed("noz", [P, 2, PACK], F32, 9 * KIB)
+        tabw[0] = placed("tabw0", [P, T], U32, 9 * KIB)
         tabw[1] = placed("tabw1", [P, T], U32, 26 * KIB)
         flow_rows = placed("flow_rows", [P, KP], F32, 4 * KIB)
         for r in range(ROWS):
             nc.sync.dma_start(out=v2s[r:P:32, :].bitcast(I32), in_=v2s_rows[TAB2_ROW + 8 * r : P : 32, :].bitcast(I32))
         load_tab(0)
         nc.sync.dma_start(out=flow_rows[FLOW_ROW:P, :], in_=flow.rearrange("(b c) -> b c", b=2))
-        nc.sync.dma_start(out=noz[:], in_=nozzle.rearrange("(b p t) -> p b t", b=2, t=PACK))
         nc.gpsimd.memset(flow_rows[0:FLOW_ROW, :], 0.0)
-        lifts = [(a, r) for a in range(2) for r in range(ROWS)]
-        lift_rows(*lifts[0])
         load_tab(1)
-        for a, r in lifts[1:]:
-            lift_rows(a, r)
+        for a in range(2):
+            for r in range(ROWS):
+                lift_rows(a, r)
 
         make_allowed(0)
         flow_bank = bank(FLOW_BANK)
@@ -185,11 +184,13 @@ def tile_list_orchard_spray_dosing_kernel(
         w1w = held("w2_bf1", [P, 2 * H], U16)
         order_columns(w1w[:], w1w_raw)
         make_allowed(1)
+        late_vectors = held("w1w_raw", [P, 6 * PACK], F32)
+        rest = late_vectors[:, 2 * PACK : 3 * PACK]
+        noz = late_vectors[:, 4 * PACK : 6 * PACK].rearrange("p (b t) -> p b t", b=2)
+        nc.sync.dma_start(out=noz, in_=nozzle.rearrange("(b p t) -> p b t", b=2, t=PACK))
         gather_words(0, 0)
         gather_words(0, 1)
-        neg_noz = placed("neg_noz", [P, 2, PACK], F32, 15 * KIB)
-        nc.vector.tensor_scalar(neg_noz[:], noz[:], -1.0, None, ALU.mult)
-        w3_bytes = placed("w3_bytes", [P, 2 * N + 2 * N // 4], U32, 10 * KIB)
+        w3_bytes = placed("w3_bytes", [P, 2 * N + 2 * N // 4], U32, 9 * KIB)
         w3w = w3_bytes[:, 0 : 2 * N]
         w3s = w3_bytes[:, 2 * N :].bitcast(U8)
         nc.sync.dma_start(
@@ -197,14 +198,14 @@ def tile_list_orchard_spray_dosing_kernel(
             in_=w3_words.rearrange("a p c i -> p a (c i)").bitcast(I32),
         )
         load_scale_rows(w3s, w3_scales)
-        rest = placed("rest", [P, PACK], F32, 15 * KIB + 64)
         with nc.allow_non_contiguous_dma(reason="one idle value a partition"):
-            nc.sync.dma_start(out=rest[:], in_=idle.rearrange("(i p) -> p i", p=P))
+            nc.sync.dma_start(out=rest, in_=idle.rearrange("(i p) -> p i", p=P))
         gather_words(1, 0)
+        nc.scalar.activation(neg_noz[:], noz, ACT.Copy, scale=-1.0)
 
         units = [(0, 0), (1, 0), (0, 1), (1, 1)]
         demand, act, rounded, h_bf, hw, hs = {}, {}, {}, {}, {}, {}
-        whole = slice(0, W)
+        whole, low, high = slice(0, W), slice(0, W // 2), slice(W // 2, W)
 
         def make_demand(k, t):
             b, u = units[k]
@@ -218,9 +219,14 @@ def tile_list_orchard_spray_dosing_kernel(
                     start=(a == passes[0]), stop=(a == passes[1]),
                 )
             if t == 0:
-                act[k] = ring.tile([P, PACK, W], F32, name="act")
+                for half in (low, high) if k == 0 else (whole,):
+                    act[k, half.start] = held("act%d_%d" % (k, half.start), [P, PACK, half.stop - half.start], F32)
                 hw[k] = held("hw%d" % k, [P, W], U32)
                 hs[k] = held("hs%d" % k, [P, W], U8)
+
+        def activated(k, part):
+            first = high.start if k == 0 and part.start >= high.start else 0
+            return act[k, first][:, :, part.start - first : part.stop - first]
 
         def dose(k, t, part):
             b, u = units[k]
@@ -228,7 +234,7 @@ def tile_list_orchard_spray_dosing_kernel(
                 make_demand(k, t)
             least = ring.tile([P, part.stop - part.start], F32, name="least", bufs=8)
             nc.vector.tensor_tensor(least[:], demand[k, t][:, part], allowed[b, u, t][:, part], ALU.min)
-            nc.scalar.activation(act[k][:, t, part], least[:], ACT.Silu, bias=neg_noz[:, b, t : t + 1])
+            nc.scalar.activation(activated(k, part)[:, t, :], least[:], ACT.Silu, bias=neg_noz[:, b, t : t + 1])
 
         def rounded_h(k, part):
             first = part.start // (W // 2) * (W // 2)
@@ -242,7 +248,7 @@ def tile_list_orchard_spray_dosing_kernel(
             pairs = (part.stop - part.start) // 2
             engine.tensor_tensor(
                 rounded_h(k, part).rearrange("p (c i t) -> p c t i", i=2, t=PACK),
-                act[k][:, :, part].rearrange("p t (c i) -> p c t i", i=2),
+                activated(k, part).rearrange("p t (c i) -> p c t i", i=2),
                 factors[:, b, :].unsqueeze(1).unsqueeze(3).to_broadcast([P, pairs, PACK, 2]),
                 ALU.mult,
             )
@@ -251,7 +257,7 @@ def tile_list_orchard_spray_dosing_kernel(
             b, u = units[k]
             rounded[k, part.start] = held("rounded%d_%d" % (k, part.start), [P, PACK, part.stop - part.start], BF16)
             for t in range(PACK):
-                nc.scalar.activation(rounded[k, part.start][:, t, :], act[k][:, t, part], ACT.Copy, scale=gain[:, b, t : t + 1])
+                nc.scalar.activation(rounded[k, part.start][:, t, :], activated(k, part)[:, t, :], ACT.Copy, scale=gain[:, b, t : t + 1])
 
         def interleave(k, part):
             nc.vector.tensor_copy(
@@ -284,12 +290,14 @@ def tile_list_orchard_spray_dosing_kernel(
                     nc.scalar.activation(res[:], acc[i][:, part], ACT.Identity, bias=rest[:, i : i + 1])
                 nc.sync.dma_start(out=out[i * P : (i + 1) * P, u * W + part.start : u * W + part.stop], in_=res[:])
 
-        low, high = slice(0, W // 2), slice(W // 2, W)
         for k in range(4):
-            for t in range(PACK):
-                dose(k, t, whole)
-                if (k, t) == (1, 0):
-                    gather_words(1, 1)
+            for part in (low, high) if k == 0 else (whole,):
+                for t in range(PACK):
+                    dose(k, t, part)
+                    if (k, t) == (1, 0):
+                        gather_words(1, 1)
+            if k == 1:
+                apply_gain(nc.gpsimd, gain, 1, slice(low.stop - POOL_EXTRA, low.stop))
             if k == 0:
                 half_tile(0, low)
                 shared = held("h_bf_shared", [P, PACK * (W - POOL_LATE)], BF16)
@@ -297,7 +305,7 @@ def tile_list_orchard_spray_dosing_kernel(
                 h_bf[1, low.start] = shared[:, PACK * (W // 2 - POOL_LATE) :]
                 apply_gain(nc.gpsimd, gain, 0, low)
                 apply_gain(nc.gpsimd, gain, 0, slice(high.start, W - POOL_LATE))
-        apply_gain(nc.vector, turned, 1, low)
+        apply_gain(nc.vector, turned, 1, slice(0, low.stop - POOL_EXTRA))
         scalar_gain(2, low)
         scalar_gain(2, high)
         scalar_gain(3, high)

@@ -21,15 +21,17 @@ P = 128
 PACK = 4
 KP = P * PACK
 W = 512
-KIB = 1024
+HALF = W // 2
 ROWS = 4
-TAB_ROWS = (48, 112)
-TAB2_ROW = 4
+TAB_ROW = 96
+TAB2_ROW = 48
+NOZZLE_ROW = 124
 FLOW_ROW = 126
-FLOW_BANK = 7
+RING = 7
+VECTOR_BANK = 7
 POOL_EXTRA = 64
 POOL_LATE = 48
-EARLY_SUMS = 3
+EARLY_SUMS = 7
 
 
 def tile_list_orchard_spray_dosing_kernel(
@@ -46,181 +48,193 @@ def tile_list_orchard_spray_dosing_kernel(
         def held(name, shape, dtype):
             return keep.tile(shape, dtype, name=name, align_bytes=64)
 
-        def placed(name, shape, dtype, offset):
-            return reuse.tile(shape, dtype, name=name, align_bytes=64, offset=offset)
+        def placed(name, shape, dtype, kib):
+            return reuse.tile(shape, dtype, name=name, align_bytes=64, offset=int(kib * 1024))
 
         def bank(i):
             return psum.tile([P, W], F32, name="bank%d" % i)
 
         list1 = keep.tile([P, S // 16], U16, name="list1")
         list2 = keep.tile([P, S // 16], U16, name="list2")
-        tabs = placed("tabs", [P, T], U8, 0)
-        tab2s = placed("tab2s", [P, T], U8, 11 * KIB // 2)
-        tab2w = placed("tab2w", [P, T], U16, 26 * KIB)
-        w1w_raw = held("w1w_raw", [P, 2 * H], U16)
-        w1s_raw = placed("w1s_raw", [P, H], U8, 34 * KIB)
-        w2_raw = held("w2_raw", [P, PACK, H], F32)
-        w2_bf = [held("w2_bf%d" % b, [P, PACK * KP], BF16) for b in range(2)]
-        w2w = [held("w2w%d" % b, [P, KP], U32) for b in range(2)]
-        w2s = [held("w2s%d" % b, [P, KP], U8) for b in range(2)]
-        neg_noz = held("neg_noz", [P, 2, PACK], F32)
-        vw = [[held("vw%d_%d" % (a, u), [P, W], U32) for u in range(2)] for a in range(2)]
-        vs_rows = held("vs_rows", [P, S], U8)
+        tab2s = placed("tab2s", [P, T], U8, 16)
+        tabs = placed("tabs", [P, T], U8, 36)
+        w1s_raw = placed("w1s_raw", [P, H], U8, 44)
+        w2_raw = [placed("w2_raw0", [P, PACK, KP], F32, 58), placed("w2_raw1", [P, PACK, KP], F32, 66)]
+        tab2w = held("tab2w", [P, T], U16)
         v2s_rows = held("v2s_rows", [P, S], U8)
+        vector_rows = held("vector_rows", [P, KP], F32)
         ident = held("ident", [P, P], F32)
-        gain = held("gain", [P, 2, PACK], F32)
-        tabw = {}
 
-        def load_scale_rows(tile, scales):
-            for r in range(ROWS):
-                nc.sync.dma_start(
-                    out=tile[r:P:32, :].bitcast(I32).rearrange("p (a c) -> p a c", a=scales.shape[0]),
-                    in_=scales.bitcast(I32).rearrange("a (q r) c -> r q a c", r=ROWS)[r],
-                )
+        def visits(u):
+            return slice(u * (W // 16), (u + 1) * (W // 16))
 
-        def load_wide(tile, scales, a):
-            nc.sync.dma_start(out=tile[TAB_ROWS[a] : TAB_ROWS[a] + 16, :].bitcast(I32), in_=scales[a].bitcast(I32))
-
-        def lift_rows(a, r):
-            queue = nc.gpsimd if (a, r) == (1, ROWS - 1) else nc.sync
-            queue.dma_start(
-                out=planes[a][r:P:32, :].bitcast(I32),
-                in_=joined[TAB_ROWS[a] + r : TAB_ROWS[a] + 16 : ROWS, :].bitcast(I32),
-            )
-
-        def load_tab(a):
-            nc.sync.dma_start(out=tabw[a][:].bitcast(I32), in_=tab_words[a].rearrange("p t i -> p (t i)").bitcast(I32))
-
-        def order_columns(ordered, raw):
-            nc.vector.tensor_copy(
-                out=ordered.rearrange("p (g t m) -> p g t m", t=PACK, m=P),
-                in_=raw[:].rearrange("p (g m t) -> p g t m", t=PACK, m=P),
-            )
-
-        def cast_w2(b, copy):
+        def order_columns(copy, ordered, raw):
             copy(
-                out=w2_bf[b][:].rearrange("p (s e m j) -> p s m j e", s=2, e=2, j=PACK),
-                in_=w2_raw[:, :, b * KP : (b + 1) * KP].rearrange("p j (m s e) -> p s m j e", s=2, e=2),
+                out=ordered.rearrange("p (g t m) -> p g t m", t=PACK, m=P),
+                in_=raw.rearrange("p (g m t) -> p g t m", t=PACK, m=P),
             )
 
-        def quantize_w2(b):
-            nc.vector.quantize_mx(out=w2w[b][:].bitcast(FP8X4), scales=w2s[b][:], in_=w2_bf[b][:])
-
-        def gather_words(a, u):
-            nc.vector.tensor_copy(vw[a][u][:], tabw[a][:].indirect(list1[:, u * (W // 16) : (u + 1) * (W // 16)]))
-
-        allowed = {}
-
-        def make_allowed(b):
-            for u in range(2):
-                for t in range(PACK):
-                    acc = bank(t)
-                    cols = slice(t * P, (t + 1) * P)
-                    toks = slice(u * W, (u + 1) * W)
-                    nc.tensor.matmul_mx(
-                        out=acc[:], lhsT=w2w[b][:, cols].bitcast(FP8X4), lhsT_scale=w2s[b][:, cols],
-                        rhs=v2w[:, toks].bitcast(FP4X4), rhs_scale=v2s[:, toks], start=True, stop=True,
-                    )
-                    allowed[b, u, t] = held("allowed%d_%d_%d" % (b, u, t), [P, W], F32)
-                    nc.scalar.copy(out=allowed[b, u, t][:], in_=acc[:])
-
-        for lo, hi in ((0, TAB_ROWS[0]), (64, TAB_ROWS[1])):
-            nc.vector.memset(tabs[lo:hi, :].bitcast(I32), 0)
-        nc.gpsimd.memset(tab2s[:].bitcast(I32), 0)
-        for lo, hi in ((0, TAB_ROWS[0]), (64, TAB_ROWS[1])):
-            nc.gpsimd.memset(w1s_raw[lo:hi, :].bitcast(I32), 0)
+        nc.vector.memset(tab2s[0:TAB2_ROW, :].bitcast(I32), 0)
+        nc.vector.memset(tab2s[TAB2_ROW + 16 : P, :].bitcast(I32), 0)
+        nc.gpsimd.memset(tabs[0:TAB_ROW, :].bitcast(I32), 0)
+        nc.gpsimd.memset(vector_rows[0:NOZZLE_ROW, :], 0.0)
         make_identity(nc, ident[:])
+        nc.gpsimd.memset(w1s_raw[0:TAB_ROW, :].bitcast(I32), 0)
 
         warm = held("warm", [P, 2], F32)
         nc.vector.memset(warm[:, 0:1], 0.0)
         nc.scalar.activation(warm[:, 1:2], warm[:, 0:1], ACT.Silu)
 
-        nc.sync.dma_start(list1[:], offs)
-        for a in range(2):
-            load_wide(tabs, tab_scales, a)
+        def load_w2(b):
+            nc.sync.dma_start(out=w2_raw[b][:], in_=w2.rearrange("(p j) c -> p j c", j=PACK)[:, :, b * KP : (b + 1) * KP])
+
         nc.sync.dma_start(list2[:], offs2)
+        nc.sync.dma_start(out=tab2s[TAB2_ROW : TAB2_ROW + 16, :].bitcast(I32), in_=tab2_scales[0].bitcast(I32))
+        nc.sync.dma_start(list1[:], offs)
+        nc.sync.dma_start(out=tabs[TAB_ROW:P, :].bitcast(I32), in_=tab_scales.rearrange("a q c -> (a q) c").bitcast(I32))
+        load_w2(0)
         nc.sync.dma_start(out=tab2w[:].bitcast(I32), in_=tab2_words[0].bitcast(I32))
-        nc.sync.dma_start(out=tab2s[TAB2_ROW:P:8, :].bitcast(I32), in_=tab2_scales[0].bitcast(I32))
-        load_wide(w1s_raw, w1_scales, 0)
-        nc.sync.dma_start(out=w2_raw[:].rearrange("p j c -> p (j c)"), in_=w2.rearrange("(p j) c -> p (j c)", j=PACK))
-        load_wide(w1s_raw, w1_scales, 1)
-        nc.sync.dma_start(
-            out=w1w_raw[:].bitcast(I32).rearrange("p (a c) -> p a c", a=2),
-            in_=w1_words.bitcast(I32).rearrange("a p c -> p a c"),
-        )
+        nc.sync.dma_start(out=vector_rows[NOZZLE_ROW:FLOW_ROW, :], in_=nozzle.rearrange("(b c) -> b c", b=2))
+        nc.sync.dma_start(out=vector_rows[FLOW_ROW:P, :], in_=flow.rearrange("(b c) -> b c", b=2))
+        nc.sync.dma_start(out=w1s_raw[TAB_ROW:P, :].bitcast(I32), in_=w1_scales.rearrange("a q c -> (a q) c").bitcast(I32))
+        load_w2(1)
 
-        nc.vector.tensor_copy(vs_rows[:], tabs[:].indirect(list1[:]))
-        nc.vector.tensor_copy(v2s_rows[:], tab2s[:].indirect(list2[:]))
-        v2w = placed("v2w", [P, S], U16, 7 * KIB)
-        nc.vector.tensor_copy(v2w[:], tab2w[:].indirect(list2[:]))
-        cast_w2(0, nc.vector.tensor_copy)
-        cast_w2(1, nc.scalar.copy)
-        quantize_w2(0)
-        joined = held("w2_bf0", [P, S + H], U8)
-        nc.vector.tensor_copy(out=joined[:, 0:S].bitcast(I32), in_=vs_rows[:].bitcast(I32))
-        order_columns(joined[:, S:], w1s_raw)
-        v2s = placed("v2s", [P, S], U8, 6 * KIB)
-        planes = [placed("plane%d" % a, [P, S + H], U8, a * (S + H)) for a in range(2)]
-        tabw[0] = placed("tabw0", [P, T], U32, 9 * KIB)
-        tabw[1] = placed("tabw1", [P, T], U32, 26 * KIB)
-        flow_rows = placed("flow_rows", [P, KP], F32, 4 * KIB)
-        for r in range(ROWS):
-            nc.sync.dma_start(out=v2s[r:P:32, :].bitcast(I32), in_=v2s_rows[TAB2_ROW + 8 * r : P : 32, :].bitcast(I32))
-        load_tab(0)
-        nc.sync.dma_start(out=flow_rows[FLOW_ROW:P, :], in_=flow.rearrange("(b c) -> b c", b=2))
-        nc.gpsimd.memset(flow_rows[0:FLOW_ROW, :], 0.0)
-        load_tab(1)
-        for a in range(2):
-            for r in range(ROWS):
-                lift_rows(a, r)
-
-        make_allowed(0)
-        flow_bank = bank(FLOW_BANK)
+        vectors = bank(VECTOR_BANK)
         for t in range(PACK):
-            nc.tensor.transpose(flow_bank[:, t * P : (t + 1) * P], flow_rows[:, t:KP:PACK], ident[:])
-        turned = flow_bank[:].rearrange("p (t j) -> p j t", t=PACK)[:, FLOW_ROW:P, :]
-        nc.scalar.copy(out=gain[:], in_=turned)
-        quantize_w2(1)
-        w1w = held("w2_bf1", [P, 2 * H], U16)
-        order_columns(w1w[:], w1w_raw)
-        make_allowed(1)
-        late_vectors = held("w1w_raw", [P, 6 * PACK], F32)
-        rest = late_vectors[:, 2 * PACK : 3 * PACK]
-        noz = late_vectors[:, 4 * PACK : 6 * PACK].rearrange("p (b t) -> p b t", b=2)
-        nc.sync.dma_start(out=noz, in_=nozzle.rearrange("(b p t) -> p b t", b=2, t=PACK))
+            nc.tensor.transpose(vectors[:, t * P : (t + 1) * P], vector_rows[:, t:KP:PACK], ident[:])
+        turned = vectors[:].rearrange("p (t j) -> p j t", t=PACK)
+
+        nc.vector.tensor_copy(v2s_rows[:], tab2s[:].indirect(list2[:]))
+        v2s = placed("v2s", [P, S], U8, 16.5)
+        for r in range(ROWS):
+            nc.sync.dma_start(out=v2s[r:P:32, :].bitcast(I32), in_=v2s_rows[TAB2_ROW + r : TAB2_ROW + 16 : ROWS, :].bitcast(I32))
+        tabw, w1_raw = {}, {}
+
+        def load_tab(a, kib):
+            tabw[a] = placed("tabw%d" % a, [P, T], U32, kib)
+            nc.sync.dma_start(out=tabw[a][:].bitcast(I32), in_=tab_words[a].rearrange("p t i -> p (t i)").bitcast(I32))
+
+        def load_w1(a, kib):
+            w1_raw[a] = placed("w1_raw%d" % a, [P, H], U16, kib)
+            nc.sync.dma_start(out=w1_raw[a][:].bitcast(I32), in_=w1_words[a].bitcast(I32))
+
+        load_tab(0, 19.75)
+        load_w1(0, 17.5)
+        vs_rows = placed("vs_rows", [P, S], U8, 90)
+        nc.vector.tensor_copy(vs_rows[:], tabs[:].indirect(list1[:]))
+        w2w = [placed("w2w%d" % b, [P, KP], U32, 50 + 2 * b) for b in range(2)]
+        w2s = [held("w2s%d" % b, [P, KP], U8) for b in range(2)]
+
+        def cast_w2(copy, rounded, b):
+            copy(
+                out=rounded[:].rearrange("p (s e m j) -> p s m j e", s=2, e=2, j=PACK),
+                in_=w2_raw[b][:].rearrange("p j (m s e) -> p s m j e", s=2, e=2),
+            )
+
+        def quantize_w2(rounded, b):
+            nc.vector.quantize_mx(out=w2w[b][:].bitcast(FP8X4), scales=w2s[b][:], in_=rounded[:])
+
+        v2w = {0: held("v2w0", [P, W], U16)}
+        nc.vector.tensor_copy(v2w[0][:], tab2w[:].indirect(list2[:, visits(0)]))
+        first_block = placed("w2_first", [P, PACK * KP], BF16, 40)
+        cast_w2(nc.scalar.copy, first_block, 0)
+        neg_noz = placed("neg_noz", [P, 2, PACK], F32, 58)
+        gain = placed("gain", [P, 2, PACK], F32, 58.25)
+        nc.scalar.activation(neg_noz[:], turned[:, NOZZLE_ROW:FLOW_ROW, :], ACT.Copy, scale=-1.0)
+        nc.scalar.copy(out=gain[:], in_=turned[:, FLOW_ROW:P, :])
+        quantize_w2(first_block, 0)
+        joined = placed("joined", [P, S + H], U8, 40)
+        order_columns(nc.vector.tensor_copy, joined[:, S:], w1s_raw[:])
+        nc.vector.tensor_copy(out=joined[:, 0:S].bitcast(I32), in_=vs_rows[:].bitcast(I32))
+        planes = [placed("plane%d" % a, [P, S + H], U8, 36 + 2 * a) for a in range(2)]
+
+        def lift_rows(a):
+            for r in range(ROWS):
+                first = TAB_ROW + 16 * a + r
+                nc.sync.dma_start(out=planes[a][r:P:32, :].bitcast(I32), in_=joined[first : TAB_ROW + 16 * (a + 1) : ROWS, :].bitcast(I32))
+
+        lift_rows(0)
+        load_tab(1, 90.5)
+        load_w1(1, 88.5)
+        lift_rows(1)
+        v2w[1] = placed("v2w1", [P, W], U16, 42)
+        nc.vector.tensor_copy(v2w[1][:], tab2w[:].indirect(list2[:, visits(1)]))
+        second_block = placed("w2_second", [P, PACK * KP], BF16, 44)
+        cast_w2(nc.vector.tensor_copy, second_block, 1)
+        quantize_w2(second_block, 1)
+
+        vw = [[placed("vw0_%d" % u, [P, W], U32, 44 + 2 * u) for u in range(2)], [held("vw1_%d" % u, [P, W], U32) for u in range(2)]]
+
+        def gather_words(a, u):
+            nc.vector.tensor_copy(vw[a][u][:], tabw[a][:].indirect(list1[:, visits(u)]))
+
         gather_words(0, 0)
+        w1_first = held("w1_first", [P, H], U16)
+        order_columns(nc.vector.tensor_copy, w1_first[:], w1_raw[0][:])
+        w1w = {(0, b): w1_first[:, b * KP : (b + 1) * KP] for b in range(2)}
         gather_words(0, 1)
-        w3_bytes = placed("w3_bytes", [P, 2 * N + 2 * N // 4], U32, 9 * KIB)
-        w3w = w3_bytes[:, 0 : 2 * N]
-        w3s = w3_bytes[:, 2 * N :].bitcast(U8)
+
+        rest = placed("rest", [P, PACK], F32, 24)
+        with nc.allow_non_contiguous_dma(reason="one idle value a partition"):
+            nc.sync.dma_start(out=rest[:], in_=idle.rearrange("(i p) -> p i", p=P))
+        w3w = placed("w3w", [P, 2 * N], U32, 24.5)
+        w3s = placed("w3s", [P, 2 * N], U8, 28.5)
         nc.sync.dma_start(
-            out=w3w.bitcast(I32).rearrange("p (a c) -> p a c", a=2),
+            out=w3w[:].bitcast(I32).rearrange("p (a c) -> p a c", a=2),
             in_=w3_words.rearrange("a p c i -> p a (c i)").bitcast(I32),
         )
-        load_scale_rows(w3s, w3_scales)
-        with nc.allow_non_contiguous_dma(reason="one idle value a partition"):
-            nc.sync.dma_start(out=rest, in_=idle.rearrange("(i p) -> p i", p=P))
-        gather_words(1, 0)
-        nc.scalar.activation(neg_noz[:], noz, ACT.Copy, scale=-1.0)
+        for r in range(ROWS):
+            nc.sync.dma_start(
+                out=w3s[r:P:32, :].bitcast(I32).rearrange("p (a c) -> p a c", a=2),
+                in_=w3_scales.bitcast(I32).rearrange("a (q r) c -> r q a c", r=ROWS)[r],
+            )
 
+        allowed = {}
+        shared_bytes = {12: 30, 13: 32}
+        sums = [(b, u, t) for b in range(2) for u in range(2) for t in range(PACK)]
+        for n, (b, u, t) in enumerate(sums):
+            acc = bank(n % 4 if n < 12 else 4 + n % 3)
+            nc.tensor.matmul_mx(
+                out=acc[:], lhsT=w2w[b][:, t * P : (t + 1) * P].bitcast(FP8X4), lhsT_scale=w2s[b][:, t * P : (t + 1) * P],
+                rhs=v2w[u][:].bitcast(FP4X4), rhs_scale=v2s[:, u * W : (u + 1) * W], start=True, stop=True,
+            )
+            if n in shared_bytes:
+                allowed[b, u, t] = placed("allowed%d_%d_%d" % (b, u, t), [P, W], F32, shared_bytes[n])
+            else:
+                allowed[b, u, t] = held("allowed%d_%d_%d" % (b, u, t), [P, W], F32)
+            if n in (12, 13):
+                nc.vector.tensor_copy(out=allowed[b, u, t][:], in_=acc[:])
+            else:
+                nc.scalar.copy(out=allowed[b, u, t][:], in_=acc[:])
+
+        gather_words(1, 0)
+        gather_words(1, 1)
+        for b in range(2):
+            ordered = placed("w1_second%d" % b, [P, KP], U16, 52 + b)
+            order_columns(nc.scalar.copy, ordered[:], w1_raw[1][:, b * KP : (b + 1) * KP])
+            w1w[1, b] = ordered[:]
+
+        flow_turned = turned[:, FLOW_ROW:P, :]
         units = [(0, 0), (1, 0), (0, 1), (1, 1)]
         demand, act, rounded, h_bf, hw, hs = {}, {}, {}, {}, {}, {}
         whole, low, high = slice(0, W), slice(0, W // 2), slice(W // 2, W)
 
         def make_demand(k, t):
             b, u = units[k]
-            demand[k, t] = bank((4 + PACK * k + t) % FLOW_BANK)
+            demand[k, t] = bank((PACK * k + t) % RING)
             passes = (0, 1) if PACK * k + t < EARLY_SUMS else (1, 0)
             for a in passes:
-                cols = slice(a * H + b * KP + t * P, a * H + b * KP + (t + 1) * P)
                 nc.tensor.matmul_mx(
-                    out=demand[k, t][:], lhsT=w1w[:, cols].bitcast(FP4X4), lhsT_scale=planes[a][:, S + b * KP + t * P : S + b * KP + (t + 1) * P],
+                    out=demand[k, t][:], lhsT=w1w[a, b][:, t * P : (t + 1) * P].bitcast(FP4X4), lhsT_scale=planes[a][:, S + b * KP + t * P : S + b * KP + (t + 1) * P],
                     rhs=vw[a][u][:].bitcast(FP8X4), rhs_scale=planes[a][:, u * W : (u + 1) * W],
                     start=(a == passes[0]), stop=(a == passes[1]),
                 )
             if t == 0:
                 for half in (low, high) if k == 0 else (whole,):
-                    act[k, half.start] = held("act%d_%d" % (k, half.start), [P, PACK, half.stop - half.start], F32)
+                    if (k, half) == (0, low):
+                        act[k, half.start] = placed("act_first", [P, PACK, HALF], F32, 86)
+                    else:
+                        act[k, half.start] = held("act%d_%d" % (k, half.start), [P, PACK, half.stop - half.start], F32)
                 hw[k] = held("hw%d" % k, [P, W], U32)
                 hs[k] = held("hs%d" % k, [P, W], U8)
 
@@ -272,7 +286,7 @@ def tile_list_orchard_spray_dosing_kernel(
             )
 
         def valves(first_bank, u, part, blocks, vector_pair):
-            acc = [bank((first_bank + i) % FLOW_BANK) for i in range(4)]
+            acc = [bank((first_bank + 3 + i) % RING) for i in range(4)]
             for b in blocks:
                 k = units.index((b, u))
                 for i in range(4):
@@ -283,7 +297,7 @@ def tile_list_orchard_spray_dosing_kernel(
                         start=(b == blocks[0]), stop=(b == blocks[1]),
                     )
             for i in range(4):
-                res = held("res%d_%d_%d" % (i, u, part.start), [P, part.stop - part.start], F32)
+                res = placed("res%d_%d_%d" % (i, u, part.start), [P, HALF], F32, first_bank + i)
                 if i % 2 == vector_pair:
                     nc.vector.tensor_scalar(res[:], acc[i][:, part], rest[:, i : i + 1], None, ALU.add)
                 else:
@@ -294,8 +308,6 @@ def tile_list_orchard_spray_dosing_kernel(
             for part in (low, high) if k == 0 else (whole,):
                 for t in range(PACK):
                     dose(k, t, part)
-                    if (k, t) == (1, 0):
-                        gather_words(1, 1)
             if k == 1:
                 apply_gain(nc.gpsimd, gain, 1, slice(low.stop - POOL_EXTRA, low.stop))
             if k == 0:
@@ -305,7 +317,7 @@ def tile_list_orchard_spray_dosing_kernel(
                 h_bf[1, low.start] = shared[:, PACK * (W // 2 - POOL_LATE) :]
                 apply_gain(nc.gpsimd, gain, 0, low)
                 apply_gain(nc.gpsimd, gain, 0, slice(high.start, W - POOL_LATE))
-        apply_gain(nc.vector, turned, 1, slice(0, low.stop - POOL_EXTRA))
+        apply_gain(nc.vector, flow_turned, 1, slice(0, low.stop - POOL_EXTRA))
         scalar_gain(2, low)
         scalar_gain(2, high)
         scalar_gain(3, high)
@@ -314,12 +326,12 @@ def tile_list_orchard_spray_dosing_kernel(
         valves(0, 0, low, (0, 1), None)
         apply_gain(nc.gpsimd, gain, 0, slice(W - POOL_LATE, W))
         h_bf[1, high.start] = h_bf[0, low.start]
-        apply_gain(nc.vector, turned, 1, high)
+        apply_gain(nc.vector, flow_turned, 1, high)
         quantize_h(0, high)
         quantize_h(1, high)
         valves(4, 0, high, (0, 1), None)
         h_bf[3, low.start] = h_bf[1, low.start]
-        apply_gain(nc.vector, turned, 3, low)
+        apply_gain(nc.vector, flow_turned, 3, low)
         half_tile(2, low)
         interleave(2, low)
         quantize_h(3, low)

@@ -29,9 +29,6 @@ NOZZLE_ROW = 124
 FLOW_ROW = 126
 RING = 7
 VECTOR_BANK = 7
-POOL_EXTRA = 64
-POOL_LATE = 48
-EARLY_SUMS = 7
 
 
 def tile_list_orchard_spray_dosing_kernel(
@@ -58,8 +55,10 @@ def tile_list_orchard_spray_dosing_kernel(
         list2 = keep.tile([P, S // 16], U16, name="list2")
         tab2s = placed("tab2s", [P, T], U8, 16)
         tabs = placed("tabs", [P, T], U8, 36)
-        w1s_raw = placed("w1s_raw", [P, H], U8, 44)
-        w2_raw = [placed("w2_raw0", [P, PACK, KP], F32, 58), placed("w2_raw1", [P, PACK, KP], F32, 66)]
+        w1s_raw = held("w1s_raw", [P, H], U8)
+        w2_raw = placed("w2_raw", [P, PACK, H], F32, 58)
+        neg_noz = held("neg_noz", [P, 2, PACK], F32)
+        gain = held("gain", [P, 2, PACK], F32)
         tab2w = held("tab2w", [P, T], U16)
         v2s_rows = held("v2s_rows", [P, S], U8)
         vector_rows = held("vector_rows", [P, KP], F32)
@@ -85,24 +84,22 @@ def tile_list_orchard_spray_dosing_kernel(
         nc.vector.memset(warm[:, 0:1], 0.0)
         nc.scalar.activation(warm[:, 1:2], warm[:, 0:1], ACT.Silu)
 
-        def load_w2(b):
-            nc.sync.dma_start(out=w2_raw[b][:], in_=w2.rearrange("(p j) c -> p j c", j=PACK)[:, :, b * KP : (b + 1) * KP])
-
         nc.sync.dma_start(list2[:], offs2)
         nc.sync.dma_start(out=tab2s[TAB2_ROW : TAB2_ROW + 16, :].bitcast(I32), in_=tab2_scales[0].bitcast(I32))
         nc.sync.dma_start(list1[:], offs)
         nc.sync.dma_start(out=tabs[TAB_ROW:P, :].bitcast(I32), in_=tab_scales.rearrange("a q c -> (a q) c").bitcast(I32))
-        load_w2(0)
         nc.sync.dma_start(out=tab2w[:].bitcast(I32), in_=tab2_words[0].bitcast(I32))
         nc.sync.dma_start(out=vector_rows[NOZZLE_ROW:FLOW_ROW, :], in_=nozzle.rearrange("(b c) -> b c", b=2))
         nc.sync.dma_start(out=vector_rows[FLOW_ROW:P, :], in_=flow.rearrange("(b c) -> b c", b=2))
         nc.sync.dma_start(out=w1s_raw[TAB_ROW:P, :].bitcast(I32), in_=w1_scales.rearrange("a q c -> (a q) c").bitcast(I32))
-        load_w2(1)
+        nc.sync.dma_start(out=w2_raw[:].rearrange("p j c -> p (j c)"), in_=w2.rearrange("(p j) c -> p (j c)", j=PACK))
 
         vectors = bank(VECTOR_BANK)
         for t in range(PACK):
             nc.tensor.transpose(vectors[:, t * P : (t + 1) * P], vector_rows[:, t:KP:PACK], ident[:])
         turned = vectors[:].rearrange("p (t j) -> p j t", t=PACK)
+        nc.scalar.activation(neg_noz[:], turned[:, NOZZLE_ROW:FLOW_ROW, :], ACT.Copy, scale=-1.0)
+        nc.scalar.copy(out=gain[:], in_=turned[:, FLOW_ROW:P, :])
 
         nc.vector.tensor_copy(v2s_rows[:], tab2s[:].indirect(list2[:]))
         v2s = placed("v2s", [P, S], U8, 16.5)
@@ -122,28 +119,7 @@ def tile_list_orchard_spray_dosing_kernel(
         load_w1(0, 17.5)
         vs_rows = placed("vs_rows", [P, S], U8, 90)
         nc.vector.tensor_copy(vs_rows[:], tabs[:].indirect(list1[:]))
-        w2w = [placed("w2w%d" % b, [P, KP], U32, 50 + 2 * b) for b in range(2)]
-        w2s = [held("w2s%d" % b, [P, KP], U8) for b in range(2)]
-
-        def cast_w2(copy, rounded, b):
-            copy(
-                out=rounded[:].rearrange("p (s e m j) -> p s m j e", s=2, e=2, j=PACK),
-                in_=w2_raw[b][:].rearrange("p j (m s e) -> p s m j e", s=2, e=2),
-            )
-
-        def quantize_w2(rounded, b):
-            nc.vector.quantize_mx(out=w2w[b][:].bitcast(FP8X4), scales=w2s[b][:], in_=rounded[:])
-
-        v2w = {0: held("v2w0", [P, W], U16)}
-        nc.vector.tensor_copy(v2w[0][:], tab2w[:].indirect(list2[:, visits(0)]))
-        first_block = placed("w2_first", [P, PACK * KP], BF16, 40)
-        cast_w2(nc.scalar.copy, first_block, 0)
-        neg_noz = placed("neg_noz", [P, 2, PACK], F32, 58)
-        gain = placed("gain", [P, 2, PACK], F32, 58.25)
-        nc.scalar.activation(neg_noz[:], turned[:, NOZZLE_ROW:FLOW_ROW, :], ACT.Copy, scale=-1.0)
-        nc.scalar.copy(out=gain[:], in_=turned[:, FLOW_ROW:P, :])
-        quantize_w2(first_block, 0)
-        joined = placed("joined", [P, S + H], U8, 40)
+        joined = held("joined", [P, S + H], U8)
         order_columns(nc.vector.tensor_copy, joined[:, S:], w1s_raw[:])
         nc.vector.tensor_copy(out=joined[:, 0:S].bitcast(I32), in_=vs_rows[:].bitcast(I32))
         planes = [placed("plane%d" % a, [P, S + H], U8, 36 + 2 * a) for a in range(2)]
@@ -157,11 +133,36 @@ def tile_list_orchard_spray_dosing_kernel(
         load_tab(1, 90.5)
         load_w1(1, 88.5)
         lift_rows(1)
-        v2w[1] = placed("v2w1", [P, W], U16, 42)
+
+        w2w, w2s = {}, {}
+
+        def cast_w2(copy, rounded, b, pairs):
+            copy(
+                out=rounded[:].rearrange("p (s e m j) -> p s m j e", e=2, m=P, j=PACK),
+                in_=w2_raw[:, :, b * KP : (b + 1) * KP].rearrange("p j (m s e) -> p s m j e", s=2, e=2)[:, pairs],
+            )
+
+        def quantize_w2(rounded, b, slots, kib):
+            words = placed("w2w%d_%d" % (b, slots[0]), [P, len(slots) * P], U32, kib)
+            scales = held("w2s%d_%d" % (b, slots[0]), [P, len(slots) * P], U8)
+            nc.vector.quantize_mx(out=words[:].bitcast(FP8X4), scales=scales[:], in_=rounded[:])
+            for i, t in enumerate(slots):
+                w2w[b, t] = words[:, i * P : (i + 1) * P]
+                w2s[b, t] = scales[:, i * P : (i + 1) * P]
+
+        v2w = {0: held("v2w0", [P, W], U16)}
+        nc.vector.tensor_copy(v2w[0][:], tab2w[:].indirect(list2[:, visits(0)]))
+        upper = placed("w2_upper", [P, 2 * KP], BF16, 40)
+        lower = placed("w2_lower", [P, 2 * KP], BF16, 44)
+        cast_w2(nc.vector.tensor_copy, upper, 0, slice(1, 2))
+        cast_w2(nc.scalar.copy, lower, 0, slice(0, 1))
+        quantize_w2(upper, 0, (2, 3), 51)
+        quantize_w2(lower, 0, (0, 1), 50)
+        v2w[1] = placed("v2w1", [P, W], U16, 40)
         nc.vector.tensor_copy(v2w[1][:], tab2w[:].indirect(list2[:, visits(1)]))
         second_block = placed("w2_second", [P, PACK * KP], BF16, 44)
-        cast_w2(nc.vector.tensor_copy, second_block, 1)
-        quantize_w2(second_block, 1)
+        cast_w2(nc.vector.tensor_copy, second_block, 1, slice(0, 2))
+        quantize_w2(second_block, 1, (0, 1, 2, 3), 52)
 
         vw = [[placed("vw0_%d" % u, [P, W], U32, 44 + 2 * u) for u in range(2)], [held("vw1_%d" % u, [P, W], U32) for u in range(2)]]
 
@@ -190,19 +191,21 @@ def tile_list_orchard_spray_dosing_kernel(
             )
 
         allowed = {}
-        shared_bytes = {12: 30, 13: 32}
-        sums = [(b, u, t) for b in range(2) for u in range(2) for t in range(PACK)]
+        shared_bytes = {12: 29.5, 13: 31.5, 14: 33.5}
+        sums = [(b, u, t) for b in range(2) for u in range(2) for t in ((2, 3, 0, 1) if (b, u) == (0, 0) else range(PACK))]
         for n, (b, u, t) in enumerate(sums):
             acc = bank(n % 4 if n < 12 else 4 + n % 3)
             nc.tensor.matmul_mx(
-                out=acc[:], lhsT=w2w[b][:, t * P : (t + 1) * P].bitcast(FP8X4), lhsT_scale=w2s[b][:, t * P : (t + 1) * P],
+                out=acc[:], lhsT=w2w[b, t].bitcast(FP8X4), lhsT_scale=w2s[b, t],
                 rhs=v2w[u][:].bitcast(FP4X4), rhs_scale=v2s[:, u * W : (u + 1) * W], start=True, stop=True,
             )
             if n in shared_bytes:
                 allowed[b, u, t] = placed("allowed%d_%d_%d" % (b, u, t), [P, W], F32, shared_bytes[n])
             else:
                 allowed[b, u, t] = held("allowed%d_%d_%d" % (b, u, t), [P, W], F32)
-            if n in (12, 13):
+            if u == 0:
+                nc.scalar.activation(allowed[b, u, t][:], acc[:], ACT.Identity, bias=neg_noz[:, b, t : t + 1])
+            elif n in shared_bytes:
                 nc.vector.tensor_copy(out=allowed[b, u, t][:], in_=acc[:])
             else:
                 nc.scalar.copy(out=allowed[b, u, t][:], in_=acc[:])
@@ -222,33 +225,43 @@ def tile_list_orchard_spray_dosing_kernel(
         def make_demand(k, t):
             b, u = units[k]
             demand[k, t] = bank((PACK * k + t) % RING)
-            passes = (0, 1) if PACK * k + t < EARLY_SUMS else (1, 0)
+            passes = (0, 1) if PACK * k + t < RING else (1, 0)
             for a in passes:
                 nc.tensor.matmul_mx(
                     out=demand[k, t][:], lhsT=w1w[a, b][:, t * P : (t + 1) * P].bitcast(FP4X4), lhsT_scale=planes[a][:, S + b * KP + t * P : S + b * KP + (t + 1) * P],
                     rhs=vw[a][u][:].bitcast(FP8X4), rhs_scale=planes[a][:, u * W : (u + 1) * W],
                     start=(a == passes[0]), stop=(a == passes[1]),
                 )
-            if t == 0:
-                for half in (low, high) if k == 0 else (whole,):
-                    if (k, half) == (0, low):
-                        act[k, half.start] = placed("act_first", [P, PACK, HALF], F32, 86)
-                    else:
-                        act[k, half.start] = held("act%d_%d" % (k, half.start), [P, PACK, half.stop - half.start], F32)
-                hw[k] = held("hw%d" % k, [P, W], U32)
-                hs[k] = held("hs%d" % k, [P, W], U8)
+
+        def excess(k, t, part, target):
+            b, u = units[k]
+            column = t * P + NOZZLE_ROW + b
+            nc.vector.scalar_tensor_tensor(
+                target, demand[k, t][:, part], vectors[:, column : column + 1], allowed[b, u, t][:, part], ALU.subtract, ALU.min,
+            )
+
+        def woven_silu(k, part, least, kib):
+            act[k, part.start] = placed("woven%d_%d" % (k, part.start), [P, part.stop - part.start, PACK], F32, kib)
+            nc.scalar.activation(act[k, part.start][:], least.rearrange("p t c -> p c t"), ACT.Silu)
+
+        def woven_gain(engine, factors, k, part):
+            b, u = units[k]
+            if part.start % HALF == 0:
+                half_tile(k, part)
+            engine.tensor_tensor(
+                rounded_h(k, part).rearrange("p (c t) -> p c t", t=PACK), act[k, part.start][:],
+                factors[:, b, :].unsqueeze(1).to_broadcast([P, part.stop - part.start, PACK]), ALU.mult,
+            )
 
         def activated(k, part):
-            first = high.start if k == 0 and part.start >= high.start else 0
-            return act[k, first][:, :, part.start - first : part.stop - first]
+            return act[k][:, :, part]
 
-        def dose(k, t, part):
+        def dose(k, t):
             b, u = units[k]
-            if part.start == 0:
-                make_demand(k, t)
-            least = ring.tile([P, part.stop - part.start], F32, name="least", bufs=8)
-            nc.vector.tensor_tensor(least[:], demand[k, t][:, part], allowed[b, u, t][:, part], ALU.min)
-            nc.scalar.activation(activated(k, part)[:, t, :], least[:], ACT.Silu, bias=neg_noz[:, b, t : t + 1])
+            make_demand(k, t)
+            least = ring.tile([P, W], F32, name="least", bufs=8)
+            nc.vector.tensor_tensor(least[:], demand[k, t][:], allowed[b, u, t][:], ALU.min)
+            nc.scalar.activation(act[k][:, t, :], least[:], ACT.Silu, bias=neg_noz[:, b, t : t + 1])
 
         def rounded_h(k, part):
             first = part.start // (W // 2) * (W // 2)
@@ -304,43 +317,53 @@ def tile_list_orchard_spray_dosing_kernel(
                     nc.scalar.activation(res[:], acc[i][:, part], ACT.Identity, bias=rest[:, i : i + 1])
                 nc.sync.dma_start(out=out[i * P : (i + 1) * P, u * W + part.start : u * W + part.stop], in_=res[:])
 
+        for i, part in enumerate((low, high)):
+            lesser = held("lesser0_%d" % i, [P, PACK, HALF], F32)
+            for t in range(PACK):
+                if i == 0:
+                    make_demand(0, t)
+                excess(0, t, part, lesser[:, t, :])
+            if i == 0:
+                for q in range(2):
+                    quarter = slice(q * HALF // 2, (q + 1) * HALF // 2)
+                    woven_silu(0, quarter, lesser[:, :, quarter], 88 - 2 * q)
+                    woven_gain(nc.gpsimd, gain, 0, quarter)
+            else:
+                woven_silu(0, part, lesser[:], 82)
+                woven_gain(nc.gpsimd, gain, 0, part)
+        lesser = held("lesser1", [P, PACK, W], F32)
+        for t in range(PACK):
+            make_demand(1, t)
+            excess(1, t, whole, lesser[:, t, :])
+        for i, part in enumerate((low, high)):
+            woven_silu(1, part, lesser[:, :, part], 74 + 4 * i)
+        woven_gain(nc.gpsimd, gain, 1, low)
+        for k in (2, 3):
+            act[k] = held("act%d" % k, [P, PACK, W], F32)
+            for t in range(PACK):
+                dose(k, t)
         for k in range(4):
-            for part in (low, high) if k == 0 else (whole,):
-                for t in range(PACK):
-                    dose(k, t, part)
-            if k == 1:
-                apply_gain(nc.gpsimd, gain, 1, slice(low.stop - POOL_EXTRA, low.stop))
-            if k == 0:
-                half_tile(0, low)
-                shared = held("h_bf_shared", [P, PACK * (W - POOL_LATE)], BF16)
-                h_bf[0, high.start] = shared[:, 0 : PACK * W // 2]
-                h_bf[1, low.start] = shared[:, PACK * (W // 2 - POOL_LATE) :]
-                apply_gain(nc.gpsimd, gain, 0, low)
-                apply_gain(nc.gpsimd, gain, 0, slice(high.start, W - POOL_LATE))
-        apply_gain(nc.vector, flow_turned, 1, slice(0, low.stop - POOL_EXTRA))
+            hw[k] = held("hw%d" % k, [P, W], U32)
+            hs[k] = placed("hs%d" % k, [P, W], U8, 74 + 0.5 * k)
+        woven_gain(nc.vector, flow_turned, 1, high)
         scalar_gain(2, low)
         scalar_gain(2, high)
-        scalar_gain(3, high)
         quantize_h(0, low)
         quantize_h(1, low)
         valves(0, 0, low, (0, 1), None)
-        apply_gain(nc.gpsimd, gain, 0, slice(W - POOL_LATE, W))
-        h_bf[1, high.start] = h_bf[0, low.start]
-        apply_gain(nc.vector, flow_turned, 1, high)
         quantize_h(0, high)
         quantize_h(1, high)
         valves(4, 0, high, (0, 1), None)
         h_bf[3, low.start] = h_bf[1, low.start]
         apply_gain(nc.vector, flow_turned, 3, low)
-        half_tile(2, low)
-        interleave(2, low)
+        for part in (low, high):
+            half_tile(2, part)
+            interleave(2, part)
         quantize_h(3, low)
         quantize_h(2, low)
         valves(8, 1, low, (1, 0), None)
-        half_tile(2, high)
-        half_tile(3, high)
-        interleave(2, high)
-        interleave(3, high)
         quantize_h(2, high)
+        h_bf[3, high.start] = h_bf[2, low.start]
+        apply_gain(nc.vector, flow_turned, 3, high)
         quantize_h(3, high)
         valves(12, 1, high, (0, 1), 1)

@@ -29,6 +29,9 @@ NOZZLE_ROW = 124
 FLOW_ROW = 126
 RING = 7
 VECTOR_BANK = 7
+POOL_EXTRA = 64
+POOL_LATE = 48
+EARLY_SUMS = 7
 
 
 def tile_list_orchard_spray_dosing_kernel(
@@ -203,9 +206,7 @@ def tile_list_orchard_spray_dosing_kernel(
                 allowed[b, u, t] = placed("allowed%d_%d_%d" % (b, u, t), [P, W], F32, shared_bytes[n])
             else:
                 allowed[b, u, t] = held("allowed%d_%d_%d" % (b, u, t), [P, W], F32)
-            if u == 0:
-                nc.scalar.activation(allowed[b, u, t][:], acc[:], ACT.Identity, bias=neg_noz[:, b, t : t + 1])
-            elif n in shared_bytes:
+            if n in shared_bytes:
                 nc.vector.tensor_copy(out=allowed[b, u, t][:], in_=acc[:])
             else:
                 nc.scalar.copy(out=allowed[b, u, t][:], in_=acc[:])
@@ -225,43 +226,33 @@ def tile_list_orchard_spray_dosing_kernel(
         def make_demand(k, t):
             b, u = units[k]
             demand[k, t] = bank((PACK * k + t) % RING)
-            passes = (0, 1) if PACK * k + t < RING else (1, 0)
+            passes = (0, 1) if PACK * k + t < EARLY_SUMS else (1, 0)
             for a in passes:
                 nc.tensor.matmul_mx(
                     out=demand[k, t][:], lhsT=w1w[a, b][:, t * P : (t + 1) * P].bitcast(FP4X4), lhsT_scale=planes[a][:, S + b * KP + t * P : S + b * KP + (t + 1) * P],
                     rhs=vw[a][u][:].bitcast(FP8X4), rhs_scale=planes[a][:, u * W : (u + 1) * W],
                     start=(a == passes[0]), stop=(a == passes[1]),
                 )
-
-        def excess(k, t, part, target):
-            b, u = units[k]
-            column = t * P + NOZZLE_ROW + b
-            nc.vector.scalar_tensor_tensor(
-                target, demand[k, t][:, part], vectors[:, column : column + 1], allowed[b, u, t][:, part], ALU.subtract, ALU.min,
-            )
-
-        def woven_silu(k, part, least, kib):
-            act[k, part.start] = placed("woven%d_%d" % (k, part.start), [P, part.stop - part.start, PACK], F32, kib)
-            nc.scalar.activation(act[k, part.start][:], least.rearrange("p t c -> p c t"), ACT.Silu)
-
-        def woven_gain(engine, factors, k, part):
-            b, u = units[k]
-            if part.start % HALF == 0:
-                half_tile(k, part)
-            engine.tensor_tensor(
-                rounded_h(k, part).rearrange("p (c t) -> p c t", t=PACK), act[k, part.start][:],
-                factors[:, b, :].unsqueeze(1).to_broadcast([P, part.stop - part.start, PACK]), ALU.mult,
-            )
+            if t == 0:
+                for half in (low, high) if k == 0 else (whole,):
+                    if (k, half) == (0, low):
+                        act[k, half.start] = placed("act_first", [P, PACK, HALF], F32, 86)
+                    else:
+                        act[k, half.start] = held("act%d_%d" % (k, half.start), [P, PACK, half.stop - half.start], F32)
+                hw[k] = held("hw%d" % k, [P, W], U32)
+                hs[k] = held("hs%d" % k, [P, W], U8)
 
         def activated(k, part):
-            return act[k][:, :, part]
+            first = high.start if k == 0 and part.start >= high.start else 0
+            return act[k, first][:, :, part.start - first : part.stop - first]
 
-        def dose(k, t):
+        def dose(k, t, part):
             b, u = units[k]
-            make_demand(k, t)
-            least = ring.tile([P, W], F32, name="least", bufs=8)
-            nc.vector.tensor_tensor(least[:], demand[k, t][:], allowed[b, u, t][:], ALU.min)
-            nc.scalar.activation(act[k][:, t, :], least[:], ACT.Silu, bias=neg_noz[:, b, t : t + 1])
+            if part.start == 0:
+                make_demand(k, t)
+            least = ring.tile([P, part.stop - part.start], F32, name="least", bufs=8)
+            nc.vector.tensor_tensor(least[:], demand[k, t][:, part], allowed[b, u, t][:, part], ALU.min)
+            nc.scalar.activation(activated(k, part)[:, t, :], least[:], ACT.Silu, bias=neg_noz[:, b, t : t + 1])
 
         def rounded_h(k, part):
             first = part.start // (W // 2) * (W // 2)
@@ -317,53 +308,43 @@ def tile_list_orchard_spray_dosing_kernel(
                     nc.scalar.activation(res[:], acc[i][:, part], ACT.Identity, bias=rest[:, i : i + 1])
                 nc.sync.dma_start(out=out[i * P : (i + 1) * P, u * W + part.start : u * W + part.stop], in_=res[:])
 
-        for i, part in enumerate((low, high)):
-            lesser = held("lesser0_%d" % i, [P, PACK, HALF], F32)
-            for t in range(PACK):
-                if i == 0:
-                    make_demand(0, t)
-                excess(0, t, part, lesser[:, t, :])
-            if i == 0:
-                for q in range(2):
-                    quarter = slice(q * HALF // 2, (q + 1) * HALF // 2)
-                    woven_silu(0, quarter, lesser[:, :, quarter], 88 - 2 * q)
-                    woven_gain(nc.gpsimd, gain, 0, quarter)
-            else:
-                woven_silu(0, part, lesser[:], 82)
-                woven_gain(nc.gpsimd, gain, 0, part)
-        lesser = held("lesser1", [P, PACK, W], F32)
-        for t in range(PACK):
-            make_demand(1, t)
-            excess(1, t, whole, lesser[:, t, :])
-        for i, part in enumerate((low, high)):
-            woven_silu(1, part, lesser[:, :, part], 74 + 4 * i)
-        woven_gain(nc.gpsimd, gain, 1, low)
-        for k in (2, 3):
-            act[k] = held("act%d" % k, [P, PACK, W], F32)
-            for t in range(PACK):
-                dose(k, t)
         for k in range(4):
-            hw[k] = held("hw%d" % k, [P, W], U32)
-            hs[k] = placed("hs%d" % k, [P, W], U8, 74 + 0.5 * k)
-        woven_gain(nc.vector, flow_turned, 1, high)
+            for part in (low, high) if k == 0 else (whole,):
+                for t in range(PACK):
+                    dose(k, t, part)
+            if k == 1:
+                apply_gain(nc.gpsimd, gain, 1, slice(low.stop - POOL_EXTRA, low.stop))
+            if k == 0:
+                half_tile(0, low)
+                shared = held("h_bf_shared", [P, PACK * (W - POOL_LATE)], BF16)
+                h_bf[0, high.start] = shared[:, 0 : PACK * W // 2]
+                h_bf[1, low.start] = shared[:, PACK * (W // 2 - POOL_LATE) :]
+                apply_gain(nc.gpsimd, gain, 0, low)
+                apply_gain(nc.gpsimd, gain, 0, slice(high.start, W - POOL_LATE))
+        apply_gain(nc.vector, flow_turned, 1, slice(0, low.stop - POOL_EXTRA))
         scalar_gain(2, low)
         scalar_gain(2, high)
+        scalar_gain(3, high)
         quantize_h(0, low)
         quantize_h(1, low)
         valves(0, 0, low, (0, 1), None)
+        apply_gain(nc.gpsimd, gain, 0, slice(W - POOL_LATE, W))
+        h_bf[1, high.start] = h_bf[0, low.start]
+        apply_gain(nc.vector, flow_turned, 1, high)
         quantize_h(0, high)
         quantize_h(1, high)
         valves(4, 0, high, (0, 1), None)
         h_bf[3, low.start] = h_bf[1, low.start]
         apply_gain(nc.vector, flow_turned, 3, low)
-        for part in (low, high):
-            half_tile(2, part)
-            interleave(2, part)
+        half_tile(2, low)
+        interleave(2, low)
         quantize_h(3, low)
         quantize_h(2, low)
         valves(8, 1, low, (1, 0), None)
+        half_tile(2, high)
+        half_tile(3, high)
+        interleave(2, high)
+        interleave(3, high)
         quantize_h(2, high)
-        h_bf[3, high.start] = h_bf[2, low.start]
-        apply_gain(nc.vector, flow_turned, 3, high)
         quantize_h(3, high)
         valves(12, 1, high, (0, 1), 1)

@@ -23,7 +23,8 @@ KP = P * PACK
 W = 512
 HALF = W // 2
 ROWS = 4
-TAB_ROW = 96
+TAB_ROWS = (16, 112)
+ZERO_ROWS = ((0, 16), (32, 64), (64, 112))
 TAB2_ROW = 48
 NOZZLE_ROW = 124
 FLOW_ROW = 126
@@ -78,23 +79,28 @@ def tile_list_orchard_spray_dosing_kernel(
 
         nc.vector.memset(tab2s[0:TAB2_ROW, :].bitcast(I32), 0)
         nc.vector.memset(tab2s[TAB2_ROW + 16 : P, :].bitcast(I32), 0)
-        nc.gpsimd.memset(tabs[0:TAB_ROW, :].bitcast(I32), 0)
+        for tile in (tabs, w1s_raw):
+            for lo, hi in ZERO_ROWS:
+                nc.gpsimd.memset(tile[lo:hi, :].bitcast(I32), 0)
         nc.gpsimd.memset(vector_rows[0:NOZZLE_ROW, :], 0.0)
         make_identity(nc, ident[:])
-        nc.gpsimd.memset(w1s_raw[0:TAB_ROW, :].bitcast(I32), 0)
 
         warm = held("warm", [P, 2], F32)
         nc.vector.memset(warm[:, 0:1], 0.0)
         nc.scalar.activation(warm[:, 1:2], warm[:, 0:1], ACT.Silu)
 
+        def load_wide(tile, scales):
+            for a in range(2):
+                nc.sync.dma_start(out=tile[TAB_ROWS[a] : TAB_ROWS[a] + 16, :].bitcast(I32), in_=scales[a].bitcast(I32))
+
         nc.sync.dma_start(list2[:], offs2)
         nc.sync.dma_start(out=tab2s[TAB2_ROW : TAB2_ROW + 16, :].bitcast(I32), in_=tab2_scales[0].bitcast(I32))
         nc.sync.dma_start(list1[:], offs)
-        nc.sync.dma_start(out=tabs[TAB_ROW:P, :].bitcast(I32), in_=tab_scales.rearrange("a q c -> (a q) c").bitcast(I32))
+        load_wide(tabs, tab_scales)
         nc.sync.dma_start(out=tab2w[:].bitcast(I32), in_=tab2_words[0].bitcast(I32))
         nc.sync.dma_start(out=vector_rows[NOZZLE_ROW:FLOW_ROW, :], in_=nozzle.rearrange("(b c) -> b c", b=2))
         nc.sync.dma_start(out=vector_rows[FLOW_ROW:P, :], in_=flow.rearrange("(b c) -> b c", b=2))
-        nc.sync.dma_start(out=w1s_raw[TAB_ROW:P, :].bitcast(I32), in_=w1_scales.rearrange("a q c -> (a q) c").bitcast(I32))
+        load_wide(w1s_raw, w1_scales)
         nc.sync.dma_start(out=w2_raw[:].rearrange("p j c -> p (j c)"), in_=w2.rearrange("(p j) c -> p (j c)", j=PACK))
 
         vectors = bank(VECTOR_BANK)
@@ -129,8 +135,7 @@ def tile_list_orchard_spray_dosing_kernel(
 
         def lift_rows(a):
             for r in range(ROWS):
-                first = TAB_ROW + 16 * a + r
-                nc.sync.dma_start(out=planes[a][r:P:32, :].bitcast(I32), in_=joined[first : TAB_ROW + 16 * (a + 1) : ROWS, :].bitcast(I32))
+                nc.sync.dma_start(out=planes[a][r:P:32, :].bitcast(I32), in_=joined[TAB_ROWS[a] + r : TAB_ROWS[a] + 16 : ROWS, :].bitcast(I32))
 
         lift_rows(0)
         load_tab(1, 90.5)

@@ -305,13 +305,16 @@ def tile_list_orchard_spray_dosing_kernel(
                         rhs=hw[k][:, part].bitcast(FP8X4), rhs_scale=hs[k][:, part],
                         start=(b == blocks[0]), stop=(b == blocks[1]),
                     )
-            for i in range(4):
-                res = placed("res%d_%d_%d" % (i, u, part.start), [P, HALF], F32, first_bank + i)
-                if i % 2 == vector_pair:
-                    nc.vector.tensor_scalar(res[:], acc[i][:, part], rest[:, i : i + 1], None, ALU.add)
-                else:
-                    nc.scalar.activation(res[:], acc[i][:, part], ACT.Identity, bias=rest[:, i : i + 1])
-                nc.sync.dma_start(out=out[i * P : (i + 1) * P, u * W + part.start : u * W + part.stop], in_=res[:])
+            group = 2 if first_bank == 0 else 1
+            for first in range(0, 4, group):
+                res = placed("res%d_%d_%d" % (first, u, part.start), [P, group, HALF], F32, first_bank + first)
+                for i in range(first, first + group):
+                    if i % 2 == vector_pair:
+                        nc.vector.tensor_scalar(res[:, i - first, :], acc[i][:, part], rest[:, i : i + 1], None, ALU.add)
+                    else:
+                        nc.scalar.activation(res[:, i - first, :], acc[i][:, part], ACT.Identity, bias=rest[:, i : i + 1])
+                rows = out[first * P : (first + group) * P, u * W + part.start : u * W + part.stop]
+                nc.sync.dma_start(out=rows.rearrange("(j p) c -> p j c", p=P), in_=res[:])
 
         for k in range(4):
             for part in (low, high) if k == 0 else (whole,):

from contextlib import ExitStack

import concourse.mybir as mybir
from concourse.masks import make_identity

K, K2, H, N, T, S = 1024, 512, 1024, 512, 4096, 1024
FLOPS = 2 * S * (K * H + K2 * H + H * N)

F32 = mybir.dt.float32
BF16 = mybir.dt.bfloat16
I32 = mybir.dt.int32
U32 = mybir.dt.uint32
U16 = mybir.dt.uint16
U8 = mybir.dt.uint8
FP8X4 = mybir.dt.float8_e4m3fn_x4
FP4X4 = mybir.dt.float4_e2m1fn_x4
ACT = mybir.ActivationFunctionType
ALU = mybir.AluOpType

P = 128
PACK = 4
KP = P * PACK
W = 512
HALF = W // 2
ROWS = 4
TAB_ROWS = (16, 112)
ZERO_ROWS = ((0, 16), (32, 64), (64, 112))
TAB2_ROW = 48
NOZZLE_ROW = 124
FLOW_ROW = 126
RING = 7
VECTOR_BANK = 7
POOL_EXTRA = 64
POOL_LATE = 48
EARLY_SUMS = 7


def tile_list_orchard_spray_dosing_kernel(
    tc, tab_words, tab_scales, tab2_words, tab2_scales, offs, offs2,
    w1_words, w1_scales, w2, w3_words, w3_scales, nozzle, flow, idle, out,
):
    nc = tc.nc
    with ExitStack() as ctx:
        keep = ctx.enter_context(tc.tile_pool(name="keep", bufs=1))
        ring = ctx.enter_context(tc.tile_pool(name="ring", bufs=4))
        reuse = ctx.enter_context(tc.tile_pool(name="reuse", bufs=1))
        psum = ctx.enter_context(tc.psum_pool(name="psum", bufs=1))

        def held(name, shape, dtype):
            return keep.tile(shape, dtype, name=name, align_bytes=64)

        def placed(name, shape, dtype, kib):
            return reuse.tile(shape, dtype, name=name, align_bytes=64, offset=int(kib * 1024))

        def bank(i):
            return psum.tile([P, W], F32, name="bank%d" % i)

        list1 = keep.tile([P, S // 16], U16, name="list1")
        list2 = keep.tile([P, S // 16], U16, name="list2")
        tab2s = placed("tab2s", [P, T], U8, 16)
        tabs = placed("tabs", [P, T], U8, 36)
        w1s_raw = held("w1s_raw", [P, H], U8)
        w2_raw = placed("w2_raw", [P, PACK, H], F32, 58)
        neg_noz = held("neg_noz", [P, 2, PACK], F32)
        gain = held("gain", [P, 2, PACK], F32)
        tab2w = held("tab2w", [P, T], U16)
        v2s_rows = held("v2s_rows", [P, S], U8)
        vector_rows = held("vector_rows", [P, KP], F32)
        ident = held("ident", [P, P], F32)

        def visits(u):
            return slice(u * (W // 16), (u + 1) * (W // 16))

        def order_columns(copy, ordered, raw):
            copy(
                out=ordered.rearrange("p (g t m) -> p g t m", t=PACK, m=P),
                in_=raw.rearrange("p (g m t) -> p g t m", t=PACK, m=P),
            )

        nc.vector.memset(tab2s[0:TAB2_ROW, :].bitcast(I32), 0)
        nc.vector.memset(tab2s[TAB2_ROW + 16 : P, :].bitcast(I32), 0)
        for tile in (tabs, w1s_raw):
            for lo, hi in ZERO_ROWS:
                nc.gpsimd.memset(tile[lo:hi, :].bitcast(I32), 0)
        nc.gpsimd.memset(vector_rows[0:NOZZLE_ROW, :], 0.0)
        make_identity(nc, ident[:])

        warm = held("warm", [P, 2], F32)
        nc.vector.memset(warm[:, 0:1], 0.0)
        nc.scalar.activation(warm[:, 1:2], warm[:, 0:1], ACT.Silu)

        def load_wide(tile, scales):
            for a in range(2):
                nc.sync.dma_start(out=tile[TAB_ROWS[a] : TAB_ROWS[a] + 16, :].bitcast(I32), in_=scales[a].bitcast(I32))

        nc.sync.dma_start(list2[:], offs2)
        nc.sync.dma_start(out=tab2s[TAB2_ROW : TAB2_ROW + 16, :].bitcast(I32), in_=tab2_scales[0].bitcast(I32))
        nc.sync.dma_start(list1[:], offs)
        load_wide(tabs, tab_scales)
        nc.sync.dma_start(out=tab2w[:].bitcast(I32), in_=tab2_words[0].bitcast(I32))
        nc.sync.dma_start(out=vector_rows[NOZZLE_ROW:FLOW_ROW, :], in_=nozzle.rearrange("(b c) -> b c", b=2))
        nc.sync.dma_start(out=vector_rows[FLOW_ROW:P, :], in_=flow.rearrange("(b c) -> b c", b=2))
        load_wide(w1s_raw, w1_scales)
        nc.sync.dma_start(out=w2_raw[:].rearrange("p j c -> p (j c)"), in_=w2.rearrange("(p j) c -> p (j c)", j=PACK))

        vectors = bank(VECTOR_BANK)
        for t in range(PACK):
            nc.tensor.transpose(vectors[:, t * P : (t + 1) * P], vector_rows[:, t:KP:PACK], ident[:])
        turned = vectors[:].rearrange("p (t j) -> p j t", t=PACK)
        nc.scalar.activation(neg_noz[:], turned[:, NOZZLE_ROW:FLOW_ROW, :], ACT.Copy, scale=-1.0)
        nc.scalar.copy(out=gain[:], in_=turned[:, FLOW_ROW:P, :])

        nc.vector.tensor_copy(v2s_rows[:], tab2s[:].indirect(list2[:]))
        v2s = placed("v2s", [P, S], U8, 16.5)
        for r in range(ROWS):
            nc.sync.dma_start(out=v2s[r:P:32, :].bitcast(I32), in_=v2s_rows[TAB2_ROW + r : TAB2_ROW + 16 : ROWS, :].bitcast(I32))
        tabw, w1_raw = {}, {}

        def load_tab(a, kib):
            tabw[a] = placed("tabw%d" % a, [P, T], U32, kib)
            nc.sync.dma_start(out=tabw[a][:].bitcast(I32), in_=tab_words[a].rearrange("p t i -> p (t i)").bitcast(I32))

        def load_w1(a, kib):
            w1_raw[a] = placed("w1_raw%d" % a, [P, H], U16, kib)
            nc.sync.dma_start(out=w1_raw[a][:].bitcast(I32), in_=w1_words[a].bitcast(I32))

        load_tab(0, 19.75)
        load_w1(0, 17.5)
        vs_rows = placed("vs_rows", [P, S], U8, 90)
        nc.vector.tensor_copy(vs_rows[:], tabs[:].indirect(list1[:]))
        joined = held("joined", [P, S + H], U8)
        order_columns(nc.vector.tensor_copy, joined[:, S:], w1s_raw[:])
        nc.vector.tensor_copy(out=joined[:, 0:S].bitcast(I32), in_=vs_rows[:].bitcast(I32))
        planes = [placed("plane%d" % a, [P, S + H], U8, 36 + 2 * a) for a in range(2)]

        def lift_rows(a):
            for r in range(ROWS):
                nc.sync.dma_start(out=planes[a][r:P:32, :].bitcast(I32), in_=joined[TAB_ROWS[a] + r : TAB_ROWS[a] + 16 : ROWS, :].bitcast(I32))

        lift_rows(0)
        load_tab(1, 90.5)
        load_w1(1, 88.5)
        lift_rows(1)

        w2w, w2s = {}, {}

        def cast_w2(copy, rounded, b, pairs):
            copy(
                out=rounded[:].rearrange("p (s e m j) -> p s m j e", e=2, m=P, j=PACK),
                in_=w2_raw[:, :, b * KP : (b + 1) * KP].rearrange("p j (m s e) -> p s m j e", s=2, e=2)[:, pairs],
            )

        def quantize_w2(rounded, b, slots, kib):
            words = placed("w2w%d_%d" % (b, slots[0]), [P, len(slots) * P], U32, kib)
            scales = held("w2s%d_%d" % (b, slots[0]), [P, len(slots) * P], U8)
            nc.vector.quantize_mx(out=words[:].bitcast(FP8X4), scales=scales[:], in_=rounded[:])
            for i, t in enumerate(slots):
                w2w[b, t] = words[:, i * P : (i + 1) * P]
                w2s[b, t] = scales[:, i * P : (i + 1) * P]

        v2w = {0: held("v2w0", [P, W], U16)}
        nc.vector.tensor_copy(v2w[0][:], tab2w[:].indirect(list2[:, visits(0)]))
        upper = placed("w2_upper", [P, 2 * KP], BF16, 40)
        lower = placed("w2_lower", [P, 2 * KP], BF16, 44)
        cast_w2(nc.vector.tensor_copy, upper, 0, slice(1, 2))
        cast_w2(nc.scalar.copy, lower, 0, slice(0, 1))
        quantize_w2(upper, 0, (2, 3), 51)
        quantize_w2(lower, 0, (0, 1), 50)
        v2w[1] = placed("v2w1", [P, W], U16, 40)
        nc.vector.tensor_copy(v2w[1][:], tab2w[:].indirect(list2[:, visits(1)]))
        second_block = placed("w2_second", [P, PACK * KP], BF16, 44)
        cast_w2(nc.vector.tensor_copy, second_block, 1, slice(0, 2))
        quantize_w2(second_block, 1, (0, 1, 2, 3), 52)

        vw = [[placed("vw0_%d" % u, [P, W], U32, 44 + 2 * u) for u in range(2)], [held("vw1_%d" % u, [P, W], U32) for u in range(2)]]

        def gather_words(a, u):
            nc.vector.tensor_copy(vw[a][u][:], tabw[a][:].indirect(list1[:, visits(u)]))

        gather_words(0, 0)
        w1_first = held("w1_first", [P, H], U16)
        order_columns(nc.vector.tensor_copy, w1_first[:], w1_raw[0][:])
        w1w = {(0, b): w1_first[:, b * KP : (b + 1) * KP] for b in range(2)}
        gather_words(0, 1)

        rest = placed("rest", [P, PACK], F32, 24)
        with nc.allow_non_contiguous_dma(reason="one idle value a partition"):
            nc.sync.dma_start(out=rest[:], in_=idle.rearrange("(i p) -> p i", p=P))
        w3w = placed("w3w", [P, 2 * N], U32, 24.5)
        w3s = placed("w3s", [P, 2 * N], U8, 28.5)
        nc.sync.dma_start(
            out=w3w[:].bitcast(I32).rearrange("p (a c) -> p a c", a=2),
            in_=w3_words.rearrange("a p c i -> p a (c i)").bitcast(I32),
        )
        for r in range(ROWS):
            nc.sync.dma_start(
                out=w3s[r:P:32, :].bitcast(I32).rearrange("p (a c) -> p a c", a=2),
                in_=w3_scales.bitcast(I32).rearrange("a (q r) c -> r q a c", r=ROWS)[r],
            )

        allowed = {}
        shared_bytes = {12: 29.5, 13: 31.5, 14: 33.5}
        sums = [(b, u, t) for b in range(2) for u in range(2) for t in ((2, 3, 0, 1) if (b, u) == (0, 0) else range(PACK))]
        for n, (b, u, t) in enumerate(sums):
            acc = bank(n % 4 if n < 12 else 4 + n % 3)
            nc.tensor.matmul_mx(
                out=acc[:], lhsT=w2w[b, t].bitcast(FP8X4), lhsT_scale=w2s[b, t],
                rhs=v2w[u][:].bitcast(FP4X4), rhs_scale=v2s[:, u * W : (u + 1) * W], start=True, stop=True,
            )
            if n in shared_bytes:
                allowed[b, u, t] = placed("allowed%d_%d_%d" % (b, u, t), [P, W], F32, shared_bytes[n])
            else:
                allowed[b, u, t] = held("allowed%d_%d_%d" % (b, u, t), [P, W], F32)
            if n in shared_bytes:
                nc.vector.tensor_copy(out=allowed[b, u, t][:], in_=acc[:])
            else:
                nc.scalar.copy(out=allowed[b, u, t][:], in_=acc[:])

        gather_words(1, 0)
        gather_words(1, 1)
        for b in range(2):
            ordered = placed("w1_second%d" % b, [P, KP], U16, 52 + b)
            order_columns(nc.scalar.copy, ordered[:], w1_raw[1][:, b * KP : (b + 1) * KP])
            w1w[1, b] = ordered[:]

        flow_turned = turned[:, FLOW_ROW:P, :]
        units = [(0, 0), (1, 0), (0, 1), (1, 1)]
        demand, act, rounded, h_bf, hw, hs = {}, {}, {}, {}, {}, {}
        whole, low, high = slice(0, W), slice(0, W // 2), slice(W // 2, W)

        def make_demand(k, t):
            b, u = units[k]
            demand[k, t] = bank((PACK * k + t) % RING)
            passes = (0, 1) if PACK * k + t < EARLY_SUMS else (1, 0)
            for a in passes:
                nc.tensor.matmul_mx(
                    out=demand[k, t][:], lhsT=w1w[a, b][:, t * P : (t + 1) * P].bitcast(FP4X4), lhsT_scale=planes[a][:, S + b * KP + t * P : S + b * KP + (t + 1) * P],
                    rhs=vw[a][u][:].bitcast(FP8X4), rhs_scale=planes[a][:, u * W : (u + 1) * W],
                    start=(a == passes[0]), stop=(a == passes[1]),
                )
            if t == 0:
                for half in (low, high) if k == 0 else (whole,):
                    if (k, half) == (0, low):
                        act[k, half.start] = placed("act_first", [P, PACK, HALF], F32, 86)
                    else:
                        act[k, half.start] = held("act%d_%d" % (k, half.start), [P, PACK, half.stop - half.start], F32)
                hw[k] = held("hw%d" % k, [P, W], U32)
                hs[k] = held("hs%d" % k, [P, W], U8)

        def activated(k, part):
            first = high.start if k == 0 and part.start >= high.start else 0
            return act[k, first][:, :, part.start - first : part.stop - first]

        def dose(k, t, part):
            b, u = units[k]
            if part.start == 0:
                make_demand(k, t)
            least = ring.tile([P, part.stop - part.start], F32, name="least", bufs=8)
            nc.vector.tensor_tensor(least[:], demand[k, t][:, part], allowed[b, u, t][:, part], ALU.min)
            nc.scalar.activation(activated(k, part)[:, t, :], least[:], ACT.Silu, bias=neg_noz[:, b, t : t + 1])

        def rounded_h(k, part):
            first = part.start // (W // 2) * (W // 2)
            return h_bf[k, first][:, PACK * (part.start - first) : PACK * (part.stop - first)]

        def half_tile(k, part):
            h_bf[k, part.start] = held("h_bf%d_%d" % (k, part.start), [P, PACK * W // 2], BF16)

        def apply_gain(engine, factors, k, part):
            b, u = units[k]
            pairs = (part.stop - part.start) // 2
            engine.tensor_tensor(
                rounded_h(k, part).rearrange("p (c i t) -> p c t i", i=2, t=PACK),
                activated(k, part).rearrange("p t (c i) -> p c t i", i=2),
                factors[:, b, :].unsqueeze(1).unsqueeze(3).to_broadcast([P, pairs, PACK, 2]),
                ALU.mult,
            )

        def scalar_gain(k, part):
            b, u = units[k]
            rounded[k, part.start] = held("rounded%d_%d" % (k, part.start), [P, PACK, part.stop - part.start], BF16)
            for t in range(PACK):
                nc.scalar.activation(rounded[k, part.start][:, t, :], activated(k, part)[:, t, :], ACT.Copy, scale=gain[:, b, t : t + 1])

        def interleave(k, part):
            nc.vector.tensor_copy(
                out=rounded_h(k, part).rearrange("p (c i t) -> p c t i", i=4, t=PACK),
                in_=rounded[k, part.start][:].rearrange("p t (c i) -> p c t i", i=4),
            )

        def quantize_h(k, part):
            nc.vector.quantize_mx(
                out=hw[k][:, part].bitcast(FP8X4), scales=hs[k][:, part],
                in_=rounded_h(k, part),
            )

        def valves(first_bank, u, part, blocks, vector_pair):
            acc = [bank((first_bank + 3 + i) % RING) for i in range(4)]
            for b in blocks:
                k = units.index((b, u))
                for i in range(4):
                    cols = slice(b * N + i * P, b * N + (i + 1) * P)
                    nc.tensor.matmul_mx(
                        out=acc[i][:, part], lhsT=w3w[:, cols].bitcast(FP8X4), lhsT_scale=w3s[:, cols],
                        rhs=hw[k][:, part].bitcast(FP8X4), rhs_scale=hs[k][:, part],
                        start=(b == blocks[0]), stop=(b == blocks[1]),
                    )
            group = 2 if first_bank == 0 else 1
            for first in range(0, 4, group):
                res = placed("res%d_%d_%d" % (first, u, part.start), [P, group, HALF], F32, first_bank + first)
                for i in range(first, first + group):
                    if i % 2 == vector_pair:
                        nc.vector.tensor_scalar(res[:, i - first, :], acc[i][:, part], rest[:, i : i + 1], None, ALU.add)
                    else:
                        nc.scalar.activation(res[:, i - first, :], acc[i][:, part], ACT.Identity, bias=rest[:, i : i + 1])
                rows = out[first * P : (first + group) * P, u * W + part.start : u * W + part.stop]
                nc.sync.dma_start(out=rows.rearrange("(j p) c -> p j c", p=P), in_=res[:])

        for k in range(4):
            for part in (low, high) if k == 0 else (whole,):
                for t in range(PACK):
                    dose(k, t, part)
            if k == 1:
                apply_gain(nc.gpsimd, gain, 1, slice(low.stop - POOL_EXTRA, low.stop))
            if k == 0:
                half_tile(0, low)
                shared = held("h_bf_shared", [P, PACK * (W - POOL_LATE)], BF16)
                h_bf[0, high.start] = shared[:, 0 : PACK * W // 2]
                h_bf[1, low.start] = shared[:, PACK * (W // 2 - POOL_LATE) :]
                apply_gain(nc.gpsimd, gain, 0, low)
                apply_gain(nc.gpsimd, gain, 0, slice(high.start, W - POOL_LATE))
        apply_gain(nc.vector, flow_turned, 1, slice(0, low.stop - POOL_EXTRA))
        scalar_gain(2, low)
        scalar_gain(2, high)
        scalar_gain(3, high)
        quantize_h(0, low)
        quantize_h(1, low)
        valves(0, 0, low, (0, 1), None)
        apply_gain(nc.gpsimd, gain, 0, slice(W - POOL_LATE, W))
        h_bf[1, high.start] = h_bf[0, low.start]
        apply_gain(nc.vector, flow_turned, 1, high)
        quantize_h(0, high)
        quantize_h(1, high)
        valves(4, 0, high, (0, 1), None)
        h_bf[3, low.start] = h_bf[1, low.start]
        apply_gain(nc.vector, flow_turned, 3, low)
        half_tile(2, low)
        interleave(2, low)
        quantize_h(3, low)
        quantize_h(2, low)
        valves(8, 1, low, (1, 0), None)
        half_tile(2, high)
        half_tile(3, high)
        interleave(2, high)
        interleave(3, high)
        quantize_h(2, high)
        quantize_h(3, high)
        valves(12, 1, high, (0, 1), 1)
